import numpy as np
import ml_dtypes


def mxq(x, axis, fmt="e4m3"):
    dtype, down = {"e4m3": (ml_dtypes.float8_e4m3fn, 7), "e5m2": (ml_dtypes.float8_e5m2, 14)}[fmt]
    v = np.moveaxis(np.asarray(x, np.float32).astype(ml_dtypes.bfloat16).astype(np.float64), axis, -1)
    blocks = v.reshape(v.shape[:-1] + (-1, 32))
    amax = np.abs(blocks).max(-1, keepdims=True)
    byte = np.maximum(np.where(amax > 0, np.frexp(amax)[1] - 1 + 127, 0) - down, 1)
    scale = np.exp2(byte - 127.0)
    codes = (blocks / scale).astype(np.float32).astype(dtype).astype(np.float64)
    return np.moveaxis((codes * scale).reshape(v.shape), -1, axis)


WIDE = False


def mx_kscale(k):
    if not WIDE:
        return np.ones(k)
    levels = np.array([10, -10, 5, -5, 0])
    if k % 512:
        return np.exp2(np.random.permutation(np.resize(levels, k // 32))).repeat(32)
    a = np.empty((k // 512, 16))
    for p in range(k // 512):
        a[p, :8] = np.random.permutation(np.resize(levels, 8))
        for g in range(8):
            far = levels[np.abs(levels - a[p, g]) >= 10]
            a[p, g + 8] = far[np.random.randint(len(far))]
    return np.exp2(a.ravel()).repeat(32)


BF16 = ml_dtypes.bfloat16


def bf(x):
    return np.asarray(x, np.float32).astype(BF16)


def f64(x):
    return np.asarray(x).astype(np.float64)


D, F, N = 2048, 128, 2048

ALPHA = 0.5


def draw0():
    s = mx_kscale(N)
    t = mx_kscale(N)
    c = 1.0 / np.sqrt(N)
    return {
        "w0": bf(np.random.standard_normal((D, F)) * 0.5),
        "coef": bf(np.random.standard_normal((N, N)) * c * s[None, :]),
        "g": bf((1.0 + 0.1 * np.random.standard_normal(N)) * t),
        "uc": bf(np.random.standard_normal((D, N)) * c / t[None, :]),
        "us": bf(np.random.standard_normal((D, N)) * c / t[None, :]),
        "vc": bf(np.random.standard_normal((N, F)) / s[:, None]),
        "vs": bf(np.random.standard_normal((N, F)) / s[:, None]),
    }


def core(w0, coef, g, uc, us, vc, vs):
    cq = mxq(f64(coef), 1, "e4m3")
    rc = cq @ mxq(f64(vc), 0, "e4m3")
    rs = cq @ mxq(f64(vs), 0, "e4m3")
    gain = f64(g)[:, None]
    zc = gain * rc
    zs = gain * rs
    pc = mxq(f64(uc), 1, "e4m3") @ mxq(zc, 0, "e4m3")
    ps = mxq(f64(us), 1, "e4m3") @ mxq(zs, 0, "e4m3")
    return f64(w0) + ALPHA * (pc - ps)


def e4m3fn_bytes(y):
    return np.clip(np.asarray(y, np.float64), -448.0, 448.0).astype(np.float32).astype(ml_dtypes.float8_e4m3fn).view(np.uint8)


def e4m3fn_values(b):
    return np.asarray(b, np.uint8).view(ml_dtypes.float8_e4m3fn).astype(np.float64)


def setup_inputs():
    d = draw0()
    x0 = np.asarray(d['us']).astype(np.float64)
    s = (np.max(np.abs(x0), axis=(0,), keepdims=True) / 448.0).astype(np.float32)
    out = {}
    for k, v in d.items():
        if k == 'us':
            out['us_bytes'] = e4m3fn_bytes(x0 / s.astype(np.float64))
            out['us_scale'] = s
        else:
            out[k] = v
    return out


def reference(w0, coef, g, uc, us_bytes, us_scale, vc, vs):
    return core(w0, coef, g, uc, e4m3fn_values(us_bytes) * us_scale.astype(np.float64), vc, vs)

@@ -1,0 +1,259 @@
+from contextlib import ExitStack
+
+import concourse.mybir as mybir
+from concourse.masks import make_identity
+
+N = 2048
+D = 2048
+F = 128
+FLOPS = 4 * 2 * N * N * F
+
+F32 = mybir.dt.float32
+BF16 = mybir.dt.bfloat16
+U32 = mybir.dt.uint32
+U8 = mybir.dt.uint8
+FP8 = mybir.dt.float8_e4m3fn
+FP8X4 = mybir.dt.float8_e4m3fn_x4
+COPY = mybir.ActivationFunctionType.Copy
+MULT = mybir.AluOpType.mult
+ADD = mybir.AluOpType.add
+
+P = 128
+C = 4
+KINDS = "ccuccuccuccuUuUUuUUuUUuU"
+LEAD = 5
+
+
+def tile_fourierftgivenbases_w_kernel(tc, w0, coef, g, uc, us_bytes, us_scale, vc, vs, out):
+    nc = tc.nc
+
+    coef_v = coef.rearrange("(g m t) k -> g t m k", m=P, t=4)
+    uc_v = uc.rearrange("(g m t) k -> g t m k", m=P, t=4)
+    us_v = us_bytes.rearrange("(g m t) k -> g t m k", m=P, t=4)
+    w0_v = w0.rearrange("(g m t) f -> m g t f", m=P, t=4)
+    out_v = out.rearrange("(g m t) f -> g m t f", m=P, t=4)
+
+    pairs = []
+    count = {"c": 0, "u": 0, "U": 0}
+    for kind in KINDS:
+        pairs.append((kind, count[kind]))
+        count[kind] += 1
+    n_pairs = len(pairs)
+    at = {}
+    for s in range(n_pairs):
+        at[pairs[s]] = s
+
+    product_step = {}
+    for k in range(16):
+        product_step[k] = min(at[("u", k // 2)] - 1, (11 * k) // 8)
+    load_step = {}
+    for s in range(n_pairs):
+        kind, q = pairs[s]
+        for j in range(2):
+            load_step[(kind, 2 * q + j)] = (product_step[2 * q + j] - 0.5) if kind == "u" else s
+    order = sorted(load_step, key=lambda key: (load_step[key], key[1]))
+
+    with ExitStack() as ctx:
+        keep = ctx.enter_context(tc.tile_pool(name="keep", bufs=1))
+        stage = ctx.enter_context(tc.tile_pool(name="stage", bufs=2))
+        psum = ctx.enter_context(tc.psum_pool(name="psum", bufs=2))
+
+        ident = keep.tile([P, P], F32, name="ident")
+        make_identity(nc, ident[:])
+
+        graw = keep.tile([P, 4, 4], BF16, name="graw")
+        gpos = keep.tile([P, 16], F32, name="gpos")
+        gneg = keep.tile([P, 16], F32, name="gneg")
+        scale_sb = keep.tile([P, N], F32, name="scale_sb", align_bytes=64)
+        vraw = keep.tile([P, C, 2, 4, F], BF16, name="vraw", align_bytes=64)
+        vgrp = keep.tile([P, C, 2 * F, 4], BF16, name="vgrp", align_bytes=64)
+        vcodes = keep.tile([P, C, 2 * F], U32, name="vcodes", align_bytes=64)
+        vscales = keep.tile([P, C, 2 * F], U8, name="vscales", align_bytes=64)
+        zcodes = keep.tile([P, C, 2 * F], U32, name="zcodes", align_bytes=64)
+        zscales = keep.tile([P, C, 2 * F], U8, name="zscales", align_bytes=64)
+        w0_sb = keep.tile([P, 4, 4, F], BF16, name="w0_sb", align_bytes=64)
+
+        raw = {}
+        codes = {}
+        scales = {}
+        grouped = {}
+        acc = {}
+        zflat = {}
+        zgrp = {}
+
+        def load(key):
+            kind, i = key
+            if kind == "u":
+                usb = stage.tile([P, N], U8, name="usb", bufs=6, align_bytes=64)
+                nc.sync.dma_start(out=usb[:], in_=us_v[i // 4, i % 4])
+                raw[key] = usb
+            else:
+                rt = stage.tile([P, N], BF16, name="raw", bufs=10, align_bytes=64)
+                src = coef_v if kind == "c" else uc_v
+                nc.sync.dma_start(out=rt[:], in_=src[i // 4, i % 4])
+                raw[key] = rt
+
+        def product(k):
+            usp = stage.tile([P, N], BF16, name="usp", bufs=5, align_bytes=64)
+            nc.vector.tensor_tensor(out=usp[:], in0=raw[("u", k)][:].bitcast(FP8), in1=scale_sb[:], op=MULT)
+            raw[("u", k)] = usp
+
+        def turn(s):
+            kind, q = pairs[s]
+            gt = stage.tile([P, 2, C, P, 4], BF16, name="grouped", bufs=3, align_bytes=64)
+            gw = gt[:].bitcast(F32)
+            for j in range(2):
+                words = raw[(kind, 2 * q + j)][:].bitcast(F32)
+                for h in range(2):
+                    xt = psum.tile([P, 2, 2, P], F32, name="xt", bufs=6)
+                    for c in range(2):
+                        for u in range(2):
+                            w = 256 * (2 * h + c)
+                            nc.tensor.transpose(xt[:, c, u, :], words[:, w + u : w + 256 : 2], ident[:])
+                    nc.scalar.copy(out=gw[:, j, 2 * h : 2 * h + 2], in_=xt[:].rearrange("p c u r -> p c r u"))
+            grouped[s] = gt
+
+        def quantize(s):
+            kind, q = pairs[s]
+            if kind == "u":
+                ct = stage.tile([P, 2, C, P], U32, name="us_codes", bufs=8, align_bytes=64)
+                st = stage.tile([P, 2, C, P], U8, name="us_scales", bufs=8, align_bytes=64)
+            elif kind == "c":
+                ct = stage.tile([P, 2, C, P], U32, name="coef_codes", bufs=3, align_bytes=64)
+                st = stage.tile([P, 2, C, P], U8, name="coef_scales", bufs=3, align_bytes=64)
+            else:
+                ct = stage.tile([P, 2, C, P], U32, name="uc_codes", bufs=4, align_bytes=64)
+                st = stage.tile([P, 2, C, P], U8, name="uc_scales", bufs=4, align_bytes=64)
+            nc.vector.quantize_mx(
+                out=ct[:].rearrange("p j c r -> p (j c r)").bitcast(FP8X4),
+                scales=st[:].rearrange("p j c r -> p (j c r)"),
+                in_=grouped[s][:].rearrange("p j c r t -> p (j c r t)"),
+            )
+            codes[(kind, q)] = ct
+            scales[(kind, q)] = st
+
+        def mm(o, kind, i, c, rc, rs, start, stop):
+            nc.tensor.matmul_mx(
+                out=o,
+                lhsT=codes[(kind, i // 2)][:, i % 2, c, :].bitcast(FP8X4),
+                lhsT_scale=scales[(kind, i // 2)][:, i % 2, c, :],
+                rhs=rc.bitcast(FP8X4),
+                rhs_scale=rs,
+                start=start,
+                stop=stop,
+            )
+
+        def stage1(i):
+            bank = psum.tile([P, 2 * F], F32, name="acc", bufs=2)
+            for c in range(C):
+                mm(bank[:], "c", i, c, vcodes[:, c, :], vscales[:, c, :], c == 0, c == C - 1)
+            acc[i] = bank
+
+        def gain(i):
+            gi = i // 4
+            if i % 4 == 0:
+                zflat[gi] = stage.tile([P, 4, 2 * F], BF16, name="zflat", bufs=2, align_bytes=64)
+            zf = zflat[gi]
+            nc.scalar.activation(out=zf[:, i % 4, 0:F], in_=acc[i][:, 0:F], func=COPY, scale=gpos[:, i : i + 1])
+            nc.scalar.activation(
+                out=zf[:, i % 4, F : 2 * F], in_=acc[i][:, F : 2 * F], func=COPY, scale=gneg[:, i : i + 1]
+            )
+            if i % 4 == 3:
+                zg = stage.tile([P, 2 * F, 4], BF16, name="zgrp", bufs=2, align_bytes=64)
+                nc.scalar.copy(out=zg[:], in_=zf[:].rearrange("p t f -> p f t"))
+                zgrp[gi] = zg
+
+        def quantize_z(gi):
+            nc.vector.quantize_mx(
+                out=zcodes[:, gi, :].bitcast(FP8X4),
+                scales=zscales[:, gi, :],
+                in_=zgrp[gi][:].rearrange("p f t -> p (f t)"),
+            )
+
+        def stage2(q):
+            bank = psum.tile([P, 2, F], F32, name="acc", bufs=2)
+            for j in range(2):
+                for c in range(C):
+                    mm(bank[:, j, :], "u", 2 * q + j, c, zcodes[:, c, F : 2 * F], zscales[:, c, F : 2 * F], c == 0, False)
+                for c in range(C):
+                    mm(bank[:, j, :], "U", 2 * q + j, c, zcodes[:, c, 0:F], zscales[:, c, 0:F], False, c == C - 1)
+            acc[("out", q)] = bank
+
+        def epilogue(q):
+            gi, t0 = q // 2, 2 * (q % 2)
+            ot = stage.tile([P, 2, F], F32, name="ot", bufs=4)
+            nc.vector.scalar_tensor_tensor(
+                out=ot[:],
+                in0=acc[("out", q)][:],
+                scalar=0.5,
+                in1=w0_sb[:, gi, t0 : t0 + 2, :],
+                op0=MULT,
+                op1=ADD,
+            )
+            nc.sync.dma_start(out=out_v[gi, :, t0 : t0 + 2, :], in_=ot[:])
+
+        with tc.manual_schedule():
+            todo = list(order)
+            load(todo.pop(0))
+            load(todo.pop(0))
+            nc.sync.dma_start(out=scale_sb[:], in_=us_scale.rearrange("o k -> (o k)").partition_broadcast(P))
+            load(todo.pop(0))
+            load(todo.pop(0))
+            for k, v in ((0, vc), (1, vs)):
+                nc.sync.dma_start(out=vraw[:, :, k, :, :], in_=v.rearrange("(c p j) f -> p c j f", p=P, j=4))
+            nc.sync.dma_start(out=graw[:], in_=g.rearrange("(c p t) -> p c t", p=P, t=4))
+
+            units1 = []
+            units2 = []
+            later = []
+            done1 = 0
+            for s in range(n_pairs + 3):
+                while todo and load_step[todo[0]] <= s + LEAD:
+                    load(todo.pop(0))
+                if s == 10:
+                    nc.sync.dma_start(out=w0_sb[:], in_=w0_v)
+                for k in range(16):
+                    if product_step[k] == s:
+                        product(k)
+                for fn, arg in later:
+                    fn(arg)
+                later = []
+                if s < n_pairs:
+                    turn(s)
+                if 1 <= s <= n_pairs:
+                    quantize(s - 1)
+                if s == 1:
+                    nc.vector.tensor_copy(
+                        out=vgrp[:, :, 0:F, :], in_=vraw[:, :, 0, :, :].rearrange("p c j f -> p c f j")
+                    )
+                    nc.scalar.copy(
+                        out=vgrp[:, :, F : 2 * F, :], in_=vraw[:, :, 1, :, :].rearrange("p c j f -> p c f j")
+                    )
+                    nc.vector.tensor_copy(out=gpos[:], in_=graw[:].rearrange("p c t -> p (c t)"))
+                    nc.vector.tensor_scalar(
+                        out=gneg[:], in0=graw[:].rearrange("p c t -> p (c t)"), scalar1=-1.0, scalar2=None, op0=MULT
+                    )
+                if s == 2:
+                    nc.vector.quantize_mx(
+                        out=vcodes[:].rearrange("p c f -> p (c f)").bitcast(FP8X4),
+                        scales=vscales[:].rearrange("p c f -> p (c f)"),
+                        in_=vgrp[:].rearrange("p c f j -> p (c f j)"),
+                    )
+                if s >= 2 and s - 2 < n_pairs and pairs[s - 2][0] == "c":
+                    units1 += [2 * pairs[s - 2][1], 2 * pairs[s - 2][1] + 1]
+                if s >= 2 and s - 2 < n_pairs and pairs[s - 2][0] == "U":
+                    units2 += [pairs[s - 2][1]]
+                n1 = 0 if s < 3 else len(units1) if (len(units1) < 2 or s >= at[("c", 7)] + 2) else (2 if len(units1) > 2 else 1)
+                for i in units1[:n1]:
+                    stage1(i)
+                    gain(i)
+                    done1 += 1
+                    if i % 4 == 3:
+                        later.append((quantize_z, i // 4))
+                units1 = units1[n1:]
+                if n1 == 0 and s >= at[("c", 7)] + 4:
+                    n2 = len(units2) if s >= n_pairs else 1
+                    for i in units2[:n2]:
+                        stage2(i)
+                        later.append((epilogue, i))
+                    units2 = units2[n2:]

@@ -4,7 +4,6 @@ import concourse.mybir as mybir
 from concourse.masks import make_identity
 
 N = 2048
-D = 2048
 F = 128
 FLOPS = 4 * 2 * N * N * F
 
@@ -19,39 +18,67 @@ MULT = mybir.AluOpType.mult
 ADD = mybir.AluOpType.add
 
 P = 128
-C = 4
-KINDS = "ccuccuccuccuUuUUuUUuUUuU"
-LEAD = 5
+PASSES = 4
+TILES = 16
+BEATS = 16
+BANKS = 6 * BEATS
+RUN = 3
+MX_LAG = 6
+MX_FIRST = 8
+LOAD_AHEAD = 12
+PRODUCT_AHEAD = 9
+ORDER_AHEAD = 7
+GAIN_LAG = 1
+ZQ_LAG = 2
+EPILOGUE_LAG = 2
+V_AT = -1
+SCALAR_ORDERS = range(11, 16)
+VECTOR_ORDERS = range(2, 7)
+SCALAR_WHICH = 1
+RUN_AT = 0
+VECTOR_SPREADS = ()
+RAW_BUFS = 10
+MADE_BUFS = 6
+TURN_BANKS = 6
+HEAD = ["s", "vc", "vs", ("coef", 0), ("coef", 1), ("us", 0), ("coef", 2), ("coef", 3), "g", ("us", 1)]
 
 
 def tile_fourierftgivenbases_w_kernel(tc, w0, coef, g, uc, us_bytes, us_scale, vc, vs, out):
     nc = tc.nc
 
-    coef_v = coef.rearrange("(g m t) k -> g t m k", m=P, t=4)
-    uc_v = uc.rearrange("(g m t) k -> g t m k", m=P, t=4)
-    us_v = us_bytes.rearrange("(g m t) k -> g t m k", m=P, t=4)
+    rows = {
+        "coef": coef.rearrange("(g m t) k -> g t m k", m=P, t=4),
+        "uc": uc.rearrange("(g m t) k -> g t m k", m=P, t=4),
+        "us": us_bytes.rearrange("(g m t) k -> g t m k", m=P, t=4),
+    }
     w0_v = w0.rearrange("(g m t) f -> m g t f", m=P, t=4)
     out_v = out.rearrange("(g m t) f -> g m t f", m=P, t=4)
 
-    pairs = []
-    count = {"c": 0, "u": 0, "U": 0}
-    for kind in KINDS:
-        pairs.append((kind, count[kind]))
-        count[kind] += 1
-    n_pairs = len(pairs)
-    at = {}
-    for s in range(n_pairs):
-        at[pairs[s]] = s
+    sequence = []
+    for beat in range(BEATS):
+        kind = "coef" if beat < BEATS // 2 else "uc"
+        pair = beat % (BEATS // 2)
+        sequence += [(kind, 2 * pair), (kind, 2 * pair + 1)]
+        if kind == "uc":
+            sequence.append(("us", beat))
+        elif beat > 0:
+            sequence.append(("us", beat - 1))
+        if beat == BEATS // 2 - 1:
+            sequence.append(("us", beat))
+    first_bank = {key: 2 * n for n, key in enumerate(sequence)}
+    wide = [key for key in sequence if key[0] != "us"]
+    orderer = {}
+    for beat in SCALAR_ORDERS:
+        orderer[wide[2 * beat + SCALAR_WHICH]] = "scalar"
+    for beat in VECTOR_ORDERS:
+        orderer[wide[2 * beat + 1]] = "vector"
 
-    product_step = {}
-    for k in range(16):
-        product_step[k] = min(at[("u", k // 2)] - 1, (11 * k) // 8)
-    load_step = {}
-    for s in range(n_pairs):
-        kind, q = pairs[s]
-        for j in range(2):
-            load_step[(kind, 2 * q + j)] = (product_step[2 * q + j] - 0.5) if kind == "u" else s
-    order = sorted(load_step, key=lambda key: (load_step[key], key[1]))
+    def first_use(key):
+        if key[0] == "us":
+            return first_bank[key] - PRODUCT_AHEAD
+        if key in orderer:
+            return first_bank[key] - ORDER_AHEAD
+        return first_bank[key]
 
     with ExitStack() as ctx:
         keep = ctx.enter_context(tc.tile_pool(name="keep", bufs=1))
@@ -61,199 +88,310 @@ def tile_fourierftgivenbases_w_kernel(tc, w0, coef, g, uc, us_bytes, us_scale, v
         ident = keep.tile([P, P], F32, name="ident")
         make_identity(nc, ident[:])
 
-        graw = keep.tile([P, 4, 4], BF16, name="graw")
-        gpos = keep.tile([P, 16], F32, name="gpos")
-        gneg = keep.tile([P, 16], F32, name="gneg")
-        scale_sb = keep.tile([P, N], F32, name="scale_sb", align_bytes=64)
-        vraw = keep.tile([P, C, 2, 4, F], BF16, name="vraw", align_bytes=64)
-        vgrp = keep.tile([P, C, 2 * F, 4], BF16, name="vgrp", align_bytes=64)
-        vcodes = keep.tile([P, C, 2 * F], U32, name="vcodes", align_bytes=64)
-        vscales = keep.tile([P, C, 2 * F], U8, name="vscales", align_bytes=64)
-        zcodes = keep.tile([P, C, 2 * F], U32, name="zcodes", align_bytes=64)
-        zscales = keep.tile([P, C, 2 * F], U8, name="zscales", align_bytes=64)
+        gain_raw = keep.tile([P, 4, 4], BF16, name="gain_raw")
+        gain_col = keep.tile([P, TILES], F32, name="gain_col")
+        scale_col = keep.tile([P, TILES], F32, name="scale_col")
+        neg_scale = keep.tile([P, N], F32, name="neg_scale", align_bytes=64)
+        v_grouped = keep.tile([P, PASSES, 2 * F, 4], BF16, name="v_grouped", align_bytes=64)
+        v_codes = keep.tile([P, PASSES, 2 * F], U32, name="v_codes", align_bytes=64)
+        v_scales = keep.tile([P, PASSES, 2 * F], U8, name="v_scales", align_bytes=64)
+        z_codes = keep.tile([P, PASSES, 2 * F], U32, name="z_codes", align_bytes=64)
+        z_scales = keep.tile([P, PASSES, 2 * F], U8, name="z_scales", align_bytes=64)
         w0_sb = keep.tile([P, 4, 4, F], BF16, name="w0_sb", align_bytes=64)
 
         raw = {}
+        grouped = {}
         codes = {}
         scales = {}
-        grouped = {}
-        acc = {}
-        zflat = {}
-        zgrp = {}
+        sums = {}
+        z_flat = {}
+        z_grouped = {}
+        results = {}
 
-        def load(key):
+        def load(key, pieces=1):
             kind, i = key
-            if kind == "u":
-                usb = stage.tile([P, N], U8, name="usb", bufs=6, align_bytes=64)
-                nc.sync.dma_start(out=usb[:], in_=us_v[i // 4, i % 4])
-                raw[key] = usb
+            if kind == "us":
+                tile = stage.tile([P, N], U8, name="us_raw", bufs=4, align_bytes=64)
             else:
-                rt = stage.tile([P, N], BF16, name="raw", bufs=10, align_bytes=64)
-                src = coef_v if kind == "c" else uc_v
-                nc.sync.dma_start(out=rt[:], in_=src[i // 4, i % 4])
-                raw[key] = rt
+                tile = stage.tile([P, N], BF16, name="raw", bufs=RAW_BUFS, align_bytes=64)
+            width = N // pieces
+            for j in range(pieces):
+                cols = slice(j * width, (j + 1) * width)
+                nc.sync.dma_start(out=tile[:, cols], in_=rows[kind][i // 4, i % 4][:, cols])
+            raw[key] = tile
 
-        def product(k):
-            usp = stage.tile([P, N], BF16, name="usp", bufs=5, align_bytes=64)
-            nc.vector.tensor_tensor(out=usp[:], in0=raw[("u", k)][:].bitcast(FP8), in1=scale_sb[:], op=MULT)
-            raw[("u", k)] = usp
-
-        def turn(s):
-            kind, q = pairs[s]
-            gt = stage.tile([P, 2, C, P, 4], BF16, name="grouped", bufs=3, align_bytes=64)
-            gw = gt[:].bitcast(F32)
-            for j in range(2):
-                words = raw[(kind, 2 * q + j)][:].bitcast(F32)
-                for h in range(2):
-                    xt = psum.tile([P, 2, 2, P], F32, name="xt", bufs=6)
-                    for c in range(2):
-                        for u in range(2):
-                            w = 256 * (2 * h + c)
-                            nc.tensor.transpose(xt[:, c, u, :], words[:, w + u : w + 256 : 2], ident[:])
-                    nc.scalar.copy(out=gw[:, j, 2 * h : 2 * h + 2], in_=xt[:].rearrange("p c u r -> p c r u"))
-            grouped[s] = gt
-
-        def quantize(s):
-            kind, q = pairs[s]
-            if kind == "u":
-                ct = stage.tile([P, 2, C, P], U32, name="us_codes", bufs=8, align_bytes=64)
-                st = stage.tile([P, 2, C, P], U8, name="us_scales", bufs=8, align_bytes=64)
-            elif kind == "c":
-                ct = stage.tile([P, 2, C, P], U32, name="coef_codes", bufs=3, align_bytes=64)
-                st = stage.tile([P, 2, C, P], U8, name="coef_scales", bufs=3, align_bytes=64)
-            else:
-                ct = stage.tile([P, 2, C, P], U32, name="uc_codes", bufs=4, align_bytes=64)
-                st = stage.tile([P, 2, C, P], U8, name="uc_scales", bufs=4, align_bytes=64)
-            nc.vector.quantize_mx(
-                out=ct[:].rearrange("p j c r -> p (j c r)").bitcast(FP8X4),
-                scales=st[:].rearrange("p j c r -> p (j c r)"),
-                in_=grouped[s][:].rearrange("p j c r t -> p (j c r t)"),
+        def load_v(name, v):
+            tile = stage.tile([P, N], BF16, name="raw", bufs=RAW_BUFS, align_bytes=64)
+            nc.sync.dma_start(
+                out=tile[:].rearrange("p (c j f) -> p c j f", c=PASSES, j=4),
+                in_=v.rearrange("(c p j) f -> p c j f", p=P, j=4),
             )
-            codes[(kind, q)] = ct
-            scales[(kind, q)] = st
+            raw[name] = tile
 
-        def mm(o, kind, i, c, rc, rs, start, stop):
+        def load_w0():
+            nc.sync.dma_start(out=w0_sb[:], in_=w0_v)
+
+        def spread_scale():
+            spread = neg_scale[:].rearrange("p (n m) -> p n m", m=TILES)
+            for b in range(4):
+                bank = psum.tile([P, 4, P], F32, name="turned", bufs=TURN_BANKS)
+                for j in range(4):
+                    m = 4 * b + j
+                    nc.tensor.transpose(bank[:, j, :], scale_col[:, m : m + 1].to_broadcast([P, P]), ident[:])
+                src = bank[:].rearrange("p j n -> p n j")
+                dst = spread[:, :, 4 * b : 4 * b + 4]
+                if b in VECTOR_SPREADS:
+                    nc.vector.tensor_scalar(out=dst, in0=src, scalar1=-1.0, scalar2=None, op0=MULT)
+                else:
+                    nc.scalar.activation(out=dst, in_=src, func=COPY, scale=-1.0)
+
+        def prepare_v():
+            for half, name in enumerate(("vc", "vs")):
+                nc.vector.tensor_copy(
+                    out=v_grouped[:, :, half * F : (half + 1) * F, :],
+                    in_=raw[name][:].rearrange("p (c j f) -> p c f j", c=PASSES, j=4),
+                )
+            nc.vector.quantize_mx(
+                out=v_codes[:].rearrange("p c f -> p (c f)").bitcast(FP8X4),
+                scales=v_scales[:].rearrange("p c f -> p (c f)"),
+                in_=v_grouped[:].rearrange("p c f j -> p (c f j)"),
+            )
+
+        def widen_gain():
+            nc.vector.tensor_copy(out=gain_col[:], in_=gain_raw[:].rearrange("p c t -> p (c t)"))
+
+        def product(key):
+            tile = stage.tile([P, N], BF16, name="made", bufs=MADE_BUFS, align_bytes=64)
+            nc.vector.tensor_tensor(out=tile[:], in0=raw[key][:].bitcast(FP8), in1=neg_scale[:], op=MULT)
+            raw[key] = tile
+
+        def order_words(key):
+            tile = stage.tile([P, N], BF16, name="made", bufs=MADE_BUFS, align_bytes=64)
+            dst = tile[:].bitcast(F32).rearrange("p (u w) -> p u w", u=2)
+            src = raw[key][:].bitcast(F32).rearrange("p (w u) -> p u w", u=2)
+            if orderer[key] == "scalar":
+                nc.scalar.copy(out=dst, in_=src)
+            else:
+                nc.vector.tensor_copy(out=dst, in_=src)
+            raw[key] = tile
+
+        def turn_bank(b):
+            key = sequence[b // 2]
+            kind, i = key
+            h = b % 2
+            if h == 0 and kind == "us":
+                grouped[key] = stage.tile([P, 4 * PASSES * P], BF16, name="us_grouped", bufs=3, align_bytes=64)[:]
+            elif h == 0 and i % 2 == 0:
+                both = stage.tile([P, 2, 4 * PASSES * P], BF16, name="grouped", bufs=3, align_bytes=64)
+                grouped[(kind, i)] = both[:, 0, :]
+                grouped[(kind, i + 1)] = both[:, 1, :]
+                grouped[(kind, "pair", i // 2)] = both[:].rearrange("p j n -> p (j n)")
+            words = raw[key][:].bitcast(F32)
+            bank = psum.tile([P, 2, 2, P], F32, name="turned", bufs=TURN_BANKS)
+            for c in range(2):
+                for u in range(2):
+                    first = 256 * (2 * h + c)
+                    if key in orderer:
+                        src = words[:, 512 * u + first // 2 : 512 * u + first // 2 + P]
+                    else:
+                        src = words[:, first + u : first + 256 : 2]
+                    nc.tensor.transpose(bank[:, c, u, :], src, ident[:])
+            dst = grouped[key].bitcast(F32).rearrange("p (c r u) -> p c r u", c=PASSES, u=2)
+            nc.scalar.copy(out=dst[:, 2 * h : 2 * h + 2], in_=bank[:].rearrange("p c u r -> p c r u"))
+
+        def code_tiles(kind, first, count):
+            depth = BEATS // 2 + 2 if kind == "us" else 4
+            ct = stage.tile([P, count * PASSES * P], U32, name=kind + "_codes", bufs=depth, align_bytes=64)
+            st = stage.tile([P, count * PASSES * P], U8, name=kind + "_scales", bufs=depth, align_bytes=64)
+            for j in range(count):
+                codes[(kind, first + j)] = ct[:, j * PASSES * P : (j + 1) * PASSES * P]
+                scales[(kind, first + j)] = st[:, j * PASSES * P : (j + 1) * PASSES * P]
+            return ct, st
+
+        def quantize_pair(kind, pair):
+            ct, st = code_tiles(kind, 2 * pair, 2)
+            nc.vector.quantize_mx(out=ct[:].bitcast(FP8X4), scales=st[:], in_=grouped[(kind, "pair", pair)])
+
+        def quantize_part(key, first, count):
+            nc.vector.quantize_mx(
+                out=codes[key][:, first * P : (first + count) * P].bitcast(FP8X4),
+                scales=scales[key][:, first * P : (first + count) * P],
+                in_=grouped[key][:, 4 * first * P : 4 * (first + count) * P],
+            )
+
+        def quantize_us(i):
+            code_tiles("us", i, 1)
+            quantize_part(("us", i), 0, PASSES)
+
+        def mm(o, key, c, moving, moving_scales, start, stop):
             nc.tensor.matmul_mx(
                 out=o,
-                lhsT=codes[(kind, i // 2)][:, i % 2, c, :].bitcast(FP8X4),
-                lhsT_scale=scales[(kind, i // 2)][:, i % 2, c, :],
-                rhs=rc.bitcast(FP8X4),
-                rhs_scale=rs,
+                lhsT=codes[key][:, c * P : (c + 1) * P].bitcast(FP8X4),
+                lhsT_scale=scales[key][:, c * P : (c + 1) * P],
+                rhs=moving.bitcast(FP8X4),
+                rhs_scale=moving_scales,
                 start=start,
                 stop=stop,
             )
 
         def stage1(i):
-            bank = psum.tile([P, 2 * F], F32, name="acc", bufs=2)
-            for c in range(C):
-                mm(bank[:], "c", i, c, vcodes[:, c, :], vscales[:, c, :], c == 0, c == C - 1)
-            acc[i] = bank
+            if i % 2 == 0:
+                sums[("r", i // 2)] = psum.tile([P, 2, 2 * F], F32, name="sums", bufs=2)
+            o = sums[("r", i // 2)][:, i % 2, :]
+            for c in range(PASSES):
+                mm(o, ("coef", i), c, v_codes[:, c, :], v_scales[:, c, :], c == 0, c == PASSES - 1)
 
-        def gain(i):
-            gi = i // 4
-            if i % 4 == 0:
-                zflat[gi] = stage.tile([P, 4, 2 * F], BF16, name="zflat", bufs=2, align_bytes=64)
-            zf = zflat[gi]
-            nc.scalar.activation(out=zf[:, i % 4, 0:F], in_=acc[i][:, 0:F], func=COPY, scale=gpos[:, i : i + 1])
-            nc.scalar.activation(
-                out=zf[:, i % 4, F : 2 * F], in_=acc[i][:, F : 2 * F], func=COPY, scale=gneg[:, i : i + 1]
-            )
-            if i % 4 == 3:
-                zg = stage.tile([P, 2 * F, 4], BF16, name="zgrp", bufs=2, align_bytes=64)
-                nc.scalar.copy(out=zg[:], in_=zf[:].rearrange("p t f -> p f t"))
-                zgrp[gi] = zg
-
-        def quantize_z(gi):
-            nc.vector.quantize_mx(
-                out=zcodes[:, gi, :].bitcast(FP8X4),
-                scales=zscales[:, gi, :],
-                in_=zgrp[gi][:].rearrange("p f t -> p (f t)"),
-            )
-
-        def stage2(q):
-            bank = psum.tile([P, 2, F], F32, name="acc", bufs=2)
+        def gains(pair):
+            if pair % 2 == 0:
+                z_flat[pair // 2] = stage.tile([P, 4, 2 * F], BF16, name="z_flat", bufs=2, align_bytes=64)
             for j in range(2):
-                for c in range(C):
-                    mm(bank[:, j, :], "u", 2 * q + j, c, zcodes[:, c, F : 2 * F], zscales[:, c, F : 2 * F], c == 0, False)
-                for c in range(C):
-                    mm(bank[:, j, :], "U", 2 * q + j, c, zcodes[:, c, 0:F], zscales[:, c, 0:F], False, c == C - 1)
-            acc[("out", q)] = bank
+                i = 2 * pair + j
+                nc.scalar.activation(
+                    out=z_flat[i // 4][:, i % 4, :],
+                    in_=sums[("r", pair)][:, j, :],
+                    func=COPY,
+                    scale=gain_col[:, i : i + 1],
+                )
 
-        def epilogue(q):
-            gi, t0 = q // 2, 2 * (q % 2)
-            ot = stage.tile([P, 2, F], F32, name="ot", bufs=4)
+        def group_z(c):
+            z_grouped[c] = stage.tile([P, 2 * F, 4], BF16, name="z_grouped", bufs=2, align_bytes=64)
+            nc.scalar.copy(out=z_grouped[c][:], in_=z_flat[c][:].rearrange("p t f -> p f t"))
+
+        def quantize_z(c):
+            nc.vector.quantize_mx(
+                out=z_codes[:, c, :].bitcast(FP8X4),
+                scales=z_scales[:, c, :],
+                in_=z_grouped[c][:].rearrange("p f t -> p (f t)"),
+            )
+
+        def open_sums(tiles, tag, depth):
+            bank = psum.tile([P, 2, F], F32, name=tag, bufs=depth)
+            sums[("out", tiles)] = bank
+            for j, i in enumerate(tiles):
+                sums[("out", i)] = bank[:, j, :]
+
+        def stage2(i, kinds, passes, start, stop):
+            todo = [(kind, c) for kind in kinds for c in passes]
+            for n, (kind, c) in enumerate(todo):
+                half = slice(F, 2 * F) if kind == "us" else slice(0, F)
+                mm(
+                    sums[("out", i)],
+                    (kind, i),
+                    c,
+                    z_codes[:, c, half],
+                    z_scales[:, c, half],
+                    start and n == 0,
+                    stop and n == len(todo) - 1,
+                )
+
+        def stage2_tile(i):
+            if i % 2 == 0:
+                open_sums((i, i + 1), "sums", 2)
+            if i < 2:
+                stage2(i, ("us", "uc"), range(PASSES - 1), i == 0, False)
+                return
+            if i == 2:
+                stage2(0, ("us", "uc"), [PASSES - 1], False, False)
+                stage2(1, ("us", "uc"), [PASSES - 1], False, True)
+            stage2(i, ("us", "uc"), range(PASSES), True, True)
+
+        def epilogue(tiles):
+            i, count = tiles[0], len(tiles)
+            results[tiles] = stage.tile([P, count, F], F32, name="result", bufs=4)
             nc.vector.scalar_tensor_tensor(
-                out=ot[:],
-                in0=acc[("out", q)][:],
+                out=results[tiles][:],
+                in0=sums[("out", tiles)][:, 0:count, :],
                 scalar=0.5,
-                in1=w0_sb[:, gi, t0 : t0 + 2, :],
+                in1=w0_sb[:, i // 4, i % 4 : i % 4 + count, :],
                 op0=MULT,
                 op1=ADD,
             )
-            nc.sync.dma_start(out=out_v[gi, :, t0 : t0 + 2, :], in_=ot[:])
+
+        def store(tiles):
+            i, count = tiles[0], len(tiles)
+            nc.sync.dma_start(out=out_v[i // 4, :, i % 4 : i % 4 + count, :], in_=results[tiles][:])
+
+        after = {b: [] for b in range(-1, BANKS)}
+
+        def plan(b, fn, *args):
+            after[min(max(b, -1), BANKS - 1)].append((fn, args))
+
+        bursts = []
+        for n, key in enumerate(wide):
+            ready = first_bank[wide[n - n % 2 + 1]] + 1 + MX_LAG
+            if key[0] == "uc":
+                ready = max(ready, first_bank[("us", key[1])] + 1 + MX_LAG)
+            b = max(ready, MX_FIRST)
+            b += (RUN_AT - b) % RUN
+            if n % 2 == 1:
+                b = max(b, bursts[-1] + RUN)
+            bursts.append(b)
+
+        def burst(n):
+            return bursts[n]
+
+        for key in sorted(sequence, key=first_use):
+            if key not in HEAD:
+                plan(first_use(key) - LOAD_AHEAD, load, key)
+        plan(BANKS // 2 - LOAD_AHEAD, load_w0)
+        for n in range(0, len(wide) - 2, 2):
+            kind, i = wide[n]
+            plan(first_bank[wide[n + 1]] + 1, quantize_pair, kind, i // 2)
+        for i in range(TILES - 1):
+            plan(first_bank[("us", i)] + 1, quantize_us, i)
+        for c in range(PASSES):
+            plan(burst(4 * c + 3) + GAIN_LAG + ZQ_LAG, quantize_z, c)
+        for pair in range(TILES // 2 - 2):
+            b = burst(TILES + max(2 * pair + 1, 2)) + EPILOGUE_LAG
+            plan(b, epilogue, (2 * pair, 2 * pair + 1))
+            plan(b + 3, store, (2 * pair, 2 * pair + 1))
+        plan(V_AT, prepare_v)
+        plan(3, widen_gain)
+        for key in sequence:
+            if key[0] == "us":
+                plan(first_use(key), product, key)
+            elif key in orderer:
+                plan(first_use(key), order_words, key)
+        for i in range(TILES):
+            plan(burst(i), stage1, i)
+        for pair in range(TILES // 2):
+            plan(burst(2 * pair + 1) + GAIN_LAG, gains, pair)
+        for c in range(PASSES):
+            plan(burst(4 * c + 3) + GAIN_LAG + 1, group_z, c)
+        for i in range(TILES - 2):
+            plan(min(burst(TILES + i), BANKS - 4), stage2_tile, i)
+        a, z = TILES - 2, TILES - 1
+        plan(first_bank[("uc", a)] + 1, code_tiles, "uc", a, 2)
+        plan(first_bank[("uc", a)] + 1, quantize_part, ("uc", a), 0, PASSES)
+        plan(first_bank[("uc", z)] + 1, quantize_part, ("uc", z), 0, PASSES)
+        plan(BANKS - 3, epilogue, (TILES - 4, TILES - 3))
+        plan(BANKS - 2, code_tiles, "us", z, 1)
+        plan(BANKS - 2, quantize_part, ("us", z), 0, 2)
+        plan(BANKS - 1, store, (TILES - 4, TILES - 3))
+        plan(BANKS - 1, quantize_part, ("us", z), 2, 2)
+        plan(BANKS - 1, open_sums, (a,), "sums", 2)
+        plan(BANKS - 1, stage2, a, ("uc", "us"), range(PASSES), True, True)
+        plan(BANKS - 1, open_sums, (z,), "sums", 2)
+        plan(BANKS - 1, stage2, z, ("uc", "us"), range(PASSES), True, True)
+        for i in (a, z):
+            plan(BANKS - 1, epilogue, (i,))
+            plan(BANKS - 1, store, (i,))
 
         with tc.manual_schedule():
-            todo = list(order)
-            load(todo.pop(0))
-            load(todo.pop(0))
-            nc.sync.dma_start(out=scale_sb[:], in_=us_scale.rearrange("o k -> (o k)").partition_broadcast(P))
-            load(todo.pop(0))
-            load(todo.pop(0))
-            for k, v in ((0, vc), (1, vs)):
-                nc.sync.dma_start(out=vraw[:, :, k, :, :], in_=v.rearrange("(c p j) f -> p c j f", p=P, j=4))
-            nc.sync.dma_start(out=graw[:], in_=g.rearrange("(c p t) -> p c t", p=P, t=4))
-
-            units1 = []
-            units2 = []
-            later = []
-            done1 = 0
-            for s in range(n_pairs + 3):
-                while todo and load_step[todo[0]] <= s + LEAD:
-                    load(todo.pop(0))
-                if s == 10:
-                    nc.sync.dma_start(out=w0_sb[:], in_=w0_v)
-                for k in range(16):
-                    if product_step[k] == s:
-                        product(k)
-                for fn, arg in later:
-                    fn(arg)
-                later = []
-                if s < n_pairs:
-                    turn(s)
-                if 1 <= s <= n_pairs:
-                    quantize(s - 1)
-                if s == 1:
-                    nc.vector.tensor_copy(
-                        out=vgrp[:, :, 0:F, :], in_=vraw[:, :, 0, :, :].rearrange("p c j f -> p c f j")
-                    )
-                    nc.scalar.copy(
-                        out=vgrp[:, :, F : 2 * F, :], in_=vraw[:, :, 1, :, :].rearrange("p c j f -> p c f j")
-                    )
-                    nc.vector.tensor_copy(out=gpos[:], in_=graw[:].rearrange("p c t -> p (c t)"))
-                    nc.vector.tensor_scalar(
-                        out=gneg[:], in0=graw[:].rearrange("p c t -> p (c t)"), scalar1=-1.0, scalar2=None, op0=MULT
-                    )
-                if s == 2:
-                    nc.vector.quantize_mx(
-                        out=vcodes[:].rearrange("p c f -> p (c f)").bitcast(FP8X4),
-                        scales=vscales[:].rearrange("p c f -> p (c f)"),
-                        in_=vgrp[:].rearrange("p c f j -> p (c f j)"),
-                    )
-                if s >= 2 and s - 2 < n_pairs and pairs[s - 2][0] == "c":
-                    units1 += [2 * pairs[s - 2][1], 2 * pairs[s - 2][1] + 1]
-                if s >= 2 and s - 2 < n_pairs and pairs[s - 2][0] == "U":
-                    units2 += [pairs[s - 2][1]]
-                n1 = 0 if s < 3 else len(units1) if (len(units1) < 2 or s >= at[("c", 7)] + 2) else (2 if len(units1) > 2 else 1)
-                for i in units1[:n1]:
-                    stage1(i)
-                    gain(i)
-                    done1 += 1
-                    if i % 4 == 3:
-                        later.append((quantize_z, i // 4))
-                units1 = units1[n1:]
-                if n1 == 0 and s >= at[("c", 7)] + 4:
-                    n2 = len(units2) if s >= n_pairs else 1
-                    for i in units2[:n2]:
-                        stage2(i)
-                        later.append((epilogue, i))
-                    units2 = units2[n2:]
+            for key in HEAD:
+                if key == "s":
+                    nc.sync.dma_start(out=scale_col[:], in_=us_scale.rearrange("o (n m) -> (o n) m", m=TILES))
+                elif key == "g":
+                    nc.sync.dma_start(out=gain_raw[:], in_=g.rearrange("(c p t) -> p c t", p=P, t=4))
+                elif key == "vc":
+                    load_v("vc", vc)
+                elif key == "vs":
+                    load_v("vs", vs)
+                else:
+                    load(key, 2 if key == ("coef", 0) else 1)
+            spread_scale()
+            for b in range(-1, BANKS):
+                if b >= 0:
+                    turn_bank(b)
+                for fn, args in after[b]:
+                    fn(*args)

@@ -23,7 +23,7 @@ TILES = 16
 BEATS = 16
 BANKS = 6 * BEATS
 RUN = 3
-MX_LAG = 6
+MX_LAG = 5
 MX_FIRST = 8
 LOAD_AHEAD = 12
 PRODUCT_AHEAD = 9
@@ -32,11 +32,13 @@ GAIN_LAG = 1
 ZQ_LAG = 2
 EPILOGUE_LAG = 2
 V_AT = -1
+GAIN_AT = 4
 SCALAR_ORDERS = range(11, 16)
-VECTOR_ORDERS = range(2, 7)
+VECTOR_ORDERS = range(2, 6, 2)
 SCALAR_WHICH = 1
-RUN_AT = 0
-VECTOR_SPREADS = ()
+VC_AT = (-1, "vector")
+VS_AT = (-1, "vector")
+US_AFTER = [3, 5, 7, 9, 11, 13, 15, 15, 17, 19, 21, 23, 25, 27, 29, 31]
 RAW_BUFS = 10
 MADE_BUFS = 6
 TURN_BANKS = 6
@@ -55,16 +57,12 @@ def tile_fourierftgivenbases_w_kernel(tc, w0, coef, g, uc, us_bytes, us_scale, v
     out_v = out.rearrange("(g m t) f -> g m t f", m=P, t=4)
 
     sequence = []
-    for beat in range(BEATS):
-        kind = "coef" if beat < BEATS // 2 else "uc"
-        pair = beat % (BEATS // 2)
-        sequence += [(kind, 2 * pair), (kind, 2 * pair + 1)]
-        if kind == "uc":
-            sequence.append(("us", beat))
-        elif beat > 0:
-            sequence.append(("us", beat - 1))
-        if beat == BEATS // 2 - 1:
-            sequence.append(("us", beat))
+    us_next = 0
+    for n in range(2 * TILES):
+        sequence.append(("coef", n) if n < TILES else ("uc", n - TILES))
+        for j in range(US_AFTER.count(n)):
+            sequence.append(("us", us_next))
+            us_next += 1
     first_bank = {key: 2 * n for n, key in enumerate(sequence)}
     wide = [key for key in sequence if key[0] != "us"]
     orderer = {}
@@ -138,19 +136,19 @@ def tile_fourierftgivenbases_w_kernel(tc, w0, coef, g, uc, us_bytes, us_scale, v
                 for j in range(4):
                     m = 4 * b + j
                     nc.tensor.transpose(bank[:, j, :], scale_col[:, m : m + 1].to_broadcast([P, P]), ident[:])
-                src = bank[:].rearrange("p j n -> p n j")
-                dst = spread[:, :, 4 * b : 4 * b + 4]
-                if b in VECTOR_SPREADS:
-                    nc.vector.tensor_scalar(out=dst, in0=src, scalar1=-1.0, scalar2=None, op0=MULT)
-                else:
-                    nc.scalar.activation(out=dst, in_=src, func=COPY, scale=-1.0)
-
-        def prepare_v():
-            for half, name in enumerate(("vc", "vs")):
-                nc.vector.tensor_copy(
-                    out=v_grouped[:, :, half * F : (half + 1) * F, :],
-                    in_=raw[name][:].rearrange("p (c j f) -> p c f j", c=PASSES, j=4),
+                nc.scalar.activation(
+                    out=spread[:, :, 4 * b : 4 * b + 4], in_=bank[:].rearrange("p j n -> p n j"), func=COPY, scale=-1.0
                 )
+
+        def group_v(half, engine):
+            dst = v_grouped[:, :, half * F : (half + 1) * F, :]
+            src = raw[("vc", "vs")[half]][:].rearrange("p (c j f) -> p c f j", c=PASSES, j=4)
+            if engine == "scalar":
+                nc.scalar.copy(out=dst, in_=src)
+            else:
+                nc.vector.tensor_copy(out=dst, in_=src)
+
+        def quantize_v():
             nc.vector.quantize_mx(
                 out=v_codes[:].rearrange("p c f -> p (c f)").bitcast(FP8X4),
                 scales=v_scales[:].rearrange("p c f -> p (c f)"),
@@ -316,16 +314,15 @@ def tile_fourierftgivenbases_w_kernel(tc, w0, coef, g, uc, us_bytes, us_scale, v
         def plan(b, fn, *args):
             after[min(max(b, -1), BANKS - 1)].append((fn, args))
 
+        points = list(range(MX_FIRST, BANKS - 2, RUN))
         bursts = []
-        for n, key in enumerate(wide):
+        for n, key in enumerate(wide[:-2]):
             ready = first_bank[wide[n - n % 2 + 1]] + 1 + MX_LAG
             if key[0] == "uc":
                 ready = max(ready, first_bank[("us", key[1])] + 1 + MX_LAG)
-            b = max(ready, MX_FIRST)
-            b += (RUN_AT - b) % RUN
-            if n % 2 == 1:
-                b = max(b, bursts[-1] + RUN)
-            bursts.append(b)
+            while len(points) > 1 and points[0] < max(ready, MX_FIRST):
+                points.pop(0)
+            bursts.append(points.pop(0) if len(points) > 1 else points[0])
 
         def burst(n):
             return bursts[n]
@@ -345,8 +342,10 @@ def tile_fourierftgivenbases_w_kernel(tc, w0, coef, g, uc, us_bytes, us_scale, v
             b = burst(TILES + max(2 * pair + 1, 2)) + EPILOGUE_LAG
             plan(b, epilogue, (2 * pair, 2 * pair + 1))
             plan(b + 3, store, (2 * pair, 2 * pair + 1))
-        plan(V_AT, prepare_v)
-        plan(3, widen_gain)
+        plan(VC_AT[0], group_v, 0, VC_AT[1])
+        plan(VS_AT[0], group_v, 1, VS_AT[1])
+        plan(V_AT, quantize_v)
+        plan(GAIN_AT, widen_gain)
         for key in sequence:
             if key[0] == "us":
                 plan(first_use(key), product, key)
@@ -358,24 +357,23 @@ def tile_fourierftgivenbases_w_kernel(tc, w0, coef, g, uc, us_bytes, us_scale, v
             plan(burst(2 * pair + 1) + GAIN_LAG, gains, pair)
         for c in range(PASSES):
             plan(burst(4 * c + 3) + GAIN_LAG + 1, group_z, c)
-        for i in range(TILES - 2):
-            plan(min(burst(TILES + i), BANKS - 4), stage2_tile, i)
+        for i in range(TILES - 3):
+            plan(burst(TILES + i), stage2_tile, i)
         a, z = TILES - 2, TILES - 1
         plan(first_bank[("uc", a)] + 1, code_tiles, "uc", a, 2)
         plan(first_bank[("uc", a)] + 1, quantize_part, ("uc", a), 0, PASSES)
         plan(first_bank[("uc", z)] + 1, quantize_part, ("uc", z), 0, PASSES)
-        plan(BANKS - 3, epilogue, (TILES - 4, TILES - 3))
         plan(BANKS - 2, code_tiles, "us", z, 1)
         plan(BANKS - 2, quantize_part, ("us", z), 0, 2)
-        plan(BANKS - 1, store, (TILES - 4, TILES - 3))
         plan(BANKS - 1, quantize_part, ("us", z), 2, 2)
+        plan(BANKS - 1, stage2_tile, TILES - 3)
         plan(BANKS - 1, open_sums, (a,), "sums", 2)
         plan(BANKS - 1, stage2, a, ("uc", "us"), range(PASSES), True, True)
-        plan(BANKS - 1, open_sums, (z,), "sums", 2)
+        plan(BANKS - 1, open_sums, (z,), "turned", TURN_BANKS)
         plan(BANKS - 1, stage2, z, ("uc", "us"), range(PASSES), True, True)
-        for i in (a, z):
-            plan(BANKS - 1, epilogue, (i,))
-            plan(BANKS - 1, store, (i,))
+        for tiles in ((TILES - 4, TILES - 3), (a,), (z,)):
+            plan(BANKS - 1, epilogue, tiles)
+            plan(BANKS - 1, store, tiles)
 
         with tc.manual_schedule():
             for key in HEAD:

@@ -23,26 +23,24 @@ TILES = 16
 BEATS = 16
 BANKS = 6 * BEATS
 RUN = 3
-MX_LAG = 5
-MX_FIRST = 8
-LOAD_AHEAD = 12
-PRODUCT_AHEAD = 9
-ORDER_AHEAD = 7
-GAIN_LAG = 1
-ZQ_LAG = 2
-EPILOGUE_LAG = 2
-V_AT = -1
-GAIN_AT = 4
+SINGLE_HEAD = 4
+SINGLE_TAIL = 6
+VS_ENGINE = "vector"
+LOAD_AHEAD = 8
+PRODUCT_PACE = (14, 5)
+PRODUCT_START = -1
+VECTOR_GROUPS = [3]
+LONG_RUNS = []
+ORDER_AHEAD = {"scalar": 7, "vector": 10}
+GAIN_AT = 10
 SCALAR_ORDERS = range(11, 16)
-VECTOR_ORDERS = range(2, 6, 2)
+VECTOR_ORDERS = [3, 5]
 SCALAR_WHICH = 1
-VC_AT = (-1, "vector")
-VS_AT = (-1, "vector")
 US_AFTER = [3, 5, 7, 9, 11, 13, 15, 15, 17, 19, 21, 23, 25, 27, 29, 31]
 RAW_BUFS = 10
 MADE_BUFS = 6
 TURN_BANKS = 6
-HEAD = ["s", "vc", "vs", ("coef", 0), ("coef", 1), ("us", 0), ("coef", 2), ("coef", 3), "g", ("us", 1)]
+HEAD = ["s", "vc", "vs", ("coef", 0), ("coef", 1), ("us", 0), ("coef", 2), ("coef", 3), ("us", 1)]
 
 
 def tile_fourierftgivenbases_w_kernel(tc, w0, coef, g, uc, us_bytes, us_scale, vc, vs, out):
@@ -71,11 +69,14 @@ def tile_fourierftgivenbases_w_kernel(tc, w0, coef, g, uc, us_bytes, us_scale, v
     for beat in VECTOR_ORDERS:
         orderer[wide[2 * beat + 1]] = "vector"
 
+    def product_slot(h):
+        return (PRODUCT_PACE[0] * h) // PRODUCT_PACE[1] + PRODUCT_START
+
     def first_use(key):
         if key[0] == "us":
-            return first_bank[key] - PRODUCT_AHEAD
+            return product_slot(2 * key[1])
         if key in orderer:
-            return first_bank[key] - ORDER_AHEAD
+            return first_bank[key] - ORDER_AHEAD[orderer[key]]
         return first_bank[key]
 
     with ExitStack() as ctx:
@@ -98,7 +99,9 @@ def tile_fourierftgivenbases_w_kernel(tc, w0, coef, g, uc, us_bytes, us_scale, v
         w0_sb = keep.tile([P, 4, 4, F], BF16, name="w0_sb", align_bytes=64)
 
         raw = {}
+        made = {}
         grouped = {}
+        turned = {}
         codes = {}
         scales = {}
         sums = {}
@@ -125,6 +128,9 @@ def tile_fourierftgivenbases_w_kernel(tc, w0, coef, g, uc, us_bytes, us_scale, v
                 in_=v.rearrange("(c p j) f -> p c j f", p=P, j=4),
             )
             raw[name] = tile
+
+        def load_gain():
+            nc.sync.dma_start(out=gain_raw[:], in_=g.rearrange("(c p t) -> p c t", p=P, t=4))
 
         def load_w0():
             nc.sync.dma_start(out=w0_sb[:], in_=w0_v)
@@ -158,10 +164,15 @@ def tile_fourierftgivenbases_w_kernel(tc, w0, coef, g, uc, us_bytes, us_scale, v
         def widen_gain():
             nc.vector.tensor_copy(out=gain_col[:], in_=gain_raw[:].rearrange("p c t -> p (c t)"))
 
-        def product(key):
-            tile = stage.tile([P, N], BF16, name="made", bufs=MADE_BUFS, align_bytes=64)
-            nc.vector.tensor_tensor(out=tile[:], in0=raw[key][:].bitcast(FP8), in1=neg_scale[:], op=MULT)
-            raw[key] = tile
+        def product(i, part):
+            if part == 0:
+                made[i] = stage.tile([P, N], BF16, name="made", bufs=MADE_BUFS, align_bytes=64)
+            cols = slice(part * N // 2, (part + 1) * N // 2)
+            nc.vector.tensor_tensor(
+                out=made[i][:, cols], in0=raw[("us", i)][:, cols].bitcast(FP8), in1=neg_scale[:, cols], op=MULT
+            )
+            if part == 1:
+                raw[("us", i)] = made[i]
 
         def order_words(key):
             tile = stage.tile([P, N], BF16, name="made", bufs=MADE_BUFS, align_bytes=64)
@@ -194,8 +205,12 @@ def tile_fourierftgivenbases_w_kernel(tc, w0, coef, g, uc, us_bytes, us_scale, v
                     else:
                         src = words[:, first + u : first + 256 : 2]
                     nc.tensor.transpose(bank[:, c, u, :], src, ident[:])
-            dst = grouped[key].bitcast(F32).rearrange("p (c r u) -> p c r u", c=PASSES, u=2)
-            nc.scalar.copy(out=dst[:, 2 * h : 2 * h + 2], in_=bank[:].rearrange("p c u r -> p c r u"))
+            turned[b] = bank
+
+        def empty_bank(b):
+            h = b % 2
+            dst = grouped[sequence[b // 2]].bitcast(F32).rearrange("p (c r u) -> p c r u", c=PASSES, u=2)
+            nc.scalar.copy(out=dst[:, 2 * h : 2 * h + 2], in_=turned[b][:].rearrange("p c u r -> p c r u"))
 
         def code_tiles(kind, first, count):
             depth = BEATS // 2 + 2 if kind == "us" else 4
@@ -251,9 +266,15 @@ def tile_fourierftgivenbases_w_kernel(tc, w0, coef, g, uc, us_bytes, us_scale, v
                     scale=gain_col[:, i : i + 1],
                 )
 
-        def group_z(c):
-            z_grouped[c] = stage.tile([P, 2 * F, 4], BF16, name="z_grouped", bufs=2, align_bytes=64)
-            nc.scalar.copy(out=z_grouped[c][:], in_=z_flat[c][:].rearrange("p t f -> p f t"))
+        def group_z(c, half):
+            if half == 0:
+                z_grouped[c] = stage.tile([P, 2 * F, 4], BF16, name="z_grouped", bufs=2, align_bytes=64)
+            cols = slice(half * F, (half + 1) * F)
+            src = z_flat[c][:, :, cols].rearrange("p t f -> p f t")
+            if c in VECTOR_GROUPS:
+                nc.vector.tensor_copy(out=z_grouped[c][:, cols, :], in_=src)
+            else:
+                nc.scalar.copy(out=z_grouped[c][:, cols, :], in_=src)
 
         def quantize_z(c):
             nc.vector.quantize_mx(
@@ -282,16 +303,11 @@ def tile_fourierftgivenbases_w_kernel(tc, w0, coef, g, uc, us_bytes, us_scale, v
                     stop and n == len(todo) - 1,
                 )
 
-        def stage2_tile(i):
-            if i % 2 == 0:
-                open_sums((i, i + 1), "sums", 2)
-            if i < 2:
-                stage2(i, ("us", "uc"), range(PASSES - 1), i == 0, False)
-                return
-            if i == 2:
-                stage2(0, ("us", "uc"), [PASSES - 1], False, False)
-                stage2(1, ("us", "uc"), [PASSES - 1], False, True)
-            stage2(i, ("us", "uc"), range(PASSES), True, True)
+        def stage2_pair(pair, kinds, passes, start, stop):
+            if start:
+                open_sums((2 * pair, 2 * pair + 1), "sums", 2)
+            stage2(2 * pair, kinds, passes, start, False)
+            stage2(2 * pair + 1, kinds, passes, False, stop)
 
         def epilogue(tiles):
             i, count = tiles[0], len(tiles)
@@ -314,63 +330,78 @@ def tile_fourierftgivenbases_w_kernel(tc, w0, coef, g, uc, us_bytes, us_scale, v
         def plan(b, fn, *args):
             after[min(max(b, -1), BANKS - 1)].append((fn, args))
 
-        points = list(range(MX_FIRST, BANKS - 2, RUN))
-        bursts = []
-        for n, key in enumerate(wide[:-2]):
-            ready = first_bank[wide[n - n % 2 + 1]] + 1 + MX_LAG
-            if key[0] == "uc":
-                ready = max(ready, first_bank[("us", key[1])] + 1 + MX_LAG)
-            while len(points) > 1 and points[0] < max(ready, MX_FIRST):
-                points.pop(0)
-            bursts.append(points.pop(0) if len(points) > 1 else points[0])
-
-        def burst(n):
-            return bursts[n]
+        half = BEATS // 2
+        beat_end = [first_bank[wide[2 * beat + 1]] + 3 for beat in range(BEATS)]
+        points = []
+        for beat in range(1, BEATS):
+            points += [beat_end[beat] - RUN, beat_end[beat]]
+            if beat == half - 1:
+                points.append(beat_end[beat] + 2)
+        run_ends = set(points) | set(range(SINGLE_HEAD)) | set(range(BANKS - SINGLE_TAIL, BANKS))
+        emptied = {b: min(e for e in run_ends if e >= b) for b in range(BANKS)}
+        all_passes = range(PASSES)
+        early_passes = range(PASSES - 1)
+        a, z = TILES - 2, TILES - 1
 
         for key in sorted(sequence, key=first_use):
             if key not in HEAD:
                 plan(first_use(key) - LOAD_AHEAD, load, key)
+        plan(GAIN_AT - 3, load_gain)
         plan(BANKS // 2 - LOAD_AHEAD, load_w0)
+
+        for b in reversed(range(BANKS)):
+            plan(emptied[b], empty_bank, b)
+        plan(-1, group_v, 0, "vector")
+        plan(-1, group_v, 1, VS_ENGINE)
+        plan(-1, quantize_v)
         for n in range(0, len(wide) - 2, 2):
             kind, i = wide[n]
-            plan(first_bank[wide[n + 1]] + 1, quantize_pair, kind, i // 2)
+            plan(emptied[first_bank[wide[n + 1]] + 1], quantize_pair, kind, i // 2)
         for i in range(TILES - 1):
-            plan(first_bank[("us", i)] + 1, quantize_us, i)
-        for c in range(PASSES):
-            plan(burst(4 * c + 3) + GAIN_LAG + ZQ_LAG, quantize_z, c)
-        for pair in range(TILES // 2 - 2):
-            b = burst(TILES + max(2 * pair + 1, 2)) + EPILOGUE_LAG
-            plan(b, epilogue, (2 * pair, 2 * pair + 1))
-            plan(b + 3, store, (2 * pair, 2 * pair + 1))
-        plan(VC_AT[0], group_v, 0, VC_AT[1])
-        plan(VS_AT[0], group_v, 1, VS_AT[1])
-        plan(V_AT, quantize_v)
-        plan(GAIN_AT, widen_gain)
-        for key in sequence:
-            if key[0] == "us":
-                plan(first_use(key), product, key)
-            elif key in orderer:
-                plan(first_use(key), order_words, key)
+            plan(emptied[first_bank[("us", i)] + 1], quantize_us, i)
+
+        late = {beat_end[beat] - RUN: beat_end[beat] for beat in LONG_RUNS}
         for i in range(TILES):
-            plan(burst(i), stage1, i)
-        for pair in range(TILES // 2):
-            plan(burst(2 * pair + 1) + GAIN_LAG, gains, pair)
+            plan(late.get(points[i + 1], points[i + 1]), stage1, i)
+        for pair in range(half):
+            plan(points[min(2 * pair + 3, TILES)], gains, pair)
         for c in range(PASSES):
-            plan(burst(4 * c + 3) + GAIN_LAG + 1, group_z, c)
-        for i in range(TILES - 3):
-            plan(burst(TILES + i), stage2_tile, i)
-        a, z = TILES - 2, TILES - 1
-        plan(first_bank[("uc", a)] + 1, code_tiles, "uc", a, 2)
-        plan(first_bank[("uc", a)] + 1, quantize_part, ("uc", a), 0, PASSES)
+            first = min(4 * c + 6, TILES)
+            second = first + (2 if c < PASSES - 2 else 1)
+            plan(points[first], group_z, c, 0)
+            plan(points[second], group_z, c, 1)
+            plan(points[second + (1 if c < PASSES - 2 else 0)], quantize_z, c)
+
+        plan(beat_end[half + 1] - RUN, stage2_pair, 0, ("us",), early_passes, True, False)
+        plan(beat_end[half + 1], stage2_pair, 0, ("uc",), early_passes, False, False)
+        plan(beat_end[half + 2] - RUN, stage2_pair, 0, ("us", "uc"), [PASSES - 1], False, True)
+        for pair in range(1, half - 1):
+            b = beat_end[half + 1 + pair] - RUN
+            plan(late.get(b, b), stage2_pair, pair, ("us",), all_passes, True, False)
+            if pair < half - 2:
+                plan(beat_end[half + 1 + pair], stage2_pair, pair, ("uc",), all_passes, False, True)
+        for pair in range(half - 2):
+            b = beat_end[half + 1 + pair] + RUN
+            plan(b, epilogue, (2 * pair, 2 * pair + 1))
+            plan(b + RUN, store, (2 * pair, 2 * pair + 1))
+
+        for h in range(2 * TILES):
+            plan(product_slot(h), product, h // 2, h % 2)
+        plan(GAIN_AT, widen_gain)
+        for key in orderer:
+            plan(first_use(key), order_words, key)
+
+        plan(emptied[first_bank[("uc", a)] + 1], code_tiles, "uc", a, 2)
+        plan(emptied[first_bank[("uc", a)] + 1], quantize_part, ("uc", a), 0, PASSES)
         plan(first_bank[("uc", z)] + 1, quantize_part, ("uc", z), 0, PASSES)
         plan(BANKS - 2, code_tiles, "us", z, 1)
         plan(BANKS - 2, quantize_part, ("us", z), 0, 2)
         plan(BANKS - 1, quantize_part, ("us", z), 2, 2)
-        plan(BANKS - 1, stage2_tile, TILES - 3)
+        plan(BANKS - 1, stage2_pair, half - 2, ("uc",), all_passes, False, True)
         plan(BANKS - 1, open_sums, (a,), "sums", 2)
-        plan(BANKS - 1, stage2, a, ("uc", "us"), range(PASSES), True, True)
+        plan(BANKS - 1, stage2, a, ("us", "uc"), all_passes, True, True)
         plan(BANKS - 1, open_sums, (z,), "turned", TURN_BANKS)
-        plan(BANKS - 1, stage2, z, ("uc", "us"), range(PASSES), True, True)
+        plan(BANKS - 1, stage2, z, ("uc", "us"), all_passes, True, True)
         for tiles in ((TILES - 4, TILES - 3), (a,), (z,)):
             plan(BANKS - 1, epilogue, tiles)
             plan(BANKS - 1, store, tiles)
@@ -379,8 +410,6 @@ def tile_fourierftgivenbases_w_kernel(tc, w0, coef, g, uc, us_bytes, us_scale, v
             for key in HEAD:
                 if key == "s":
                     nc.sync.dma_start(out=scale_col[:], in_=us_scale.rearrange("o (n m) -> (o n) m", m=TILES))
-                elif key == "g":
-                    nc.sync.dma_start(out=gain_raw[:], in_=g.rearrange("(c p t) -> p c t", p=P, t=4))
                 elif key == "vc":
                     load_v("vc", vc)
                 elif key == "vs":

@@ -23,24 +23,25 @@ TILES = 16
 BEATS = 16
 BANKS = 6 * BEATS
 RUN = 3
-SINGLE_HEAD = 4
+SINGLE_HEAD = 96
 SINGLE_TAIL = 6
-VS_ENGINE = "vector"
+VS_ENGINE = "scalar"
 LOAD_AHEAD = 8
 PRODUCT_PACE = (14, 5)
-PRODUCT_START = -1
-VECTOR_GROUPS = [3]
+PRODUCT_START = -2
+VECTOR_GROUPS = [(0, 1), (1, 1), (2, 1), (3, 0), (3, 1)]
 LONG_RUNS = []
 ORDER_AHEAD = {"scalar": 7, "vector": 10}
+QV_AT = 0
 GAIN_AT = 10
-SCALAR_ORDERS = range(11, 16)
-VECTOR_ORDERS = [3, 5]
+SCALAR_ORDERS = range(10, 15)
+VECTOR_ORDERS = [3, 5, 15]
 SCALAR_WHICH = 1
 US_AFTER = [3, 5, 7, 9, 11, 13, 15, 15, 17, 19, 21, 23, 25, 27, 29, 31]
 RAW_BUFS = 10
-MADE_BUFS = 6
+MADE_BUFS = 8
 TURN_BANKS = 6
-HEAD = ["s", "vc", "vs", ("coef", 0), ("coef", 1), ("us", 0), ("coef", 2), ("coef", 3), ("us", 1)]
+HEAD = ["s", "vc", "vs", ("us", 0), ("coef", 0), ("coef", 1), ("coef", 2), ("coef", 3), ("us", 1)]
 
 
 def tile_fourierftgivenbases_w_kernel(tc, w0, coef, g, uc, us_bytes, us_scale, vc, vs, out):
@@ -271,7 +272,7 @@ def tile_fourierftgivenbases_w_kernel(tc, w0, coef, g, uc, us_bytes, us_scale, v
                 z_grouped[c] = stage.tile([P, 2 * F, 4], BF16, name="z_grouped", bufs=2, align_bytes=64)
             cols = slice(half * F, (half + 1) * F)
             src = z_flat[c][:, :, cols].rearrange("p t f -> p f t")
-            if c in VECTOR_GROUPS:
+            if (c, half) in VECTOR_GROUPS:
                 nc.vector.tensor_copy(out=z_grouped[c][:, cols, :], in_=src)
             else:
                 nc.scalar.copy(out=z_grouped[c][:, cols, :], in_=src)
@@ -353,7 +354,6 @@ def tile_fourierftgivenbases_w_kernel(tc, w0, coef, g, uc, us_bytes, us_scale, v
             plan(emptied[b], empty_bank, b)
         plan(-1, group_v, 0, "vector")
         plan(-1, group_v, 1, VS_ENGINE)
-        plan(-1, quantize_v)
         for n in range(0, len(wide) - 2, 2):
             kind, i = wide[n]
             plan(emptied[first_bank[wide[n + 1]] + 1], quantize_pair, kind, i // 2)
@@ -387,6 +387,7 @@ def tile_fourierftgivenbases_w_kernel(tc, w0, coef, g, uc, us_bytes, us_scale, v
 
         for h in range(2 * TILES):
             plan(product_slot(h), product, h // 2, h % 2)
+        plan(QV_AT, quantize_v)
         plan(GAIN_AT, widen_gain)
         for key in orderer:
             plan(first_use(key), order_words, key)

@@ -148,8 +148,8 @@ def tile_fourierftgivenbases_w_kernel(tc, w0, coef, g, uc, us_bytes, us_scale, v
                 )
 
         def group_v(half, engine):
-            dst = v_grouped[:, :, half * F : (half + 1) * F, :]
-            src = raw[("vc", "vs")[half]][:].rearrange("p (c j f) -> p c f j", c=PASSES, j=4)
+            dst = v_grouped[:, :, half * F : (half + 1) * F, :].rearrange("p c (n i) j -> p c n j i", i=4)
+            src = raw[("vc", "vs")[half]][:].rearrange("p (c j n i) -> p c n j i", c=PASSES, j=4, i=4)
             if engine == "scalar":
                 nc.scalar.copy(out=dst, in_=src)
             else:
@@ -177,8 +177,8 @@ def tile_fourierftgivenbases_w_kernel(tc, w0, coef, g, uc, us_bytes, us_scale, v
 
         def order_words(key):
             tile = stage.tile([P, N], BF16, name="made", bufs=MADE_BUFS, align_bytes=64)
-            dst = tile[:].bitcast(F32).rearrange("p (u w) -> p u w", u=2)
-            src = raw[key][:].bitcast(F32).rearrange("p (w u) -> p u w", u=2)
+            dst = tile[:].bitcast(F32).rearrange("p (u n i) -> p n u i", u=2, i=4)
+            src = raw[key][:].bitcast(F32).rearrange("p (n i u) -> p n u i", u=2, i=4)
             if orderer[key] == "scalar":
                 nc.scalar.copy(out=dst, in_=src)
             else:
@@ -205,13 +205,16 @@ def tile_fourierftgivenbases_w_kernel(tc, w0, coef, g, uc, us_bytes, us_scale, v
                         src = words[:, 512 * u + first // 2 : 512 * u + first // 2 + P]
                     else:
                         src = words[:, first + u : first + 256 : 2]
-                    nc.tensor.transpose(bank[:, c, u, :], src, ident[:])
+                    nc.tensor.transpose(bank[:, u, c, :], src, ident[:])
             turned[b] = bank
 
         def empty_bank(b):
             h = b % 2
-            dst = grouped[sequence[b // 2]].bitcast(F32).rearrange("p (c r u) -> p c r u", c=PASSES, u=2)
-            nc.scalar.copy(out=dst[:, 2 * h : 2 * h + 2], in_=turned[b][:].rearrange("p c u r -> p c r u"))
+            dst = grouped[sequence[b // 2]].bitcast(F32)[:, 512 * h : 512 * (h + 1)]
+            nc.scalar.copy(
+                out=dst.rearrange("p (n i u) -> p n u i", u=2, i=4),
+                in_=turned[b][:].rearrange("p u c (n i) -> p (c n) u i", i=4),
+            )
 
         def code_tiles(kind, first, count):
             depth = BEATS // 2 + 2 if kind == "us" else 4
@@ -271,11 +274,12 @@ def tile_fourierftgivenbases_w_kernel(tc, w0, coef, g, uc, us_bytes, us_scale, v
             if half == 0:
                 z_grouped[c] = stage.tile([P, 2 * F, 4], BF16, name="z_grouped", bufs=2, align_bytes=64)
             cols = slice(half * F, (half + 1) * F)
-            src = z_flat[c][:, :, cols].rearrange("p t f -> p f t")
+            src = z_flat[c][:, :, cols].rearrange("p t (n i) -> p n t i", i=4)
+            dst = z_grouped[c][:, cols, :].rearrange("p (n i) t -> p n t i", i=4)
             if (c, half) in VECTOR_GROUPS:
-                nc.vector.tensor_copy(out=z_grouped[c][:, cols, :], in_=src)
+                nc.vector.tensor_copy(out=dst, in_=src)
             else:
-                nc.scalar.copy(out=z_grouped[c][:, cols, :], in_=src)
+                nc.scalar.copy(out=dst, in_=src)
 
         def quantize_z(c):
             nc.vector.quantize_mx(

@@ -35,7 +35,7 @@ ORDER_AHEAD = {"scalar": 7, "vector": 10}
 QV_AT = 0
 GAIN_AT = 10
 SCALAR_ORDERS = range(10, 15)
-VECTOR_ORDERS = [3, 5, 15]
+VECTOR_ORDERS = []
 SCALAR_WHICH = 1
 US_AFTER = [3, 5, 7, 9, 11, 13, 15, 15, 17, 19, 21, 23, 25, 27, 29, 31]
 RAW_BUFS = 10

@@ -28,20 +28,24 @@ SINGLE_TAIL = 6
 VS_ENGINE = "scalar"
 LOAD_AHEAD = 8
 PRODUCT_PACE = (14, 5)
-PRODUCT_START = -2
-VECTOR_GROUPS = [(0, 1), (1, 1), (2, 1), (3, 0), (3, 1)]
+PRODUCT_START = -4
+EARLY_HALVES = 4
+PRODUCT_LEAD = 99
+EPILOGUE_LAG = 2
+LAST_GAP = 0
+VECTOR_GROUPS = [(0, 1), (1, 1), (2, 1), (3, 1)]
 LONG_RUNS = []
 ORDER_AHEAD = {"scalar": 7, "vector": 10}
-QV_AT = 0
+QV_AT = 1
 GAIN_AT = 10
-SCALAR_ORDERS = range(10, 15)
+SCALAR_ORDERS = range(11, 15)
 VECTOR_ORDERS = []
 SCALAR_WHICH = 1
 US_AFTER = [3, 5, 7, 9, 11, 13, 15, 15, 17, 19, 21, 23, 25, 27, 29, 31]
 RAW_BUFS = 10
 MADE_BUFS = 8
 TURN_BANKS = 6
-HEAD = ["s", "vc", "vs", ("us", 0), ("coef", 0), ("coef", 1), ("coef", 2), ("coef", 3), ("us", 1)]
+HEAD = ["s", "vc", ("us", 0), "vs", ("coef", 0), ("us", 1), ("coef", 1), ("coef", 2), ("coef", 3)]
 
 
 def tile_fourierftgivenbases_w_kernel(tc, w0, coef, g, uc, us_bytes, us_scale, vc, vs, out):
@@ -71,7 +75,11 @@ def tile_fourierftgivenbases_w_kernel(tc, w0, coef, g, uc, us_bytes, us_scale, v
         orderer[wide[2 * beat + 1]] = "vector"
 
     def product_slot(h):
-        return (PRODUCT_PACE[0] * h) // PRODUCT_PACE[1] + PRODUCT_START
+        if h < EARLY_HALVES:
+            return h - 1
+        early = (PRODUCT_PACE[0] * h) // PRODUCT_PACE[1] + PRODUCT_START
+        late = first_bank[("us", h // 2)] - PRODUCT_LEAD + 3 * (h % 2)
+        return max(early, late)
 
     def first_use(key):
         if key[0] == "us":
@@ -166,13 +174,13 @@ def tile_fourierftgivenbases_w_kernel(tc, w0, coef, g, uc, us_bytes, us_scale, v
             nc.vector.tensor_copy(out=gain_col[:], in_=gain_raw[:].rearrange("p c t -> p (c t)"))
 
         def product(i, part):
-            if part == 0:
+            if part == 1:
                 made[i] = stage.tile([P, N], BF16, name="made", bufs=MADE_BUFS, align_bytes=64)
             cols = slice(part * N // 2, (part + 1) * N // 2)
             nc.vector.tensor_tensor(
                 out=made[i][:, cols], in0=raw[("us", i)][:, cols].bitcast(FP8), in1=neg_scale[:, cols], op=MULT
             )
-            if part == 1:
+            if part == 0:
                 raw[("us", i)] = made[i]
 
         def order_words(key):
@@ -371,10 +379,10 @@ def tile_fourierftgivenbases_w_kernel(tc, w0, coef, g, uc, us_bytes, us_scale, v
             plan(points[min(2 * pair + 3, TILES)], gains, pair)
         for c in range(PASSES):
             first = min(4 * c + 6, TILES)
-            second = first + (2 if c < PASSES - 2 else 1)
+            second = first + (2 if c < PASSES - 2 else 1 if c < PASSES - 1 else LAST_GAP)
             plan(points[first], group_z, c, 0)
             plan(points[second], group_z, c, 1)
-            plan(points[second + (1 if c < PASSES - 2 else 0)], quantize_z, c)
+            plan(points[second + (1 if c < PASSES - 2 else 0 if c < PASSES - 1 else 1 - LAST_GAP)], quantize_z, c)
 
         plan(beat_end[half + 1] - RUN, stage2_pair, 0, ("us",), early_passes, True, False)
         plan(beat_end[half + 1], stage2_pair, 0, ("uc",), early_passes, False, False)
@@ -385,12 +393,12 @@ def tile_fourierftgivenbases_w_kernel(tc, w0, coef, g, uc, us_bytes, us_scale, v
             if pair < half - 2:
                 plan(beat_end[half + 1 + pair], stage2_pair, pair, ("uc",), all_passes, False, True)
         for pair in range(half - 2):
-            b = beat_end[half + 1 + pair] + RUN
+            b = beat_end[half + 1 + pair] + (EPILOGUE_LAG if pair > 0 else RUN)
             plan(b, epilogue, (2 * pair, 2 * pair + 1))
             plan(b + RUN, store, (2 * pair, 2 * pair + 1))
 
         for h in range(2 * TILES):
-            plan(product_slot(h), product, h // 2, h % 2)
+            plan(product_slot(h), product, h // 2, 1 - h % 2)
         plan(QV_AT, quantize_v)
         plan(GAIN_AT, widen_gain)
         for key in orderer:

@@ -98,7 +98,7 @@ def tile_fourierftgivenbases_w_kernel(tc, w0, coef, g, uc, us_bytes, us_scale, v
 
         gain_raw = keep.tile([P, 4, 4], BF16, name="gain_raw")
         gain_col = keep.tile([P, TILES], F32, name="gain_col")
-        scale_col = keep.tile([P, TILES], F32, name="scale_col")
+        scale_col = keep.tile([P, 2, 8], F32, name="scale_col")
         neg_scale = keep.tile([P, N], F32, name="neg_scale", align_bytes=64)
         v_grouped = keep.tile([P, PASSES, 2 * F, 4], BF16, name="v_grouped", align_bytes=64)
         v_codes = keep.tile([P, PASSES, 2 * F], U32, name="v_codes", align_bytes=64)
@@ -145,15 +145,19 @@ def tile_fourierftgivenbases_w_kernel(tc, w0, coef, g, uc, us_bytes, us_scale, v
             nc.sync.dma_start(out=w0_sb[:], in_=w0_v)
 
         def spread_scale():
-            spread = neg_scale[:].rearrange("p (n m) -> p n m", m=TILES)
-            for b in range(4):
-                bank = psum.tile([P, 4, P], F32, name="turned", bufs=TURN_BANKS)
-                for j in range(4):
-                    m = 4 * b + j
-                    nc.tensor.transpose(bank[:, j, :], scale_col[:, m : m + 1].to_broadcast([P, P]), ident[:])
-                nc.scalar.activation(
-                    out=spread[:, :, 4 * b : 4 * b + 4], in_=bank[:].rearrange("p j n -> p n j"), func=COPY, scale=-1.0
-                )
+            spread = neg_scale[:].rearrange("p (h n m) -> p h n m", h=2, m=8)
+            for h in (1, 0):
+                for first in (0, 4):
+                    bank = psum.tile([P, 4, P], F32, name="turned", bufs=TURN_BANKS)
+                    for j in range(4):
+                        column = scale_col[:, h, first + j : first + j + 1]
+                        nc.tensor.transpose(bank[:, j, :], column.to_broadcast([P, P]), ident[:])
+                    nc.scalar.activation(
+                        out=spread[:, h, :, first : first + 4],
+                        in_=bank[:].rearrange("p j n -> p n j"),
+                        func=COPY,
+                        scale=-1.0,
+                    )
 
         def group_v(half, engine):
             dst = v_grouped[:, :, half * F : (half + 1) * F, :].rearrange("p c (n i) j -> p c n j i", i=4)
@@ -422,7 +426,7 @@ def tile_fourierftgivenbases_w_kernel(tc, w0, coef, g, uc, us_bytes, us_scale, v
         with tc.manual_schedule():
             for key in HEAD:
                 if key == "s":
-                    nc.sync.dma_start(out=scale_col[:], in_=us_scale.rearrange("o (n m) -> (o n) m", m=TILES))
+                    nc.sync.dma_start(out=scale_col[:], in_=us_scale.rearrange("o (h n m) -> (o n) h m", h=2, m=8))
                 elif key == "vc":
                     load_v("vc", vc)
                 elif key == "vs":

@@ -21,31 +21,20 @@ P = 128
 PASSES = 4
 TILES = 16
 BEATS = 16
-BANKS = 6 * BEATS
-RUN = 3
-SINGLE_HEAD = 96
-SINGLE_TAIL = 6
-VS_ENGINE = "scalar"
-LOAD_AHEAD = 8
-PRODUCT_PACE = (14, 5)
-PRODUCT_START = -4
-EARLY_HALVES = 4
-PRODUCT_LEAD = 99
-EPILOGUE_LAG = 2
-LAST_GAP = 0
-VECTOR_GROUPS = [(0, 1), (1, 1), (2, 1), (3, 1)]
-LONG_RUNS = []
-ORDER_AHEAD = {"scalar": 7, "vector": 10}
-QV_AT = 1
-GAIN_AT = 10
-SCALAR_ORDERS = range(11, 15)
-VECTOR_ORDERS = []
-SCALAR_WHICH = 1
-US_AFTER = [3, 5, 7, 9, 11, 13, 15, 15, 17, 19, 21, 23, 25, 27, 29, 31]
-RAW_BUFS = 10
-MADE_BUFS = 8
-TURN_BANKS = 6
-HEAD = ["s", "vc", ("us", 0), "vs", ("coef", 0), ("us", 1), ("coef", 1), ("coef", 2), ("coef", 3)]
+HALF = BEATS // 2
+LOAD_BEATS = 3
+RAW_BUFS = 8
+SLOTS = 4
+US_BANKS = 3
+WIDE_BANKS = 3
+HEAD = [("us", 0), "s", ("us", 1), ("coef", 0), "g", "vc", ("coef", 1), ("us", 2), "vs", ("coef", 2), ("coef", 3), ("us", 3), ("coef", 4), ("coef", 5)]
+V_GROUPS = [(1, "V", 0, 0, 4, "vector"), (2, "V", 1, 0, 4, "vector")]
+QV_BEAT = 2
+STAGE1_FROM = 5
+SCALAR_ORDERS = range(10, 16)
+POOL_ORDERS = []
+POOL_PASSES = 3
+Z_ENGINES = ("scalar", "vector")
 
 
 def tile_fourierftgivenbases_w_kernel(tc, w0, coef, g, uc, us_bytes, us_scale, vc, vs, out):
@@ -58,35 +47,7 @@ def tile_fourierftgivenbases_w_kernel(tc, w0, coef, g, uc, us_bytes, us_scale, v
     }
     w0_v = w0.rearrange("(g m t) f -> m g t f", m=P, t=4)
     out_v = out.rearrange("(g m t) f -> g m t f", m=P, t=4)
-
-    sequence = []
-    us_next = 0
-    for n in range(2 * TILES):
-        sequence.append(("coef", n) if n < TILES else ("uc", n - TILES))
-        for j in range(US_AFTER.count(n)):
-            sequence.append(("us", us_next))
-            us_next += 1
-    first_bank = {key: 2 * n for n, key in enumerate(sequence)}
-    wide = [key for key in sequence if key[0] != "us"]
-    orderer = {}
-    for beat in SCALAR_ORDERS:
-        orderer[wide[2 * beat + SCALAR_WHICH]] = "scalar"
-    for beat in VECTOR_ORDERS:
-        orderer[wide[2 * beat + 1]] = "vector"
-
-    def product_slot(h):
-        if h < EARLY_HALVES:
-            return h - 1
-        early = (PRODUCT_PACE[0] * h) // PRODUCT_PACE[1] + PRODUCT_START
-        late = first_bank[("us", h // 2)] - PRODUCT_LEAD + 3 * (h % 2)
-        return max(early, late)
-
-    def first_use(key):
-        if key[0] == "us":
-            return product_slot(2 * key[1])
-        if key in orderer:
-            return first_bank[key] - ORDER_AHEAD[orderer[key]]
-        return first_bank[key]
+    wide = [("coef", i) for i in range(TILES)] + [("uc", i) for i in range(TILES)]
 
     with ExitStack() as ctx:
         keep = ctx.enter_context(tc.tile_pool(name="keep", bufs=1))
@@ -98,17 +59,20 @@ def tile_fourierftgivenbases_w_kernel(tc, w0, coef, g, uc, us_bytes, us_scale, v
 
         gain_raw = keep.tile([P, 4, 4], BF16, name="gain_raw")
         gain_col = keep.tile([P, TILES], F32, name="gain_col")
-        scale_col = keep.tile([P, 2, 8], F32, name="scale_col")
-        neg_scale = keep.tile([P, N], F32, name="neg_scale", align_bytes=64)
+        scale_raw = keep.tile([P, PASSES, 4], F32, name="scale_raw")
+        neg_scale = keep.tile([P, PASSES, 4], F32, name="neg_scale")
+        v_raw = [keep.tile([P, N], BF16, name="v_raw%d" % j, align_bytes=64) for j in range(2)]
         v_grouped = keep.tile([P, PASSES, 2 * F, 4], BF16, name="v_grouped", align_bytes=64)
         v_codes = keep.tile([P, PASSES, 2 * F], U32, name="v_codes", align_bytes=64)
         v_scales = keep.tile([P, PASSES, 2 * F], U8, name="v_scales", align_bytes=64)
         z_codes = keep.tile([P, PASSES, 2 * F], U32, name="z_codes", align_bytes=64)
         z_scales = keep.tile([P, PASSES, 2 * F], U8, name="z_scales", align_bytes=64)
         w0_sb = keep.tile([P, 4, 4, F], BF16, name="w0_sb", align_bytes=64)
+        slots = [keep.tile([P, N], BF16, name="slot%d" % j, align_bytes=64) for j in range(SLOTS)]
 
         raw = {}
-        made = {}
+        widened = {}
+        ordered = {}
         grouped = {}
         turned = {}
         codes = {}
@@ -130,38 +94,15 @@ def tile_fourierftgivenbases_w_kernel(tc, w0, coef, g, uc, us_bytes, us_scale, v
                 nc.sync.dma_start(out=tile[:, cols], in_=rows[kind][i // 4, i % 4][:, cols])
             raw[key] = tile
 
-        def load_v(name, v):
-            tile = stage.tile([P, N], BF16, name="raw", bufs=RAW_BUFS, align_bytes=64)
+        def load_v(which):
             nc.sync.dma_start(
-                out=tile[:].rearrange("p (c j f) -> p c j f", c=PASSES, j=4),
-                in_=v.rearrange("(c p j) f -> p c j f", p=P, j=4),
+                out=v_raw[which][:].rearrange("p (c j f) -> p c j f", c=PASSES, j=4),
+                in_=(vc, vs)[which].rearrange("(c p j) f -> p c j f", p=P, j=4),
             )
-            raw[name] = tile
 
-        def load_gain():
-            nc.sync.dma_start(out=gain_raw[:], in_=g.rearrange("(c p t) -> p c t", p=P, t=4))
-
-        def load_w0():
-            nc.sync.dma_start(out=w0_sb[:], in_=w0_v)
-
-        def spread_scale():
-            spread = neg_scale[:].rearrange("p (h n m) -> p h n m", h=2, m=8)
-            for h in (1, 0):
-                for first in (0, 4):
-                    bank = psum.tile([P, 4, P], F32, name="turned", bufs=TURN_BANKS)
-                    for j in range(4):
-                        column = scale_col[:, h, first + j : first + j + 1]
-                        nc.tensor.transpose(bank[:, j, :], column.to_broadcast([P, P]), ident[:])
-                    nc.scalar.activation(
-                        out=spread[:, h, :, first : first + 4],
-                        in_=bank[:].rearrange("p j n -> p n j"),
-                        func=COPY,
-                        scale=-1.0,
-                    )
-
-        def group_v(half, engine):
-            dst = v_grouped[:, :, half * F : (half + 1) * F, :].rearrange("p c (n i) j -> p c n j i", i=4)
-            src = raw[("vc", "vs")[half]][:].rearrange("p (c j n i) -> p c n j i", c=PASSES, j=4, i=4)
+        def group_v(which, first, last, engine):
+            dst = v_grouped[:, first:last, which * F : (which + 1) * F, :].rearrange("p c (n i) j -> p c n j i", i=4)
+            src = v_raw[which][:].rearrange("p (c j n i) -> p c n j i", c=PASSES, j=4, i=4)[:, first:last]
             if engine == "scalar":
                 nc.scalar.copy(out=dst, in_=src)
             else:
@@ -174,62 +115,81 @@ def tile_fourierftgivenbases_w_kernel(tc, w0, coef, g, uc, us_bytes, us_scale, v
                 in_=v_grouped[:].rearrange("p c f j -> p (c f j)"),
             )
 
-        def widen_gain():
-            nc.vector.tensor_copy(out=gain_col[:], in_=gain_raw[:].rearrange("p c t -> p (c t)"))
-
-        def product(i, part):
-            if part == 1:
-                made[i] = stage.tile([P, N], BF16, name="made", bufs=MADE_BUFS, align_bytes=64)
-            cols = slice(part * N // 2, (part + 1) * N // 2)
-            nc.vector.tensor_tensor(
-                out=made[i][:, cols], in0=raw[("us", i)][:, cols].bitcast(FP8), in1=neg_scale[:, cols], op=MULT
-            )
-            if part == 0:
-                raw[("us", i)] = made[i]
-
-        def order_words(key):
-            tile = stage.tile([P, N], BF16, name="made", bufs=MADE_BUFS, align_bytes=64)
-            dst = tile[:].bitcast(F32).rearrange("p (u n i) -> p n u i", u=2, i=4)
-            src = raw[key][:].bitcast(F32).rearrange("p (n i u) -> p n u i", u=2, i=4)
-            if orderer[key] == "scalar":
-                nc.scalar.copy(out=dst, in_=src)
+        def widen(i, h, engine):
+            if h == 0:
+                widened[i] = stage.tile([P, N], BF16, name="widened", bufs=3, align_bytes=64)
+            cols = slice(h * N // 2, (h + 1) * N // 2)
+            if engine == "scalar":
+                nc.scalar.copy(out=widened[i][:, cols], in_=raw[("us", i)][:, cols].bitcast(FP8))
             else:
-                nc.vector.tensor_copy(out=dst, in_=src)
-            raw[key] = tile
+                nc.vector.tensor_copy(out=widened[i][:, cols], in_=raw[("us", i)][:, cols].bitcast(FP8))
 
-        def turn_bank(b):
-            key = sequence[b // 2]
+        def scalar_order(key):
+            tile = stage.tile([P, N], BF16, name="ordered", bufs=2, align_bytes=64)
+            nc.scalar.copy(
+                out=tile[:].bitcast(F32).rearrange("p (u n i) -> p n u i", u=2, i=4),
+                in_=raw[key][:].bitcast(F32).rearrange("p (n i u) -> p n u i", u=2, i=4),
+            )
+            ordered[key] = (tile, PASSES)
+
+        def pool_order(key, tile):
+            width = POOL_PASSES * 512
+            nc.gpsimd.tensor_scalar(
+                out=tile[:, 0:width].rearrange("p (u n e) -> p u n e", u=2, e=2),
+                in0=raw[key][:, 0:width].rearrange("p (n u e) -> p u n e", u=2, e=2),
+                scalar1=1.0,
+                scalar2=0.0,
+                op0=MULT,
+                op1=ADD,
+            )
+            ordered[key] = (tile, POOL_PASSES)
+
+        def turn(key, h):
             kind, i = key
-            h = b % 2
-            if h == 0 and kind == "us":
-                grouped[key] = stage.tile([P, 4 * PASSES * P], BF16, name="us_grouped", bufs=3, align_bytes=64)[:]
-            elif h == 0 and i % 2 == 0:
-                both = stage.tile([P, 2, 4 * PASSES * P], BF16, name="grouped", bufs=3, align_bytes=64)
+            if kind == "us":
+                bank = psum.tile([P, 2, 2, P], F32, name="us_bank", bufs=US_BANKS)
+                words = widened[i][:].bitcast(F32)
+            else:
+                bank = psum.tile([P, 2, 2, P], F32, name="wide_bank", bufs=WIDE_BANKS)
+                words = raw[key][:].bitcast(F32)
+            tile, count = ordered.get(key, (None, 0))
+            for j in range(2):
+                c = 2 * h + j
+                for u in range(2):
+                    if c < count:
+                        first = P * (count * u + c)
+                        src = tile[:].bitcast(F32)[:, first : first + P]
+                    else:
+                        src = words[:, 256 * c + u : 256 * (c + 1) : 2]
+                    nc.tensor.transpose(bank[:, u, j, :], src, ident[:])
+            turned[(key, h)] = bank
+
+        def empty(key, h):
+            kind, i = key
+            if h == 0 and i % 2 == 0:
+                both = stage.tile([P, 2, N], BF16, name="grouped", bufs=3, align_bytes=64)
                 grouped[(kind, i)] = both[:, 0, :]
                 grouped[(kind, i + 1)] = both[:, 1, :]
                 grouped[(kind, "pair", i // 2)] = both[:].rearrange("p j n -> p (j n)")
-            words = raw[key][:].bitcast(F32)
-            bank = psum.tile([P, 2, 2, P], F32, name="turned", bufs=TURN_BANKS)
-            for c in range(2):
-                for u in range(2):
-                    first = 256 * (2 * h + c)
-                    if key in orderer:
-                        src = words[:, 512 * u + first // 2 : 512 * u + first // 2 + P]
-                    else:
-                        src = words[:, first + u : first + 256 : 2]
-                    nc.tensor.transpose(bank[:, u, c, :], src, ident[:])
-            turned[b] = bank
-
-        def empty_bank(b):
-            h = b % 2
-            dst = grouped[sequence[b // 2]].bitcast(F32)[:, 512 * h : 512 * (h + 1)]
+            dst = grouped[key].bitcast(F32)[:, 512 * h : 512 * (h + 1)]
             nc.scalar.copy(
                 out=dst.rearrange("p (n i u) -> p n u i", u=2, i=4),
-                in_=turned[b][:].rearrange("p u c (n i) -> p (c n) u i", i=4),
+                in_=turned[(key, h)][:].rearrange("p u c (n i) -> p (c n) u i", i=4),
+            )
+
+        def product(i, h):
+            grouped[("us", i)] = slots[i % SLOTS][:]
+            values = turned[(("us", i), h)][:].rearrange("p u c m -> p (u c m)").bitcast(BF16)
+            factors = neg_scale[:, 2 * h : 2 * h + 2, :].rearrange("p c (o u e) -> p c o u e", o=1, u=2)
+            nc.vector.tensor_tensor(
+                out=grouped[("us", i)][:, 1024 * h : 1024 * (h + 1)].rearrange("p (c m u e) -> p c m u e", c=2, u=2, e=2),
+                in0=values.rearrange("p (u c m e) -> p c m u e", u=2, c=2, e=2),
+                in1=factors.to_broadcast([P, 2, P, 2, 2]),
+                op=MULT,
             )
 
         def code_tiles(kind, first, count):
-            depth = BEATS // 2 + 2 if kind == "us" else 4
+            depth = HALF + 3 if kind == "us" else 4
             ct = stage.tile([P, count * PASSES * P], U32, name=kind + "_codes", bufs=depth, align_bytes=64)
             st = stage.tile([P, count * PASSES * P], U8, name=kind + "_scales", bufs=depth, align_bytes=64)
             for j in range(count):
@@ -237,9 +197,10 @@ def tile_fourierftgivenbases_w_kernel(tc, w0, coef, g, uc, us_bytes, us_scale, v
                 scales[(kind, first + j)] = st[:, j * PASSES * P : (j + 1) * PASSES * P]
             return ct, st
 
-        def quantize_pair(kind, pair):
-            ct, st = code_tiles(kind, 2 * pair, 2)
-            nc.vector.quantize_mx(out=ct[:].bitcast(FP8X4), scales=st[:], in_=grouped[(kind, "pair", pair)])
+        def quantize_pair(beat):
+            kind, i = wide[2 * beat]
+            ct, st = code_tiles(kind, i, 2)
+            nc.vector.quantize_mx(out=ct[:].bitcast(FP8X4), scales=st[:], in_=grouped[(kind, "pair", i // 2)])
 
         def quantize_part(key, first, count):
             nc.vector.quantize_mx(
@@ -264,31 +225,24 @@ def tile_fourierftgivenbases_w_kernel(tc, w0, coef, g, uc, us_bytes, us_scale, v
             )
 
         def stage1(i):
-            if i % 2 == 0:
-                sums[("r", i // 2)] = psum.tile([P, 2, 2 * F], F32, name="sums", bufs=2)
-            o = sums[("r", i // 2)][:, i % 2, :]
+            sums[("r", i)] = psum.tile([P, 2 * F], F32, name="sums", bufs=2)
             for c in range(PASSES):
-                mm(o, ("coef", i), c, v_codes[:, c, :], v_scales[:, c, :], c == 0, c == PASSES - 1)
+                mm(sums[("r", i)][:], ("coef", i), c, v_codes[:, c, :], v_scales[:, c, :], c == 0, c == PASSES - 1)
 
-        def gains(pair):
-            if pair % 2 == 0:
-                z_flat[pair // 2] = stage.tile([P, 4, 2 * F], BF16, name="z_flat", bufs=2, align_bytes=64)
-            for j in range(2):
-                i = 2 * pair + j
-                nc.scalar.activation(
-                    out=z_flat[i // 4][:, i % 4, :],
-                    in_=sums[("r", pair)][:, j, :],
-                    func=COPY,
-                    scale=gain_col[:, i : i + 1],
-                )
+        def gain(i):
+            if i % 4 == 0:
+                z_flat[i // 4] = stage.tile([P, 4, 2 * F], BF16, name="z_flat", bufs=2, align_bytes=64)
+            nc.scalar.activation(
+                out=z_flat[i // 4][:, i % 4, :], in_=sums[("r", i)][:], func=COPY, scale=gain_col[:, i : i + 1]
+            )
 
         def group_z(c, half):
-            if half == 0:
+            if c not in z_grouped:
                 z_grouped[c] = stage.tile([P, 2 * F, 4], BF16, name="z_grouped", bufs=2, align_bytes=64)
             cols = slice(half * F, (half + 1) * F)
             src = z_flat[c][:, :, cols].rearrange("p t (n i) -> p n t i", i=4)
             dst = z_grouped[c][:, cols, :].rearrange("p (n i) t -> p n t i", i=4)
-            if (c, half) in VECTOR_GROUPS:
+            if Z_ENGINES[half] == "vector":
                 nc.vector.tensor_copy(out=dst, in_=src)
             else:
                 nc.scalar.copy(out=dst, in_=src)
@@ -306,9 +260,8 @@ def tile_fourierftgivenbases_w_kernel(tc, w0, coef, g, uc, us_bytes, us_scale, v
             for j, i in enumerate(tiles):
                 sums[("out", i)] = bank[:, j, :]
 
-        def stage2(i, kinds, passes, start, stop):
-            todo = [(kind, c) for kind in kinds for c in passes]
-            for n, (kind, c) in enumerate(todo):
+        def stage2(i, parts, start, stop):
+            for n, (kind, c) in enumerate(parts):
                 half = slice(F, 2 * F) if kind == "us" else slice(0, F)
                 mm(
                     sums[("out", i)],
@@ -317,14 +270,14 @@ def tile_fourierftgivenbases_w_kernel(tc, w0, coef, g, uc, us_bytes, us_scale, v
                     z_codes[:, c, half],
                     z_scales[:, c, half],
                     start and n == 0,
-                    stop and n == len(todo) - 1,
+                    stop and n == len(parts) - 1,
                 )
 
-        def stage2_pair(pair, kinds, passes, start, stop):
+        def stage2_pair(pair, parts, start, stop):
             if start:
                 open_sums((2 * pair, 2 * pair + 1), "sums", 2)
-            stage2(2 * pair, kinds, passes, start, False)
-            stage2(2 * pair + 1, kinds, passes, False, stop)
+            stage2(2 * pair, parts, start, False)
+            stage2(2 * pair + 1, parts, False, stop)
 
         def epilogue(tiles):
             i, count = tiles[0], len(tiles)
@@ -342,100 +295,133 @@ def tile_fourierftgivenbases_w_kernel(tc, w0, coef, g, uc, us_bytes, us_scale, v
             i, count = tiles[0], len(tiles)
             nc.sync.dma_start(out=out_v[i // 4, :, i % 4 : i % 4 + count, :], in_=results[tiles][:])
 
-        after = {b: [] for b in range(-1, BANKS)}
+        def parts(kinds, passes):
+            return [(kind, c) for kind in kinds for c in passes]
 
-        def plan(b, fn, *args):
-            after[min(max(b, -1), BANKS - 1)].append((fn, args))
+        every = range(PASSES)
+        early = range(PASSES - 1)
+        last = [PASSES - 1]
+        stage1_at = {i: max(i + 3, STAGE1_FROM + i // 2) for i in range(TILES)}
 
-        half = BEATS // 2
-        beat_end = [first_bank[wide[2 * beat + 1]] + 3 for beat in range(BEATS)]
-        points = []
-        for beat in range(1, BEATS):
-            points += [beat_end[beat] - RUN, beat_end[beat]]
-            if beat == half - 1:
-                points.append(beat_end[beat] + 2)
-        run_ends = set(points) | set(range(SINGLE_HEAD)) | set(range(BANKS - SINGLE_TAIL, BANKS))
-        emptied = {b: min(e for e in run_ends if e >= b) for b in range(BANKS)}
-        all_passes = range(PASSES)
-        early_passes = range(PASSES - 1)
-        a, z = TILES - 2, TILES - 1
+        def burst(j):
+            for i in range(TILES):
+                if stage1_at[i] == j:
+                    stage1(i)
+                    if stage1_at.get(i + 1) == j:
+                        gain(i)
+            beat, second = divmod(j, 2)
+            pair = beat - HALF - 1
+            if (pair, second) == (0, 1):
+                stage2_pair(0, parts(("us", "uc"), early), True, False)
+            elif (pair, second) == (1, 0):
+                stage2_pair(1, parts(("us",), early), True, False)
+            elif (pair, second) == (1, 1):
+                stage2_pair(0, parts(("us", "uc"), last), False, True)
+                stage2_pair(1, parts(("us",), last) + parts(("uc",), every), False, True)
+            elif pair > 1:
+                stage2_pair(pair, parts((("us", "uc")[second],), every), second == 0, second == 1)
 
-        for key in sorted(sequence, key=first_use):
-            if key not in HEAD:
-                plan(first_use(key) - LOAD_AHEAD, load, key)
-        plan(GAIN_AT - 3, load_gain)
-        plan(BANKS // 2 - LOAD_AHEAD, load_w0)
+        def gains_after(j):
+            done = [i for i in range(TILES) if stage1_at[i] == j]
+            if done:
+                gain(done[-1])
+            return done
 
-        for b in reversed(range(BANKS)):
-            plan(emptied[b], empty_bank, b)
-        plan(-1, group_v, 0, "vector")
-        plan(-1, group_v, 1, VS_ENGINE)
-        for n in range(0, len(wide) - 2, 2):
-            kind, i = wide[n]
-            plan(emptied[first_bank[wide[n + 1]] + 1], quantize_pair, kind, i // 2)
-        for i in range(TILES - 1):
-            plan(emptied[first_bank[("us", i)] + 1], quantize_us, i)
-
-        late = {beat_end[beat] - RUN: beat_end[beat] for beat in LONG_RUNS}
-        for i in range(TILES):
-            plan(late.get(points[i + 1], points[i + 1]), stage1, i)
-        for pair in range(half):
-            plan(points[min(2 * pair + 3, TILES)], gains, pair)
-        for c in range(PASSES):
-            first = min(4 * c + 6, TILES)
-            second = first + (2 if c < PASSES - 2 else 1 if c < PASSES - 1 else LAST_GAP)
-            plan(points[first], group_z, c, 0)
-            plan(points[second], group_z, c, 1)
-            plan(points[second + (1 if c < PASSES - 2 else 0 if c < PASSES - 1 else 1 - LAST_GAP)], quantize_z, c)
-
-        plan(beat_end[half + 1] - RUN, stage2_pair, 0, ("us",), early_passes, True, False)
-        plan(beat_end[half + 1], stage2_pair, 0, ("uc",), early_passes, False, False)
-        plan(beat_end[half + 2] - RUN, stage2_pair, 0, ("us", "uc"), [PASSES - 1], False, True)
-        for pair in range(1, half - 1):
-            b = beat_end[half + 1 + pair] - RUN
-            plan(late.get(b, b), stage2_pair, pair, ("us",), all_passes, True, False)
-            if pair < half - 2:
-                plan(beat_end[half + 1 + pair], stage2_pair, pair, ("uc",), all_passes, False, True)
-        for pair in range(half - 2):
-            b = beat_end[half + 1 + pair] + (EPILOGUE_LAG if pair > 0 else RUN)
-            plan(b, epilogue, (2 * pair, 2 * pair + 1))
-            plan(b + RUN, store, (2 * pair, 2 * pair + 1))
-
-        for h in range(2 * TILES):
-            plan(product_slot(h), product, h // 2, 1 - h % 2)
-        plan(QV_AT, quantize_v)
-        plan(GAIN_AT, widen_gain)
-        for key in orderer:
-            plan(first_use(key), order_words, key)
-
-        plan(emptied[first_bank[("uc", a)] + 1], code_tiles, "uc", a, 2)
-        plan(emptied[first_bank[("uc", a)] + 1], quantize_part, ("uc", a), 0, PASSES)
-        plan(first_bank[("uc", z)] + 1, quantize_part, ("uc", z), 0, PASSES)
-        plan(BANKS - 2, code_tiles, "us", z, 1)
-        plan(BANKS - 2, quantize_part, ("us", z), 0, 2)
-        plan(BANKS - 1, quantize_part, ("us", z), 2, 2)
-        plan(BANKS - 1, stage2_pair, half - 2, ("uc",), all_passes, False, True)
-        plan(BANKS - 1, open_sums, (a,), "sums", 2)
-        plan(BANKS - 1, stage2, a, ("us", "uc"), all_passes, True, True)
-        plan(BANKS - 1, open_sums, (z,), "turned", TURN_BANKS)
-        plan(BANKS - 1, stage2, z, ("uc", "us"), all_passes, True, True)
-        for tiles in ((TILES - 4, TILES - 3), (a,), (z,)):
-            plan(BANKS - 1, epilogue, tiles)
-            plan(BANKS - 1, store, tiles)
+        def head_groups(beat, where):
+            for at, place, which, first, end, engine in V_GROUPS:
+                if (at, place) == (beat, where):
+                    group_v(which, first, end, engine)
 
         with tc.manual_schedule():
             for key in HEAD:
                 if key == "s":
-                    nc.sync.dma_start(out=scale_col[:], in_=us_scale.rearrange("o (h n m) -> (o n) h m", h=2, m=8))
-                elif key == "vc":
-                    load_v("vc", vc)
-                elif key == "vs":
-                    load_v("vs", vs)
+                    nc.sync.dma_start(out=scale_raw[:], in_=us_scale.rearrange("o (c p t) -> p (o c) t", p=P, t=4))
+                elif key == "g":
+                    nc.sync.dma_start(out=gain_raw[:], in_=g.rearrange("(c p t) -> p c t", p=P, t=4))
+                elif key in ("vc", "vs"):
+                    load_v(("vc", "vs").index(key))
                 else:
-                    load(key, 2 if key == ("coef", 0) else 1)
-            spread_scale()
-            for b in range(-1, BANKS):
-                if b >= 0:
-                    turn_bank(b)
-                for fn, args in after[b]:
-                    fn(*args)
+                    load(key, 2 if key[1] == 0 else 1)
+            widen(0, 0, "vector")
+            widen(0, 1, "scalar")
+            nc.vector.tensor_scalar(out=neg_scale[:], in0=scale_raw[:], scalar1=-1.0, scalar2=None, op0=MULT)
+
+            z_ready = []
+            for n in range(BEATS):
+                a, b = wide[2 * n], wide[2 * n + 1]
+                ahead = n + LOAD_BEATS
+                if ahead < BEATS:
+                    for key in (("us", ahead), wide[2 * ahead], wide[2 * ahead + 1]):
+                        if key not in HEAD:
+                            load(key)
+                if n == HALF - 2:
+                    nc.sync.dma_start(out=w0_sb[:], in_=w0_v)
+                if n >= HALF + 4:
+                    for pair in (0, 1) if n == HALF + 4 else (n - HALF - 3,):
+                        store((2 * pair, 2 * pair + 1))
+
+                turn(("us", n), 0)
+                if n > 0:
+                    gains_after(2 * n - 1)
+                    head_groups(n, "V")
+                    for c in z_ready:
+                        for half in range(2):
+                            if Z_ENGINES[half] == "vector":
+                                group_z(c, half)
+                    quantize_pair(n - 1)
+                    if n == QV_BEAT:
+                        quantize_v()
+                    for c in z_ready:
+                        quantize_z(c)
+                    z_ready = []
+                    quantize_us(n - 1)
+                    if n + 1 in POOL_ORDERS:
+                        pool_order(wide[2 * (n + 1)], slots[(n - 1) % SLOTS])
+                    if n >= HALF + 3:
+                        for pair in (0, 1) if n == HALF + 3 else (n - HALF - 2,):
+                            epilogue((2 * pair, 2 * pair + 1))
+                product(n, 0)
+                turn(("us", n), 1)
+                product(n, 1)
+                if n + 1 < BEATS:
+                    widen(n + 1, 0, "scalar")
+                    widen(n + 1, 1, "scalar")
+                if n == 1:
+                    nc.scalar.copy(out=gain_col[:], in_=gain_raw[:].rearrange("p c t -> p (c t)"))
+                turn(a, 0)
+                empty(a, 0)
+                burst(2 * n)
+                head_groups(n, "A")
+                done = gains_after(2 * n)
+                if n + 1 in SCALAR_ORDERS:
+                    scalar_order(wide[2 * (n + 1) + 1])
+                turn(a, 1)
+                empty(a, 1)
+                for i in done:
+                    if i % 4 == 3:
+                        z_ready.append(i // 4)
+                        for half in range(2):
+                            if Z_ENGINES[half] == "scalar":
+                                group_z(i // 4, half)
+                turn(b, 0)
+                empty(b, 0)
+                turn(b, 1)
+                empty(b, 1)
+                head_groups(n, "B")
+                burst(2 * n + 1)
+
+            y, z = TILES - 2, TILES - 1
+            before = (TILES - 4, TILES - 3)
+            store((TILES - 6, TILES - 5))
+            code_tiles("uc", y, 2)
+            quantize_part(("uc", y), 0, PASSES)
+            quantize_us(z)
+            quantize_part(("uc", z), 0, 2)
+            quantize_part(("uc", z), 2, 2)
+            open_sums((y,), "sums", 2)
+            stage2(y, parts(("us", "uc"), every), True, True)
+            open_sums((z,), "us_bank", US_BANKS)
+            stage2(z, parts(("us", "uc"), every), True, True)
+            for tiles in (before, (y,), (z,)):
+                epilogue(tiles)
+                store(tiles)

@@ -22,19 +22,24 @@ PASSES = 4
 TILES = 16
 BEATS = 16
 HALF = BEATS // 2
-LOAD_BEATS = 3
+LOAD_BEATS = 2
 RAW_BUFS = 8
 SLOTS = 4
-US_BANKS = 3
-WIDE_BANKS = 3
-HEAD = [("us", 0), "s", ("us", 1), ("coef", 0), "g", "vc", ("coef", 1), ("us", 2), "vs", ("coef", 2), ("coef", 3), ("us", 3), ("coef", 4), ("coef", 5)]
-V_GROUPS = [(1, "V", 0, 0, 4, "vector"), (2, "V", 1, 0, 4, "vector")]
-QV_BEAT = 2
-STAGE1_FROM = 5
-SCALAR_ORDERS = range(10, 16)
+US_BANKS = 2
+WIDE_BANKS = 4
+HEAD = [("coef",0,0),("us",0,0),("coef",0,1),("us",0,1),"s",("coef",1),("us",1),"vc",("coef",2),("us",2),"vs",("coef",3),("coef",4),"g",("coef",5),("us",3),("coef",6),("coef",7),("us",4)]
+GAIN_BEAT = -1
+HEAD_STEPS = "t.c.0.0 w.0.0.v w.0.1.v neg t.c.0.1 t.u.0.0 p.0.0 t.u.0.1 p.0.1 w.1.0.s w.1.1.s t.c.1.0 t.c.1.1 g.0.0.4.v t.u.1.0 t.u.1.1 p.1.0 p.1.1 w.2.0.s t.c.2.0 w.2.1.s g.1.0.2.s t.c.2.1 t.u.2.0 t.u.2.1 g.1.2.4.v qp.0 qv p.2.0 p.2.1 qu.0 qu.1 t.c.3.0 t.c.3.1 qp.1 qu.2 t.c.4.0 t.c.4.1 gc l w.3.0.s w.3.1.s m.0 a.0 t.c.5.0 t.c.5.1 m.1 a.1"
+US_AHEAD = 0
+START_BEAT = 3
+STAGE1_DONE = 2
+V_GROUPS = []
+QV_BEAT = -1
+STAGE1_FROM = 4
+SCALAR_ORDERS = [11,13]
 POOL_ORDERS = []
 POOL_PASSES = 3
-Z_ENGINES = ("scalar", "vector")
+Z_ENGINES = ("vector","vector")
 
 
 def tile_fourierftgivenbases_w_kernel(tc, w0, coef, g, uc, us_bytes, us_scale, vc, vs, out):
@@ -82,17 +87,23 @@ def tile_fourierftgivenbases_w_kernel(tc, w0, coef, g, uc, us_bytes, us_scale, v
         z_grouped = {}
         results = {}
 
-        def load(key, pieces=1):
-            kind, i = key
-            if kind == "us":
-                tile = stage.tile([P, N], U8, name="us_raw", bufs=4, align_bytes=64)
+        def raw_tile(key):
+            if key[0] == "us":
+                raw[key] = stage.tile([P, N], U8, name="us_raw", bufs=6, align_bytes=64)
             else:
-                tile = stage.tile([P, N], BF16, name="raw", bufs=RAW_BUFS, align_bytes=64)
-            width = N // pieces
-            for j in range(pieces):
-                cols = slice(j * width, (j + 1) * width)
-                nc.sync.dma_start(out=tile[:, cols], in_=rows[kind][i // 4, i % 4][:, cols])
-            raw[key] = tile
+                raw[key] = stage.tile([P, N], BF16, name="raw", bufs=RAW_BUFS, align_bytes=64)
+
+        def load(key):
+            kind, i = key
+            raw_tile(key)
+            nc.sync.dma_start(out=raw[key][:], in_=rows[kind][i // 4, i % 4])
+
+        def load_half(key, h):
+            kind, i = key
+            if h == 0:
+                raw_tile(key)
+            cols = slice(h * N // 2, (h + 1) * N // 2)
+            nc.sync.dma_start(out=raw[key][:, cols], in_=rows[kind][i // 4, i % 4][:, cols])
 
         def load_v(which):
             nc.sync.dma_start(
@@ -189,7 +200,7 @@ def tile_fourierftgivenbases_w_kernel(tc, w0, coef, g, uc, us_bytes, us_scale, v
             )
 
         def code_tiles(kind, first, count):
-            depth = HALF + 3 if kind == "us" else 4
+            depth = HALF + 5 if kind == "us" else 4
             ct = stage.tile([P, count * PASSES * P], U32, name=kind + "_codes", bufs=depth, align_bytes=64)
             st = stage.tile([P, count * PASSES * P], U8, name=kind + "_scales", bufs=depth, align_bytes=64)
             for j in range(count):
@@ -301,36 +312,43 @@ def tile_fourierftgivenbases_w_kernel(tc, w0, coef, g, uc, us_bytes, us_scale, v
         every = range(PASSES)
         early = range(PASSES - 1)
         last = [PASSES - 1]
-        stage1_at = {i: max(i + 3, STAGE1_FROM + i // 2) for i in range(TILES)}
+        stage1_at = {i: max(i + 4, STAGE1_FROM + i // 2) for i in range(STAGE1_DONE, TILES)}
+        y, z = TILES - 2, TILES - 1
 
         def burst(j):
-            for i in range(TILES):
+            for i in stage1_at:
                 if stage1_at[i] == j:
                     stage1(i)
                     if stage1_at.get(i + 1) == j:
                         gain(i)
             beat, second = divmod(j, 2)
-            pair = beat - HALF - 1
-            if (pair, second) == (0, 1):
-                stage2_pair(0, parts(("us", "uc"), early), True, False)
-            elif (pair, second) == (1, 0):
-                stage2_pair(1, parts(("us",), early), True, False)
-            elif (pair, second) == (1, 1):
-                stage2_pair(0, parts(("us", "uc"), last), False, True)
-                stage2_pair(1, parts(("us",), last) + parts(("uc",), every), False, True)
-            elif pair > 1:
+            pair = beat - HALF - 2
+            if pair == 0:
+                stage2_pair(0, parts((("us", "uc")[second],), early), second == 0, False)
+            elif pair > 0:
+                if (pair, second) == (1, 0):
+                    stage2_pair(0, parts(("us", "uc"), last), False, True)
                 stage2_pair(pair, parts((("us", "uc")[second],), every), second == 0, second == 1)
 
         def gains_after(j):
-            done = [i for i in range(TILES) if stage1_at[i] == j]
+            done = [i for i in stage1_at if stage1_at[i] == j]
             if done:
                 gain(done[-1])
-            return done
+            return [i // 4 for i in done if i % 4 == 3]
 
         def head_groups(beat, where):
             for at, place, which, first, end, engine in V_GROUPS:
                 if (at, place) == (beat, where):
                     group_v(which, first, end, engine)
+
+        def z_halves(ready, engine):
+            for c in ready:
+                for half in range(2):
+                    if Z_ENGINES[half] == engine:
+                        group_z(c, half)
+
+        def pair_tiles(pair):
+            return (2 * pair, 2 * pair + 1)
 
         with tc.manual_schedule():
             for key in HEAD:
@@ -340,69 +358,95 @@ def tile_fourierftgivenbases_w_kernel(tc, w0, coef, g, uc, us_bytes, us_scale, v
                     nc.sync.dma_start(out=gain_raw[:], in_=g.rearrange("(c p t) -> p c t", p=P, t=4))
                 elif key in ("vc", "vs"):
                     load_v(("vc", "vs").index(key))
+                elif len(key) == 3:
+                    load_half(key[:2], key[2])
                 else:
-                    load(key, 2 if key[1] == 0 else 1)
-            widen(0, 0, "vector")
-            widen(0, 1, "scalar")
-            nc.vector.tensor_scalar(out=neg_scale[:], in0=scale_raw[:], scalar1=-1.0, scalar2=None, op0=MULT)
+                    load(key)
 
-            z_ready = []
-            for n in range(BEATS):
+            names = {"u": "us", "c": "coef"}
+            engines = {"s": "scalar", "v": "vector"}
+            for word in HEAD_STEPS.split():
+                step = word.split(".")
+                if step[0] == "t":
+                    key, h = (names[step[1]], int(step[2])), int(step[3])
+                    turn(key, h)
+                    if key[0] == "coef":
+                        empty(key, h)
+                elif step[0] == "p":
+                    product(int(step[1]), int(step[2]))
+                elif step[0] == "w":
+                    widen(int(step[1]), int(step[2]), engines[step[3]])
+                elif step[0] == "g":
+                    group_v(int(step[1]), int(step[2]), int(step[3]), engines[step[4]])
+                elif step[0] == "qv":
+                    quantize_v()
+                elif step[0] == "qu":
+                    quantize_us(int(step[1]))
+                elif step[0] == "qp":
+                    quantize_pair(int(step[1]))
+                elif step[0] == "m":
+                    stage1(int(step[1]))
+                elif step[0] == "a":
+                    gain(int(step[1]))
+                elif step[0] == "l":
+                    load(("coef", 8))
+                    load(("coef", 9))
+                elif step[0] == "gc":
+                    nc.scalar.copy(out=gain_col[:], in_=gain_raw[:].rearrange("p c t -> p (c t)"))
+                elif step[0] == "neg":
+                    nc.vector.tensor_scalar(out=neg_scale[:], in0=scale_raw[:], scalar1=-1.0, scalar2=None, op0=MULT)
+
+            for n in range(START_BEAT, BEATS):
                 a, b = wide[2 * n], wide[2 * n + 1]
+                u = n + US_AHEAD
                 ahead = n + LOAD_BEATS
                 if ahead < BEATS:
-                    for key in (("us", ahead), wide[2 * ahead], wide[2 * ahead + 1]):
-                        if key not in HEAD:
+                    for key in (("us", ahead + US_AHEAD), wide[2 * ahead], wide[2 * ahead + 1]):
+                        if key not in HEAD and key[1] < TILES:
                             load(key)
-                if n == HALF - 2:
+                if n == HALF - 1:
                     nc.sync.dma_start(out=w0_sb[:], in_=w0_v)
+                if n >= HALF + 5:
+                    for pair in (0, 1) if n == HALF + 5 else (n - HALF - 4,):
+                        store(pair_tiles(pair))
+
+                if u < TILES:
+                    turn(("us", u), 0)
+                z_ready = gains_after(2 * n - 1)
+                z_halves(z_ready, "scalar")
                 if n >= HALF + 4:
                     for pair in (0, 1) if n == HALF + 4 else (n - HALF - 3,):
-                        store((2 * pair, 2 * pair + 1))
-
-                turn(("us", n), 0)
-                if n > 0:
-                    gains_after(2 * n - 1)
-                    head_groups(n, "V")
-                    for c in z_ready:
-                        for half in range(2):
-                            if Z_ENGINES[half] == "vector":
-                                group_z(c, half)
-                    quantize_pair(n - 1)
-                    if n == QV_BEAT:
-                        quantize_v()
-                    for c in z_ready:
-                        quantize_z(c)
-                    z_ready = []
-                    quantize_us(n - 1)
-                    if n + 1 in POOL_ORDERS:
-                        pool_order(wide[2 * (n + 1)], slots[(n - 1) % SLOTS])
-                    if n >= HALF + 3:
-                        for pair in (0, 1) if n == HALF + 3 else (n - HALF - 2,):
-                            epilogue((2 * pair, 2 * pair + 1))
-                product(n, 0)
-                turn(("us", n), 1)
-                product(n, 1)
-                if n + 1 < BEATS:
-                    widen(n + 1, 0, "scalar")
-                    widen(n + 1, 1, "scalar")
-                if n == 1:
+                        epilogue(pair_tiles(pair))
+                if u < TILES:
+                    product(u, 0)
+                    turn(("us", u), 1)
+                    product(u, 1)
+                head_groups(n, "V")
+                z_halves(z_ready, "vector")
+                quantize_pair(n - 1)
+                if n == QV_BEAT:
+                    quantize_v()
+                for c in z_ready:
+                    quantize_z(c)
+                if u < TILES:
+                    quantize_us(u)
+                if n + 2 in POOL_ORDERS:
+                    pool_order(wide[2 * (n + 2)], slots[u % SLOTS])
+                head_groups(n, "W")
+                if u + 1 < TILES:
+                    widen(u + 1, 0, "scalar")
+                    widen(u + 1, 1, "scalar")
+                if n == GAIN_BEAT:
                     nc.scalar.copy(out=gain_col[:], in_=gain_raw[:].rearrange("p c t -> p (c t)"))
                 turn(a, 0)
                 empty(a, 0)
                 burst(2 * n)
                 head_groups(n, "A")
-                done = gains_after(2 * n)
+                gains_after(2 * n)
                 if n + 1 in SCALAR_ORDERS:
                     scalar_order(wide[2 * (n + 1) + 1])
                 turn(a, 1)
                 empty(a, 1)
-                for i in done:
-                    if i % 4 == 3:
-                        z_ready.append(i // 4)
-                        for half in range(2):
-                            if Z_ENGINES[half] == "scalar":
-                                group_z(i // 4, half)
                 turn(b, 0)
                 empty(b, 0)
                 turn(b, 1)
@@ -410,18 +454,18 @@ def tile_fourierftgivenbases_w_kernel(tc, w0, coef, g, uc, us_bytes, us_scale, v
                 head_groups(n, "B")
                 burst(2 * n + 1)
 
-            y, z = TILES - 2, TILES - 1
-            before = (TILES - 4, TILES - 3)
-            store((TILES - 6, TILES - 5))
+            store(pair_tiles(HALF - 4))
             code_tiles("uc", y, 2)
             quantize_part(("uc", y), 0, PASSES)
-            quantize_us(z)
+            epilogue(pair_tiles(HALF - 3))
+            store(pair_tiles(HALF - 3))
             quantize_part(("uc", z), 0, 2)
             quantize_part(("uc", z), 2, 2)
-            open_sums((y,), "sums", 2)
+            stage2_pair(HALF - 2, parts(("us", "uc"), every), True, True)
+            open_sums((y,), "us_bank", US_BANKS)
             stage2(y, parts(("us", "uc"), every), True, True)
             open_sums((z,), "us_bank", US_BANKS)
             stage2(z, parts(("us", "uc"), every), True, True)
-            for tiles in (before, (y,), (z,)):
+            for tiles in (pair_tiles(HALF - 2), (y,), (z,)):
                 epilogue(tiles)
                 store(tiles)

@@ -27,19 +27,17 @@ RAW_BUFS = 8
 SLOTS = 4
 US_BANKS = 2
 WIDE_BANKS = 4
-HEAD = [("coef",0,0),("us",0,0),("coef",0,1),("us",0,1),"s",("coef",1),("us",1),"vc",("coef",2),("us",2),"vs",("coef",3),("coef",4),"g",("coef",5),("us",3),("coef",6),("coef",7),("us",4)]
-GAIN_BEAT = -1
-HEAD_STEPS = "t.c.0.0 w.0.0.v w.0.1.v neg t.c.0.1 t.u.0.0 p.0.0 t.u.0.1 p.0.1 w.1.0.s w.1.1.s t.c.1.0 t.c.1.1 g.0.0.4.v t.u.1.0 t.u.1.1 p.1.0 p.1.1 w.2.0.s t.c.2.0 w.2.1.s g.1.0.2.s t.c.2.1 t.u.2.0 t.u.2.1 g.1.2.4.v qp.0 qv p.2.0 p.2.1 qu.0 qu.1 t.c.3.0 t.c.3.1 qp.1 qu.2 t.c.4.0 t.c.4.1 gc l w.3.0.s w.3.1.s m.0 a.0 t.c.5.0 t.c.5.1 m.1 a.1"
-US_AHEAD = 0
-START_BEAT = 3
-STAGE1_DONE = 2
-V_GROUPS = []
-QV_BEAT = -1
+HEAD = [("us",0,0,1),("us",0,1,2),"s",("us",0,2,4),("us",1),"vc",("us",2),"vs",("us",3),("coef",0),("coef",1),("coef",2),"g",("coef",3),("us",4),("coef",4),("coef",5),("us",5),("coef",6),("coef",7)]
+V_SLOT = 0
+HEAD_STEPS = "w.0.0.1.v w.0.1.2.s neg w.0.2.4.s t.u.0.0.1 p.0.0.1 t.u.0.1.2 p.0.1.2 t.u.0.2.4.w p.0.2.4 w.1.0.2.s w.1.2.4.s t.u.1.0.2 p.1.0.2 t.u.1.2.4 p.1.2.4 H.0.0 H.0.1 H.1.0 H.1.1 w.2.0.4.s t.u.2.0.2.w p.2.0.2 t.u.2.2.4.w p.2.2.4 w.3.0.4.s t.u.3.0.2 p.3.0.2 t.u.3.2.4 p.3.2.4 t.c.0.0.2 t.c.0.2.4 t.c.1.0.2 t.c.1.2.4 qv.0 qv.1 qp.0 qu.0 qu.1 qu.2 qu.3 t.c.2.0.2 w.4.0.4.s t.c.2.2.4 gc t.c.3.0.2 t.c.3.2.4"
+US_AHEAD = 2
+START_BEAT = 2
+STAGE1_DONE = 0
 STAGE1_FROM = 4
-SCALAR_ORDERS = [11,13]
-POOL_ORDERS = []
-POOL_PASSES = 3
-Z_ENGINES = ("vector","vector")
+SCALAR_ORDERS = [11,13,15]
+POOL_ORDERS = [4,6,8,10,12,13,14]
+POOL_PASSES = 2
+Z_ENGINES = ("pool","pool")
 
 
 def tile_fourierftgivenbases_w_kernel(tc, w0, coef, g, uc, us_bytes, us_scale, vc, vs, out):
@@ -66,8 +64,9 @@ def tile_fourierftgivenbases_w_kernel(tc, w0, coef, g, uc, us_bytes, us_scale, v
         gain_col = keep.tile([P, TILES], F32, name="gain_col")
         scale_raw = keep.tile([P, PASSES, 4], F32, name="scale_raw")
         neg_scale = keep.tile([P, PASSES, 4], F32, name="neg_scale")
-        v_raw = [keep.tile([P, N], BF16, name="v_raw%d" % j, align_bytes=64) for j in range(2)]
-        v_grouped = keep.tile([P, PASSES, 2 * F, 4], BF16, name="v_grouped", align_bytes=64)
+        v_raw = keep.tile([P, 2, N], BF16, name="v_raw", align_bytes=64)
+        v_second = keep.tile([P, N], BF16, name="v_second", align_bytes=64)
+        v_first = keep.tile([P, N], BF16, name="v_first", align_bytes=64)
         v_codes = keep.tile([P, PASSES, 2 * F], U32, name="v_codes", align_bytes=64)
         v_scales = keep.tile([P, PASSES, 2 * F], U8, name="v_scales", align_bytes=64)
         z_codes = keep.tile([P, PASSES, 2 * F], U32, name="z_codes", align_bytes=64)
@@ -98,38 +97,57 @@ def tile_fourierftgivenbases_w_kernel(tc, w0, coef, g, uc, us_bytes, us_scale, v
             raw_tile(key)
             nc.sync.dma_start(out=raw[key][:], in_=rows[kind][i // 4, i % 4])
 
-        def load_half(key, h):
+        def load_part(key, first, end):
             kind, i = key
-            if h == 0:
+            if first == 0:
                 raw_tile(key)
-            cols = slice(h * N // 2, (h + 1) * N // 2)
+            cols = slice(first * 512, end * 512)
             nc.sync.dma_start(out=raw[key][:, cols], in_=rows[kind][i // 4, i % 4][:, cols])
 
         def load_v(which):
             nc.sync.dma_start(
-                out=v_raw[which][:].rearrange("p (c j f) -> p c j f", c=PASSES, j=4),
+                out=v_raw[:, which, :].rearrange("p (c j f) -> p c j f", c=PASSES, j=4),
                 in_=(vc, vs)[which].rearrange("(c p j) f -> p c j f", p=P, j=4),
             )
 
-        def group_v(which, first, last, engine):
-            dst = v_grouped[:, first:last, which * F : (which + 1) * F, :].rearrange("p c (n i) j -> p c n j i", i=4)
-            src = v_raw[which][:].rearrange("p (c j n i) -> p c n j i", c=PASSES, j=4, i=4)[:, first:last]
+        def v_half(h):
+            return (v_first, v_second)[h][:]
+
+        def group_v(which, first, end, engine):
+            h = first // 2
+            dst = v_half(h).rearrange("p (c w n i j) -> p c w n j i", c=2, w=2, i=4, j=4)[:, first - 2 * h : end - 2 * h, which]
+            src = v_raw[:, which, :].rearrange("p (c j n i) -> p c n j i", c=PASSES, j=4, i=4)[:, first:end]
             if engine == "scalar":
                 nc.scalar.copy(out=dst, in_=src)
             else:
                 nc.vector.tensor_copy(out=dst, in_=src)
 
-        def quantize_v():
-            nc.vector.quantize_mx(
-                out=v_codes[:].rearrange("p c f -> p (c f)").bitcast(FP8X4),
-                scales=v_scales[:].rearrange("p c f -> p (c f)"),
-                in_=v_grouped[:].rearrange("p c f j -> p (c f j)"),
+        def pool_copy(dst, src):
+            nc.gpsimd.tensor_scalar(out=dst, in0=src, scalar1=1.0, scalar2=0.0, op0=MULT, op1=ADD)
+
+        def pool_group_v(c):
+            pool_copy(
+                v_half(c // 2).rearrange("p (c w f j) -> p c w f j", c=2, w=2, j=4)[:, c % 2],
+                v_raw[:].rearrange("p w (c j f) -> p c w f j", c=PASSES, j=4)[:, c],
             )
 
-        def widen(i, h, engine):
-            if h == 0:
+        def pool_group_whole(which, h):
+            pool_copy(
+                v_half(h).rearrange("p (c w f j) -> p w c f j", c=2, w=2, j=4)[:, which],
+                v_raw[:, which, :].rearrange("p (c j f) -> p c f j", c=PASSES, j=4)[:, 2 * h : 2 * h + 2],
+            )
+
+        def quantize_v(h):
+            nc.vector.quantize_mx(
+                out=v_codes[:, 2 * h : 2 * h + 2, :].rearrange("p c f -> p (c f)").bitcast(FP8X4),
+                scales=v_scales[:, 2 * h : 2 * h + 2, :].rearrange("p c f -> p (c f)"),
+                in_=v_half(h),
+            )
+
+        def widen(i, first, end, engine):
+            if first == 0:
                 widened[i] = stage.tile([P, N], BF16, name="widened", bufs=3, align_bytes=64)
-            cols = slice(h * N // 2, (h + 1) * N // 2)
+            cols = slice(first * 512, end * 512)
             if engine == "scalar":
                 nc.scalar.copy(out=widened[i][:, cols], in_=raw[("us", i)][:, cols].bitcast(FP8))
             else:
@@ -155,25 +173,23 @@ def tile_fourierftgivenbases_w_kernel(tc, w0, coef, g, uc, us_bytes, us_scale, v
             )
             ordered[key] = (tile, POOL_PASSES)
 
-        def turn(key, h):
+        def turn(key, first, end, tag=None):
             kind, i = key
-            if kind == "us":
+            if kind == "us" and tag is None:
                 bank = psum.tile([P, 2, 2, P], F32, name="us_bank", bufs=US_BANKS)
-                words = widened[i][:].bitcast(F32)
             else:
                 bank = psum.tile([P, 2, 2, P], F32, name="wide_bank", bufs=WIDE_BANKS)
-                words = raw[key][:].bitcast(F32)
+            words = (widened[i] if kind == "us" else raw[key])[:].bitcast(F32)
             tile, count = ordered.get(key, (None, 0))
-            for j in range(2):
-                c = 2 * h + j
+            for c in range(first, end):
                 for u in range(2):
                     if c < count:
-                        first = P * (count * u + c)
-                        src = tile[:].bitcast(F32)[:, first : first + P]
+                        start = P * (count * u + c)
+                        src = tile[:].bitcast(F32)[:, start : start + P]
                     else:
                         src = words[:, 256 * c + u : 256 * (c + 1) : 2]
-                    nc.tensor.transpose(bank[:, u, j, :], src, ident[:])
-            turned[(key, h)] = bank
+                    nc.tensor.transpose(bank[:, u, c - first, :], src, ident[:])
+            turned[(key, first)] = bank
 
         def empty(key, h):
             kind, i = key
@@ -185,22 +201,23 @@ def tile_fourierftgivenbases_w_kernel(tc, w0, coef, g, uc, us_bytes, us_scale, v
             dst = grouped[key].bitcast(F32)[:, 512 * h : 512 * (h + 1)]
             nc.scalar.copy(
                 out=dst.rearrange("p (n i u) -> p n u i", u=2, i=4),
-                in_=turned[(key, h)][:].rearrange("p u c (n i) -> p (c n) u i", i=4),
+                in_=turned[(key, 2 * h)][:].rearrange("p u c (n i) -> p (c n) u i", i=4),
             )
 
-        def product(i, h):
+        def product(i, first, end):
+            count = end - first
             grouped[("us", i)] = slots[i % SLOTS][:]
-            values = turned[(("us", i), h)][:].rearrange("p u c m -> p (u c m)").bitcast(BF16)
-            factors = neg_scale[:, 2 * h : 2 * h + 2, :].rearrange("p c (o u e) -> p c o u e", o=1, u=2)
+            values = turned[(("us", i), first)][:].rearrange("p u c m -> p (u c m)").bitcast(BF16)
+            factors = neg_scale[:, first:end, :].rearrange("p c (o u e) -> p c o u e", o=1, u=2)
             nc.vector.tensor_tensor(
-                out=grouped[("us", i)][:, 1024 * h : 1024 * (h + 1)].rearrange("p (c m u e) -> p c m u e", c=2, u=2, e=2),
-                in0=values.rearrange("p (u c m e) -> p c m u e", u=2, c=2, e=2),
-                in1=factors.to_broadcast([P, 2, P, 2, 2]),
+                out=grouped[("us", i)][:, 512 * first : 512 * end].rearrange("p (c m u e) -> p c m u e", c=count, u=2, e=2),
+                in0=values.rearrange("p (u c m e) -> p c m u e", u=2, c=2, e=2)[:, 0:count],
+                in1=factors.to_broadcast([P, count, P, 2, 2]),
                 op=MULT,
             )
 
         def code_tiles(kind, first, count):
-            depth = HALF + 5 if kind == "us" else 4
+            depth = TILES if kind == "us" else 4
             ct = stage.tile([P, count * PASSES * P], U32, name=kind + "_codes", bufs=depth, align_bytes=64)
             st = stage.tile([P, count * PASSES * P], U8, name=kind + "_scales", bufs=depth, align_bytes=64)
             for j in range(count):
@@ -257,6 +274,10 @@ def tile_fourierftgivenbases_w_kernel(tc, w0, coef, g, uc, us_bytes, us_scale, v
                 nc.vector.tensor_copy(out=dst, in_=src)
             else:
                 nc.scalar.copy(out=dst, in_=src)
+
+        def pool_group_z(c, tile):
+            z_grouped[c] = tile[:, 0 : 8 * F].rearrange("p (f t) -> p f t", t=4)
+            pool_copy(z_grouped[c], z_flat[c][:].rearrange("p t f -> p f t"))
 
         def quantize_z(c):
             nc.vector.quantize_mx(
@@ -336,11 +357,6 @@ def tile_fourierftgivenbases_w_kernel(tc, w0, coef, g, uc, us_bytes, us_scale, v
                 gain(done[-1])
             return [i // 4 for i in done if i % 4 == 3]
 
-        def head_groups(beat, where):
-            for at, place, which, first, end, engine in V_GROUPS:
-                if (at, place) == (beat, where):
-                    group_v(which, first, end, engine)
-
         def z_halves(ready, engine):
             for c in ready:
                 for half in range(2):
@@ -358,8 +374,8 @@ def tile_fourierftgivenbases_w_kernel(tc, w0, coef, g, uc, us_bytes, us_scale, v
                     nc.sync.dma_start(out=gain_raw[:], in_=g.rearrange("(c p t) -> p c t", p=P, t=4))
                 elif key in ("vc", "vs"):
                     load_v(("vc", "vs").index(key))
-                elif len(key) == 3:
-                    load_half(key[:2], key[2])
+                elif len(key) == 4:
+                    load_part(key[:2], key[2], key[3])
                 else:
                     load(key)
 
@@ -368,18 +384,22 @@ def tile_fourierftgivenbases_w_kernel(tc, w0, coef, g, uc, us_bytes, us_scale, v
             for word in HEAD_STEPS.split():
                 step = word.split(".")
                 if step[0] == "t":
-                    key, h = (names[step[1]], int(step[2])), int(step[3])
-                    turn(key, h)
+                    key, first, end = (names[step[1]], int(step[2])), int(step[3]), int(step[4])
+                    turn(key, first, end, step[5] if len(step) > 5 else None)
                     if key[0] == "coef":
-                        empty(key, h)
+                        empty(key, first // 2)
                 elif step[0] == "p":
-                    product(int(step[1]), int(step[2]))
+                    product(int(step[1]), int(step[2]), int(step[3]))
                 elif step[0] == "w":
-                    widen(int(step[1]), int(step[2]), engines[step[3]])
+                    widen(int(step[1]), int(step[2]), int(step[3]), engines[step[4]])
                 elif step[0] == "g":
                     group_v(int(step[1]), int(step[2]), int(step[3]), engines[step[4]])
+                elif step[0] == "G":
+                    pool_group_v(int(step[1]))
+                elif step[0] == "H":
+                    pool_group_whole(int(step[1]), int(step[2]))
                 elif step[0] == "qv":
-                    quantize_v()
+                    quantize_v(int(step[1]))
                 elif step[0] == "qu":
                     quantize_us(int(step[1]))
                 elif step[0] == "qp":
@@ -389,8 +409,7 @@ def tile_fourierftgivenbases_w_kernel(tc, w0, coef, g, uc, us_bytes, us_scale, v
                 elif step[0] == "a":
                     gain(int(step[1]))
                 elif step[0] == "l":
-                    load(("coef", 8))
-                    load(("coef", 9))
+                    load((names[step[1]], int(step[2])))
                 elif step[0] == "gc":
                     nc.scalar.copy(out=gain_col[:], in_=gain_raw[:].rearrange("p c t -> p (c t)"))
                 elif step[0] == "neg":
@@ -411,47 +430,41 @@ def tile_fourierftgivenbases_w_kernel(tc, w0, coef, g, uc, us_bytes, us_scale, v
                         store(pair_tiles(pair))
 
                 if u < TILES:
-                    turn(("us", u), 0)
+                    turn(("us", u), 0, 2)
                 z_ready = gains_after(2 * n - 1)
                 z_halves(z_ready, "scalar")
+                if Z_ENGINES[0] == "pool":
+                    for c in z_ready:
+                        pool_group_z(c, slots[(u - 1) % SLOTS])
                 if n >= HALF + 4:
                     for pair in (0, 1) if n == HALF + 4 else (n - HALF - 3,):
                         epilogue(pair_tiles(pair))
                 if u < TILES:
-                    product(u, 0)
-                    turn(("us", u), 1)
-                    product(u, 1)
-                head_groups(n, "V")
+                    product(u, 0, 2)
+                    turn(("us", u), 2, 4)
+                    product(u, 2, 4)
                 z_halves(z_ready, "vector")
                 quantize_pair(n - 1)
-                if n == QV_BEAT:
-                    quantize_v()
                 for c in z_ready:
                     quantize_z(c)
                 if u < TILES:
                     quantize_us(u)
                 if n + 2 in POOL_ORDERS:
                     pool_order(wide[2 * (n + 2)], slots[u % SLOTS])
-                head_groups(n, "W")
                 if u + 1 < TILES:
-                    widen(u + 1, 0, "scalar")
-                    widen(u + 1, 1, "scalar")
-                if n == GAIN_BEAT:
-                    nc.scalar.copy(out=gain_col[:], in_=gain_raw[:].rearrange("p c t -> p (c t)"))
-                turn(a, 0)
+                    widen(u + 1, 0, 4, "scalar")
+                turn(a, 0, 2)
                 empty(a, 0)
                 burst(2 * n)
-                head_groups(n, "A")
                 gains_after(2 * n)
                 if n + 1 in SCALAR_ORDERS:
                     scalar_order(wide[2 * (n + 1) + 1])
-                turn(a, 1)
+                turn(a, 2, 4)
                 empty(a, 1)
-                turn(b, 0)
+                turn(b, 0, 2)
                 empty(b, 0)
-                turn(b, 1)
+                turn(b, 2, 4)
                 empty(b, 1)
-                head_groups(n, "B")
                 burst(2 * n + 1)
 
             store(pair_tiles(HALF - 4))

@@ -36,7 +36,8 @@ STAGE1_DONE = 0
 STAGE1_FROM = 4
 SCALAR_ORDERS = [11,13,15]
 POOL_ORDERS = [4,6,8,10,12,13,14]
-POOL_PASSES = 2
+POOL_PASSES = 4
+POOL_WORDS = True
 Z_ENGINES = ("pool","pool")
 
 
@@ -163,14 +164,16 @@ def tile_fourierftgivenbases_w_kernel(tc, w0, coef, g, uc, us_bytes, us_scale, v
 
         def pool_order(key, tile):
             width = POOL_PASSES * 512
-            nc.gpsimd.tensor_scalar(
-                out=tile[:, 0:width].rearrange("p (u n e) -> p u n e", u=2, e=2),
-                in0=raw[key][:, 0:width].rearrange("p (n u e) -> p u n e", u=2, e=2),
-                scalar1=1.0,
-                scalar2=0.0,
-                op0=MULT,
-                op1=ADD,
-            )
+            if POOL_WORDS:
+                nc.gpsimd.tensor_copy(
+                    out=tile[:, 0:width].bitcast(F32).rearrange("p (u n) -> p u n", u=2),
+                    in_=raw[key][:, 0:width].bitcast(F32).rearrange("p (n u) -> p u n", u=2),
+                )
+            else:
+                pool_copy(
+                    tile[:, 0:width].rearrange("p (u n e) -> p u n e", u=2, e=2),
+                    raw[key][:, 0:width].rearrange("p (n u e) -> p u n e", u=2, e=2),
+                )
             ordered[key] = (tile, POOL_PASSES)
 
         def turn(key, first, end, tag=None):

@@ -27,18 +27,26 @@ RAW_BUFS = 8
 SLOTS = 4
 US_BANKS = 2
 WIDE_BANKS = 4
-HEAD = [("us",0,0,1),("us",0,1,2),"s",("us",0,2,4),("us",1),"vc",("us",2),"vs",("us",3),("coef",0),("coef",1),("coef",2),"g",("coef",3),("us",4),("coef",4),("coef",5),("us",5),("coef",6),("coef",7)]
-V_SLOT = 0
-HEAD_STEPS = "w.0.0.1.v w.0.1.2.s neg w.0.2.4.s t.u.0.0.1 p.0.0.1 t.u.0.1.2 p.0.1.2 t.u.0.2.4.w p.0.2.4 w.1.0.2.s w.1.2.4.s t.u.1.0.2 p.1.0.2 t.u.1.2.4 p.1.2.4 H.0.0 H.0.1 H.1.0 H.1.1 w.2.0.4.s t.u.2.0.2.w p.2.0.2 t.u.2.2.4.w p.2.2.4 w.3.0.4.s t.u.3.0.2 p.3.0.2 t.u.3.2.4 p.3.2.4 t.c.0.0.2 t.c.0.2.4 t.c.1.0.2 t.c.1.2.4 qv.0 qv.1 qp.0 qu.0 qu.1 qu.2 qu.3 t.c.2.0.2 w.4.0.4.s t.c.2.2.4 gc t.c.3.0.2 t.c.3.2.4"
-US_AHEAD = 2
+HEAD = [("us",0,0,1),("us",0,1,2),"s",("us",0,2,4),("us",1),("us",2),"vc",("us",3),("coef",0),"vs",("us",4),("coef",1),("coef",2),"g",("coef",3),("coef",4),("us",5),("coef",5),("coef",6),("coef",7)]
+HEAD_STEPS = "w.0.0.1.v w.0.1.2.s neg w.0.2.4.s t.u.0.0.1 p.0.0.1 t.u.0.1.2 p.0.1.2 t.u.0.2.4.w p.0.2.4 w.1.0.2.s w.1.2.4.g t.u.1.0.2 p.1.0.2 t.u.1.2.4 p.1.2.4 H.0 H.1 w.2.0.4.s t.u.2.0.2.w p.2.0.2 t.u.2.2.4.w p.2.2.4 w.3.0.4.s t.c.0.0.2 t.c.0.2.4 t.u.3.0.2 p.3.0.2 t.u.3.2.4 p.3.2.4 w.4.0.4.s t.c.1.0.2 t.c.1.2.4 qv qp.0 qu.0 qu.1 qu.2 qu.3 t.c.2.0.2 t.c.2.2.4 gc t.c.3.0.2 t.c.3.2.4"
+US_SKIP = [14, 15]
+US_LOAD_BEATS = 3
+POOL_WIDENS = [2,4,8]
+POOL_WIDEN_PASSES = 2
+V_EMPTIES = []
+LAST_EARLY = 1
+LAST_Z = "pool"
+POOL_PRODUCTS = []
+V_WIDEN = []
+V_ORDERS = []
 START_BEAT = 2
 STAGE1_DONE = 0
 STAGE1_FROM = 4
-SCALAR_ORDERS = [11,13,15]
-POOL_ORDERS = [4,6,8,10,12,13,14]
+SCALAR_ORDERS = [12,14,15]
+POOL_ORDERS = [4,7,12,13,14]
 POOL_PASSES = 4
 POOL_WORDS = True
-Z_ENGINES = ("pool","pool")
+Z_ENGINES = ("scalar","scalar")
 
 
 def tile_fourierftgivenbases_w_kernel(tc, w0, coef, g, uc, us_bytes, us_scale, vc, vs, out):
@@ -61,13 +69,15 @@ def tile_fourierftgivenbases_w_kernel(tc, w0, coef, g, uc, us_bytes, us_scale, v
         ident = keep.tile([P, P], F32, name="ident")
         make_identity(nc, ident[:])
 
+        ones = keep.tile([P, 1], F32, name="ones")
+        if V_WIDEN:
+            nc.gpsimd.memset(ones[:], 1.0)
         gain_raw = keep.tile([P, 4, 4], BF16, name="gain_raw")
         gain_col = keep.tile([P, TILES], F32, name="gain_col")
         scale_raw = keep.tile([P, PASSES, 4], F32, name="scale_raw")
         neg_scale = keep.tile([P, PASSES, 4], F32, name="neg_scale")
         v_raw = keep.tile([P, 2, N], BF16, name="v_raw", align_bytes=64)
-        v_second = keep.tile([P, N], BF16, name="v_second", align_bytes=64)
-        v_first = keep.tile([P, N], BF16, name="v_first", align_bytes=64)
+        v_grouped = keep.tile([P, PASSES, 2, F, 4], BF16, name="v_grouped", align_bytes=64)
         v_codes = keep.tile([P, PASSES, 2 * F], U32, name="v_codes", align_bytes=64)
         v_scales = keep.tile([P, PASSES, 2 * F], U8, name="v_scales", align_bytes=64)
         z_codes = keep.tile([P, PASSES, 2 * F], U32, name="z_codes", align_bytes=64)
@@ -78,6 +88,9 @@ def tile_fourierftgivenbases_w_kernel(tc, w0, coef, g, uc, us_bytes, us_scale, v
         raw = {}
         widened = {}
         ordered = {}
+        words_of = {}
+        plain = {}
+        last_pass = {}
         grouped = {}
         turned = {}
         codes = {}
@@ -111,52 +124,59 @@ def tile_fourierftgivenbases_w_kernel(tc, w0, coef, g, uc, us_bytes, us_scale, v
                 in_=(vc, vs)[which].rearrange("(c p j) f -> p c j f", p=P, j=4),
             )
 
-        def v_half(h):
-            return (v_first, v_second)[h][:]
-
-        def group_v(which, first, end, engine):
-            h = first // 2
-            dst = v_half(h).rearrange("p (c w n i j) -> p c w n j i", c=2, w=2, i=4, j=4)[:, first - 2 * h : end - 2 * h, which]
-            src = v_raw[:, which, :].rearrange("p (c j n i) -> p c n j i", c=PASSES, j=4, i=4)[:, first:end]
-            if engine == "scalar":
-                nc.scalar.copy(out=dst, in_=src)
-            else:
-                nc.vector.tensor_copy(out=dst, in_=src)
-
         def pool_copy(dst, src):
             nc.gpsimd.tensor_scalar(out=dst, in0=src, scalar1=1.0, scalar2=0.0, op0=MULT, op1=ADD)
 
-        def pool_group_v(c):
+        def pool_group_v(which):
             pool_copy(
-                v_half(c // 2).rearrange("p (c w f j) -> p c w f j", c=2, w=2, j=4)[:, c % 2],
-                v_raw[:].rearrange("p w (c j f) -> p c w f j", c=PASSES, j=4)[:, c],
+                v_grouped[:, :, which],
+                v_raw[:, which, :].rearrange("p (c j f) -> p c f j", c=PASSES, j=4),
             )
 
-        def pool_group_whole(which, h):
-            pool_copy(
-                v_half(h).rearrange("p (c w f j) -> p w c f j", c=2, w=2, j=4)[:, which],
-                v_raw[:, which, :].rearrange("p (c j f) -> p c f j", c=PASSES, j=4)[:, 2 * h : 2 * h + 2],
-            )
-
-        def quantize_v(h):
+        def quantize_v():
             nc.vector.quantize_mx(
-                out=v_codes[:, 2 * h : 2 * h + 2, :].rearrange("p c f -> p (c f)").bitcast(FP8X4),
-                scales=v_scales[:, 2 * h : 2 * h + 2, :].rearrange("p c f -> p (c f)"),
-                in_=v_half(h),
+                out=v_codes[:].rearrange("p c f -> p (c f)").bitcast(FP8X4),
+                scales=v_scales[:].rearrange("p c f -> p (c f)"),
+                in_=v_grouped[:].rearrange("p c w f j -> p (c w f j)"),
             )
 
-        def widen(i, first, end, engine):
-            if first == 0:
-                widened[i] = stage.tile([P, N], BF16, name="widened", bufs=3, align_bytes=64)
+        def widen(i, first, end, engine, tile=None):
+            if tile is None and i not in widened:
+                widened[i] = stage.tile([P, N], BF16, name="widened", bufs=4, align_bytes=64)
+            tile = widened[i] if tile is None else tile
+            for c in range(first, end):
+                words_of[(i, c)] = tile
             cols = slice(first * 512, end * 512)
+            src = raw[("us", i)][:, cols].bitcast(FP8)
             if engine == "scalar":
-                nc.scalar.copy(out=widened[i][:, cols], in_=raw[("us", i)][:, cols].bitcast(FP8))
+                nc.scalar.copy(out=tile[:, cols], in_=src)
+            elif engine == "pool":
+                nc.gpsimd.tensor_copy(out=tile[:, cols], in_=src)
             else:
-                nc.vector.tensor_copy(out=widened[i][:, cols], in_=raw[("us", i)][:, cols].bitcast(FP8))
+                nc.vector.tensor_copy(out=tile[:, cols], in_=src)
+
+        def widen_ordered(i):
+            tile = stage.tile([P, N], BF16, name="widened", bufs=4, align_bytes=64)
+            nc.vector.tensor_scalar(
+                out=tile[:].rearrange("p (u n e) -> p n u e", u=2, e=2),
+                in0=raw[("us", i)][:].bitcast(FP8).rearrange("p (n u e) -> p n u e", u=2, e=2),
+                scalar1=ones[:],
+                scalar2=None,
+                op0=MULT,
+            )
+            ordered[("us", i)] = (tile, PASSES)
 
         def scalar_order(key):
             tile = stage.tile([P, N], BF16, name="ordered", bufs=2, align_bytes=64)
             nc.scalar.copy(
+                out=tile[:].bitcast(F32).rearrange("p (u n i) -> p n u i", u=2, i=4),
+                in_=raw[key][:].bitcast(F32).rearrange("p (n i u) -> p n u i", u=2, i=4),
+            )
+            ordered[key] = (tile, PASSES)
+
+        def vector_order(key):
+            tile = stage.tile([P, N], BF16, name="ordered", bufs=2, align_bytes=64)
+            nc.vector.tensor_copy(
                 out=tile[:].bitcast(F32).rearrange("p (u n i) -> p n u i", u=2, i=4),
                 in_=raw[key][:].bitcast(F32).rearrange("p (n i u) -> p n u i", u=2, i=4),
             )
@@ -182,7 +202,6 @@ def tile_fourierftgivenbases_w_kernel(tc, w0, coef, g, uc, us_bytes, us_scale, v
                 bank = psum.tile([P, 2, 2, P], F32, name="us_bank", bufs=US_BANKS)
             else:
                 bank = psum.tile([P, 2, 2, P], F32, name="wide_bank", bufs=WIDE_BANKS)
-            words = (widened[i] if kind == "us" else raw[key])[:].bitcast(F32)
             tile, count = ordered.get(key, (None, 0))
             for c in range(first, end):
                 for u in range(2):
@@ -190,11 +209,12 @@ def tile_fourierftgivenbases_w_kernel(tc, w0, coef, g, uc, us_bytes, us_scale, v
                         start = P * (count * u + c)
                         src = tile[:].bitcast(F32)[:, start : start + P]
                     else:
+                        words = (words_of[(i, c)] if kind == "us" else raw[key])[:].bitcast(F32)
                         src = words[:, 256 * c + u : 256 * (c + 1) : 2]
                     nc.tensor.transpose(bank[:, u, c - first, :], src, ident[:])
             turned[(key, first)] = bank
 
-        def empty(key, h):
+        def empty(key, h, engine="scalar"):
             kind, i = key
             if h == 0 and i % 2 == 0:
                 both = stage.tile([P, 2, N], BF16, name="grouped", bufs=3, align_bytes=64)
@@ -202,7 +222,8 @@ def tile_fourierftgivenbases_w_kernel(tc, w0, coef, g, uc, us_bytes, us_scale, v
                 grouped[(kind, i + 1)] = both[:, 1, :]
                 grouped[(kind, "pair", i // 2)] = both[:].rearrange("p j n -> p (j n)")
             dst = grouped[key].bitcast(F32)[:, 512 * h : 512 * (h + 1)]
-            nc.scalar.copy(
+            copy = nc.scalar.copy if engine == "scalar" else nc.vector.tensor_copy
+            copy(
                 out=dst.rearrange("p (n i u) -> p n u i", u=2, i=4),
                 in_=turned[(key, 2 * h)][:].rearrange("p u c (n i) -> p (c n) u i", i=4),
             )
@@ -218,6 +239,23 @@ def tile_fourierftgivenbases_w_kernel(tc, w0, coef, g, uc, us_bytes, us_scale, v
                 in1=factors.to_broadcast([P, count, P, 2, 2]),
                 op=MULT,
             )
+
+        def empty_last_pass(i):
+            plain[i] = stage.tile([P, 512], BF16, name="plain", bufs=2, align_bytes=64)
+            nc.scalar.copy(
+                out=plain[i][:].bitcast(F32).rearrange("p (n i u) -> p n u i", u=2, i=4),
+                in_=turned[(("us", i), 3)][:, :, 0, :].rearrange("p u (n i) -> p n u i", i=4),
+            )
+
+        def pool_product(i, tile):
+            factors = neg_scale[:, 3:4, :].to_broadcast([P, P, 4])
+            nc.gpsimd.tensor_tensor(
+                out=tile[:, 0:512].rearrange("p (m t) -> p m t", t=4),
+                in0=plain[i][:].rearrange("p (m t) -> p m t", t=4),
+                in1=factors,
+                op=MULT,
+            )
+            last_pass[i] = tile[:, 0:512]
 
         def code_tiles(kind, first, count):
             depth = TILES if kind == "us" else 4
@@ -241,8 +279,13 @@ def tile_fourierftgivenbases_w_kernel(tc, w0, coef, g, uc, us_bytes, us_scale, v
             )
 
         def quantize_us(i):
+            key = ("us", i)
             code_tiles("us", i, 1)
-            quantize_part(("us", i), 0, PASSES)
+            if i in last_pass:
+                nc.vector.quantize_mx(
+                    out=codes[key][:, 3 * P :].bitcast(FP8X4), scales=scales[key][:, 3 * P :], in_=last_pass[i]
+                )
+            quantize_part(key, 0, 3 if i in last_pass else PASSES)
 
         def mm(o, key, c, moving, moving_scales, start, stop):
             nc.tensor.matmul_mx(
@@ -337,6 +380,7 @@ def tile_fourierftgivenbases_w_kernel(tc, w0, coef, g, uc, us_bytes, us_scale, v
         early = range(PASSES - 1)
         last = [PASSES - 1]
         stage1_at = {i: max(i + 4, STAGE1_FROM + i // 2) for i in range(STAGE1_DONE, TILES)}
+        stage1_at[TILES - 1] -= LAST_EARLY
         y, z = TILES - 2, TILES - 1
 
         def burst(j):
@@ -347,7 +391,11 @@ def tile_fourierftgivenbases_w_kernel(tc, w0, coef, g, uc, us_bytes, us_scale, v
                         gain(i)
             beat, second = divmod(j, 2)
             pair = beat - HALF - 2
-            if pair == 0:
+            if (pair, second) == (-1, 1) and LAST_EARLY:
+                stage2_pair(0, parts(("us",), early[:2]), True, False)
+            elif pair == 0 and LAST_EARLY:
+                stage2_pair(0, (parts(("us",), early[2:]) + parts(("uc",), early[:1]), parts(("uc",), early[1:]))[second], False, False)
+            elif pair == 0:
                 stage2_pair(0, parts((("us", "uc")[second],), early), second == 0, False)
             elif pair > 0:
                 if (pair, second) == (1, 0):
@@ -383,7 +431,7 @@ def tile_fourierftgivenbases_w_kernel(tc, w0, coef, g, uc, us_bytes, us_scale, v
                     load(key)
 
             names = {"u": "us", "c": "coef"}
-            engines = {"s": "scalar", "v": "vector"}
+            engines = {"s": "scalar", "v": "vector", "g": "pool"}
             for word in HEAD_STEPS.split():
                 step = word.split(".")
                 if step[0] == "t":
@@ -395,14 +443,10 @@ def tile_fourierftgivenbases_w_kernel(tc, w0, coef, g, uc, us_bytes, us_scale, v
                     product(int(step[1]), int(step[2]), int(step[3]))
                 elif step[0] == "w":
                     widen(int(step[1]), int(step[2]), int(step[3]), engines[step[4]])
-                elif step[0] == "g":
-                    group_v(int(step[1]), int(step[2]), int(step[3]), engines[step[4]])
-                elif step[0] == "G":
-                    pool_group_v(int(step[1]))
                 elif step[0] == "H":
-                    pool_group_whole(int(step[1]), int(step[2]))
+                    pool_group_v(int(step[1]))
                 elif step[0] == "qv":
-                    quantize_v(int(step[1]))
+                    quantize_v()
                 elif step[0] == "qu":
                     quantize_us(int(step[1]))
                 elif step[0] == "qp":
@@ -418,13 +462,22 @@ def tile_fourierftgivenbases_w_kernel(tc, w0, coef, g, uc, us_bytes, us_scale, v
                 elif step[0] == "neg":
                     nc.vector.tensor_scalar(out=neg_scale[:], in0=scale_raw[:], scalar1=-1.0, scalar2=None, op0=MULT)
 
+            us_beats = [n for n in range(START_BEAT, BEATS) if n not in US_SKIP]
+            us_of = {n: TILES - len(us_beats) + j for j, n in enumerate(us_beats)}
+            newest = TILES - len(us_beats) - 1
+            waiting = []
+            late = []
             for n in range(START_BEAT, BEATS):
                 a, b = wide[2 * n], wide[2 * n + 1]
-                u = n + US_AHEAD
+                u = us_of.get(n)
+                following = us_of.get(min([m for m in us_beats if m > n], default=None))
                 ahead = n + LOAD_BEATS
+                for m in us_beats:
+                    if max(m - US_LOAD_BEATS, START_BEAT) == n and ("us", us_of[m]) not in HEAD:
+                        load(("us", us_of[m]))
                 if ahead < BEATS:
-                    for key in (("us", ahead + US_AHEAD), wide[2 * ahead], wide[2 * ahead + 1]):
-                        if key not in HEAD and key[1] < TILES:
+                    for key in (wide[2 * ahead], wide[2 * ahead + 1]):
+                        if key not in HEAD:
                             load(key)
                 if n == HALF - 1:
                     nc.sync.dma_start(out=w0_sb[:], in_=w0_v)
@@ -432,34 +485,59 @@ def tile_fourierftgivenbases_w_kernel(tc, w0, coef, g, uc, us_bytes, us_scale, v
                     for pair in (0, 1) if n == HALF + 5 else (n - HALF - 4,):
                         store(pair_tiles(pair))
 
-                if u < TILES:
+                if u is not None:
                     turn(("us", u), 0, 2)
-                z_ready = gains_after(2 * n - 1)
-                z_halves(z_ready, "scalar")
-                if Z_ENGINES[0] == "pool":
-                    for c in z_ready:
-                        pool_group_z(c, slots[(u - 1) % SLOTS])
+                gained = late + gains_after(2 * n - 1)
+                z_ready = waiting + [c for c in gained if c == PASSES - 1]
+                waiting = [c for c in gained if c < PASSES - 1]
+                if LAST_Z == "scalar" and PASSES - 1 in z_ready:
+                    for half in range(2):
+                        group_z(PASSES - 1, half)
+                by_pool = 0
+                if u is not None:
+                    free = slots[newest % SLOTS]
+                    if z_ready and z_ready[0] not in z_grouped:
+                        pool_group_z(z_ready[0], free)
+                    elif n in POOL_PRODUCTS:
+                        pool_product(u, free)
+                    elif n in POOL_WIDENS:
+                        by_pool = POOL_WIDEN_PASSES
+                        widen(following, 0, by_pool, "pool", free)
+                    elif n + 1 in POOL_ORDERS:
+                        pool_order(wide[2 * (n + 1)], free)
                 if n >= HALF + 4:
-                    for pair in (0, 1) if n == HALF + 4 else (n - HALF - 3,):
-                        epilogue(pair_tiles(pair))
-                if u < TILES:
+                    epilogue(pair_tiles(n - HALF - 3))
+                if n - 1 in V_EMPTIES:
+                    empty(wide[2 * n - 1], 1, "vector")
+                if u is not None:
                     product(u, 0, 2)
-                    turn(("us", u), 2, 4)
-                    product(u, 2, 4)
-                z_halves(z_ready, "vector")
-                quantize_pair(n - 1)
-                for c in z_ready:
-                    quantize_z(c)
-                if u < TILES:
-                    quantize_us(u)
-                if n + 2 in POOL_ORDERS:
-                    pool_order(wide[2 * (n + 2)], slots[u % SLOTS])
-                if u + 1 < TILES:
-                    widen(u + 1, 0, 4, "scalar")
+                    turn(("us", u), 2, 3 if n in POOL_PRODUCTS else 4)
+                    product(u, 2, 3 if n in POOL_PRODUCTS else 4)
+                else:
+                    z_halves(z_ready, "vector")
+                if n + 1 in POOL_PRODUCTS:
+                    turn(("us", following), 3, 4, "wide")
+                    empty_last_pass(following)
+                if following is not None and following not in V_WIDEN:
+                    widen(following, by_pool, 3 if n + 1 in POOL_PRODUCTS else 4, "scalar")
+                if n + 2 in POOL_PRODUCTS:
+                    widen(us_of[n + 2], 3, 4, "scalar")
                 turn(a, 0, 2)
                 empty(a, 0)
                 burst(2 * n)
-                gains_after(2 * n)
+                if n == HALF + 3:
+                    epilogue(pair_tiles(0))
+                quantize_pair(n - 1)
+                if following in V_WIDEN and u is not None:
+                    widen_ordered(following)
+                if n + 1 in V_ORDERS:
+                    vector_order(wide[2 * (n + 1) + 1])
+                for c in z_ready:
+                    quantize_z(c)
+                if u is not None:
+                    quantize_us(u)
+                    newest = u
+                late = gains_after(2 * n)
                 if n + 1 in SCALAR_ORDERS:
                     scalar_order(wide[2 * (n + 1) + 1])
                 turn(a, 2, 4)
@@ -467,7 +545,8 @@ def tile_fourierftgivenbases_w_kernel(tc, w0, coef, g, uc, us_bytes, us_scale, v
                 turn(b, 0, 2)
                 empty(b, 0)
                 turn(b, 2, 4)
-                empty(b, 1)
+                if n not in V_EMPTIES:
+                    empty(b, 1)
                 burst(2 * n + 1)
 
             store(pair_tiles(HALF - 4))

@@ -28,10 +28,10 @@ SLOTS = 4
 US_BANKS = 2
 WIDE_BANKS = 4
 HEAD = [("us",0,0,1),("us",0,1,2),"s",("us",0,2,4),("us",1),("us",2),"vc",("us",3),("coef",0),"vs",("us",4),("coef",1),("coef",2),"g",("coef",3),("coef",4),("us",5),("coef",5),("coef",6),("coef",7)]
-HEAD_STEPS = "w.0.0.1.v w.0.1.2.s neg w.0.2.4.s t.u.0.0.1 p.0.0.1 t.u.0.1.2 p.0.1.2 t.u.0.2.4.w p.0.2.4 w.1.0.2.s w.1.2.4.g t.u.1.0.2 p.1.0.2 t.u.1.2.4 p.1.2.4 H.0 H.1 w.2.0.4.s t.u.2.0.2.w p.2.0.2 t.u.2.2.4.w p.2.2.4 w.3.0.4.s t.c.0.0.2 t.c.0.2.4 t.u.3.0.2 p.3.0.2 t.u.3.2.4 p.3.2.4 w.4.0.4.s t.c.1.0.2 t.c.1.2.4 qv qp.0 qu.0 qu.1 qu.2 qu.3 t.c.2.0.2 t.c.2.2.4 gc t.c.3.0.2 t.c.3.2.4"
+HEAD_STEPS = "w.0.0.1.v w.0.1.2.s neg w.0.2.3.s w.0.3.4.v t.u.0.0.1 p.0.0.1 t.u.0.1.2 p.0.1.2 t.u.0.2.4.w p.0.2.4 w.1.0.2.s w.1.2.4.s t.u.1.0.2 p.1.0.2 t.u.1.2.4 p.1.2.4 H.0 H.1 w.2.0.4.s t.u.2.0.2.w p.2.0.2 t.u.2.2.4.w p.2.2.4 w.3.0.4.s t.c.0.0.2 t.c.0.2.4 t.u.3.0.2 p.3.0.2 t.u.3.2.4 p.3.2.4 w.4.0.4.s t.c.1.0.2 t.c.1.2.4 qv qp.0 qu.0 qu.1 qu.2 qu.3 t.c.2.0.2 t.c.2.2.4 gc t.c.3.0.2 t.c.3.2.4"
 US_SKIP = [14, 15]
 US_LOAD_BEATS = 3
-POOL_WIDENS = [2,4,8]
+POOL_WIDENS = []
 POOL_WIDEN_PASSES = 2
 V_EMPTIES = []
 LAST_EARLY = 1
@@ -43,8 +43,8 @@ START_BEAT = 2
 STAGE1_DONE = 0
 STAGE1_FROM = 4
 SCALAR_ORDERS = [12,14,15]
-POOL_ORDERS = [4,7,12,13,14]
-POOL_PASSES = 4
+POOL_ORDERS = [3,4,5,7,9,12,13,14]
+POOL_PASSES = 3
 POOL_WORDS = True
 Z_ENGINES = ("scalar","scalar")
 

@@ -19,34 +19,27 @@ ADD = mybir.AluOpType.add
 
 P = 128
 PASSES = 4
-TILES = 16
-BEATS = 16
+SPAN = 4 * P
+TILES = N // P
+BEATS = TILES
 HALF = BEATS // 2
-LOAD_BEATS = 2
-RAW_BUFS = 8
+HEAD_BEATS = 2
+US_AHEAD = 2
+LOAD_AHEAD = 2
+US_LOAD_AHEAD = 3
+STAGE1_LAG = 4
+STAGE2_BEAT = HALF + 2
+SORTED_PASSES = 3
+SCALAR_SORTS_FROM = STAGE2_BEAT + 1
+RAW_BUFS = 2 * (LOAD_AHEAD + 2)
+US_RAW_BUFS = 6
+WIDENED_BUFS = 4
 SLOTS = 4
+GROUPED_BUFS = 3
+CODE_BUFS = 4
 US_BANKS = 2
 WIDE_BANKS = 4
-HEAD = [("us",0,0,1),("us",0,1,2),"s",("us",0,2,4),("us",1),("us",2),"vc",("us",3),("coef",0),"vs",("us",4),("coef",1),("coef",2),"g",("coef",3),("coef",4),("us",5),("coef",5),("coef",6),("coef",7)]
-HEAD_STEPS = "w.0.0.1.v w.0.1.2.s neg w.0.2.3.s w.0.3.4.v t.u.0.0.1 p.0.0.1 t.u.0.1.2 p.0.1.2 t.u.0.2.4.w p.0.2.4 w.1.0.2.s w.1.2.4.s t.u.1.0.2 p.1.0.2 t.u.1.2.4 p.1.2.4 H.0 H.1 w.2.0.4.s t.u.2.0.2.w p.2.0.2 t.u.2.2.4.w p.2.2.4 w.3.0.4.s t.c.0.0.2 t.c.0.2.4 t.u.3.0.2 p.3.0.2 t.u.3.2.4 p.3.2.4 w.4.0.4.s t.c.1.0.2 t.c.1.2.4 qv qp.0 qu.0 qu.1 qu.2 qu.3 t.c.2.0.2 t.c.2.2.4 gc t.c.3.0.2 t.c.3.2.4"
-US_SKIP = [14, 15]
-US_LOAD_BEATS = 3
-POOL_WIDENS = []
-POOL_WIDEN_PASSES = 2
-V_EMPTIES = []
-LAST_EARLY = 1
-LAST_Z = "pool"
-POOL_PRODUCTS = []
-V_WIDEN = []
-V_ORDERS = []
-START_BEAT = 2
-STAGE1_DONE = 0
-STAGE1_FROM = 4
-SCALAR_ORDERS = [12,14,15]
-POOL_ORDERS = [3,4,5,7,9,12,13,14]
-POOL_PASSES = 3
-POOL_WORDS = True
-Z_ENGINES = ("scalar","scalar")
+SUM_BANKS = 2
 
 
 def tile_fourierftgivenbases_w_kernel(tc, w0, coef, g, uc, us_bytes, us_scale, vc, vs, out):
@@ -57,8 +50,8 @@ def tile_fourierftgivenbases_w_kernel(tc, w0, coef, g, uc, us_bytes, us_scale, v
         "uc": uc.rearrange("(g m t) k -> g t m k", m=P, t=4),
         "us": us_bytes.rearrange("(g m t) k -> g t m k", m=P, t=4),
     }
-    w0_v = w0.rearrange("(g m t) f -> m g t f", m=P, t=4)
-    out_v = out.rearrange("(g m t) f -> g m t f", m=P, t=4)
+    w0_rows = w0.rearrange("(g m t) f -> m g t f", m=P, t=4)
+    out_rows = out.rearrange("(g m t) f -> g m t f", m=P, t=4)
     wide = [("coef", i) for i in range(TILES)] + [("uc", i) for i in range(TILES)]
 
     with ExitStack() as ctx:
@@ -66,16 +59,11 @@ def tile_fourierftgivenbases_w_kernel(tc, w0, coef, g, uc, us_bytes, us_scale, v
         stage = ctx.enter_context(tc.tile_pool(name="stage", bufs=2))
         psum = ctx.enter_context(tc.psum_pool(name="psum", bufs=2))
 
+        scale_rows = keep.tile([P, SPAN], F32, name="scale_rows", align_bytes=64)
+        gain_rows = keep.tile([P, SPAN], BF16, name="gain_rows", align_bytes=64)
         ident = keep.tile([P, P], F32, name="ident")
-        make_identity(nc, ident[:])
-
-        ones = keep.tile([P, 1], F32, name="ones")
-        if V_WIDEN:
-            nc.gpsimd.memset(ones[:], 1.0)
-        gain_raw = keep.tile([P, 4, 4], BF16, name="gain_raw")
-        gain_col = keep.tile([P, TILES], F32, name="gain_col")
-        scale_raw = keep.tile([P, PASSES, 4], F32, name="scale_raw")
         neg_scale = keep.tile([P, PASSES, 4], F32, name="neg_scale")
+        gain_col = keep.tile([P, TILES], F32, name="gain_col")
         v_raw = keep.tile([P, 2, N], BF16, name="v_raw", align_bytes=64)
         v_grouped = keep.tile([P, PASSES, 2, F, 4], BF16, name="v_grouped", align_bytes=64)
         v_codes = keep.tile([P, PASSES, 2 * F], U32, name="v_codes", align_bytes=64)
@@ -87,10 +75,7 @@ def tile_fourierftgivenbases_w_kernel(tc, w0, coef, g, uc, us_bytes, us_scale, v
 
         raw = {}
         widened = {}
-        ordered = {}
-        words_of = {}
-        plain = {}
-        last_pass = {}
+        sorted_words = {}
         grouped = {}
         turned = {}
         codes = {}
@@ -100,130 +85,105 @@ def tile_fourierftgivenbases_w_kernel(tc, w0, coef, g, uc, us_bytes, us_scale, v
         z_grouped = {}
         results = {}
 
-        def raw_tile(key):
-            if key[0] == "us":
-                raw[key] = stage.tile([P, N], U8, name="us_raw", bufs=6, align_bytes=64)
-            else:
+        def load(key, first=0, end=PASSES):
+            kind, i = key
+            if first == 0 and kind == "us":
+                raw[key] = stage.tile([P, N], U8, name="us_raw", bufs=US_RAW_BUFS, align_bytes=64)
+            elif first == 0:
                 raw[key] = stage.tile([P, N], BF16, name="raw", bufs=RAW_BUFS, align_bytes=64)
-
-        def load(key):
-            kind, i = key
-            raw_tile(key)
-            nc.sync.dma_start(out=raw[key][:], in_=rows[kind][i // 4, i % 4])
-
-        def load_part(key, first, end):
-            kind, i = key
-            if first == 0:
-                raw_tile(key)
-            cols = slice(first * 512, end * 512)
+            cols = slice(first * SPAN, end * SPAN)
             nc.sync.dma_start(out=raw[key][:, cols], in_=rows[kind][i // 4, i % 4][:, cols])
 
         def load_v(which):
             nc.sync.dma_start(
-                out=v_raw[:, which, :].rearrange("p (c j f) -> p c j f", c=PASSES, j=4),
-                in_=(vc, vs)[which].rearrange("(c p j) f -> p c j f", p=P, j=4),
+                out=v_raw[:, which, :].rearrange("p (c t f) -> p c t f", c=PASSES, t=4),
+                in_=(vc, vs)[which].rearrange("(c p t) f -> p c t f", p=P, t=4),
             )
 
-        def pool_copy(dst, src):
+        def load_rows(tile, vector):
+            nc.sync.dma_start(out=tile[0:PASSES, :], in_=vector)
+
+        def turn_scale():
+            bank = psum.tile([P, 4, P], F32, name="sums", bufs=SUM_BANKS)
+            for t in range(4):
+                nc.tensor.transpose(bank[:, t, :], scale_rows[:, t:SPAN:4], ident[:])
+            return bank
+
+        def negate_scale(bank):
+            nc.scalar.activation(
+                out=neg_scale[:], in_=bank[:, :, 0:PASSES].rearrange("p t c -> p c t"), func=COPY, scale=-1.0
+            )
+
+        def turn_gain():
+            bank = psum.tile([P, 2, P], F32, name="sums", bufs=SUM_BANKS)
+            for u in range(2):
+                nc.tensor.transpose(bank[:, u, :], gain_rows[:].bitcast(F32)[:, u : 2 * P : 2], ident[:])
+            values = bank[:].rearrange("p u c -> p (u c)").bitcast(BF16).rearrange("p (u c e) -> p c u e", u=2, e=2)
+            nc.scalar.copy(out=gain_col[:].rearrange("p (c u e) -> p c u e", u=2, e=2), in_=values[:, 0:PASSES])
+
+        def pool_group(dst, src):
             nc.gpsimd.tensor_scalar(out=dst, in0=src, scalar1=1.0, scalar2=0.0, op0=MULT, op1=ADD)
 
-        def pool_group_v(which):
-            pool_copy(
-                v_grouped[:, :, which],
-                v_raw[:, which, :].rearrange("p (c j f) -> p c f j", c=PASSES, j=4),
-            )
+        def group_v(which):
+            pool_group(v_grouped[:, :, which], v_raw[:, which, :].rearrange("p (c t f) -> p c f t", c=PASSES, t=4))
 
         def quantize_v():
             nc.vector.quantize_mx(
                 out=v_codes[:].rearrange("p c f -> p (c f)").bitcast(FP8X4),
                 scales=v_scales[:].rearrange("p c f -> p (c f)"),
-                in_=v_grouped[:].rearrange("p c w f j -> p (c w f j)"),
+                in_=v_grouped[:].rearrange("p c w f t -> p (c w f t)"),
             )
 
-        def widen(i, first, end, engine, tile=None):
-            if tile is None and i not in widened:
-                widened[i] = stage.tile([P, N], BF16, name="widened", bufs=4, align_bytes=64)
-            tile = widened[i] if tile is None else tile
-            for c in range(first, end):
-                words_of[(i, c)] = tile
-            cols = slice(first * 512, end * 512)
-            src = raw[("us", i)][:, cols].bitcast(FP8)
-            if engine == "scalar":
-                nc.scalar.copy(out=tile[:, cols], in_=src)
-            elif engine == "pool":
-                nc.gpsimd.tensor_copy(out=tile[:, cols], in_=src)
-            else:
-                nc.vector.tensor_copy(out=tile[:, cols], in_=src)
+        def widen(i, first=0, end=PASSES, copy=nc.scalar.copy):
+            if first == 0:
+                widened[i] = stage.tile([P, N], BF16, name="widened", bufs=WIDENED_BUFS, align_bytes=64)
+            cols = slice(first * SPAN, end * SPAN)
+            copy(out=widened[i][:, cols], in_=raw[("us", i)][:, cols].bitcast(FP8))
 
-        def widen_ordered(i):
-            tile = stage.tile([P, N], BF16, name="widened", bufs=4, align_bytes=64)
-            nc.vector.tensor_scalar(
-                out=tile[:].rearrange("p (u n e) -> p n u e", u=2, e=2),
-                in0=raw[("us", i)][:].bitcast(FP8).rearrange("p (n u e) -> p n u e", u=2, e=2),
-                scalar1=ones[:],
-                scalar2=None,
-                op0=MULT,
-            )
-            ordered[("us", i)] = (tile, PASSES)
-
-        def scalar_order(key):
-            tile = stage.tile([P, N], BF16, name="ordered", bufs=2, align_bytes=64)
+        def scalar_sort(key):
+            tile = stage.tile([P, N], BF16, name="sorted", bufs=2, align_bytes=64)
             nc.scalar.copy(
                 out=tile[:].bitcast(F32).rearrange("p (u n i) -> p n u i", u=2, i=4),
                 in_=raw[key][:].bitcast(F32).rearrange("p (n i u) -> p n u i", u=2, i=4),
             )
-            ordered[key] = (tile, PASSES)
+            sorted_words[key] = (tile, PASSES)
 
-        def vector_order(key):
-            tile = stage.tile([P, N], BF16, name="ordered", bufs=2, align_bytes=64)
-            nc.vector.tensor_copy(
-                out=tile[:].bitcast(F32).rearrange("p (u n i) -> p n u i", u=2, i=4),
-                in_=raw[key][:].bitcast(F32).rearrange("p (n i u) -> p n u i", u=2, i=4),
+        def pool_sort(key, tile):
+            width = SORTED_PASSES * SPAN
+            nc.gpsimd.tensor_copy(
+                out=tile[:, 0:width].bitcast(F32).rearrange("p (u n) -> p u n", u=2),
+                in_=raw[key][:, 0:width].bitcast(F32).rearrange("p (n u) -> p u n", u=2),
             )
-            ordered[key] = (tile, PASSES)
+            sorted_words[key] = (tile, SORTED_PASSES)
 
-        def pool_order(key, tile):
-            width = POOL_PASSES * 512
-            if POOL_WORDS:
-                nc.gpsimd.tensor_copy(
-                    out=tile[:, 0:width].bitcast(F32).rearrange("p (u n) -> p u n", u=2),
-                    in_=raw[key][:, 0:width].bitcast(F32).rearrange("p (n u) -> p u n", u=2),
-                )
-            else:
-                pool_copy(
-                    tile[:, 0:width].rearrange("p (u n e) -> p u n e", u=2, e=2),
-                    raw[key][:, 0:width].rearrange("p (n u e) -> p u n e", u=2, e=2),
-                )
-            ordered[key] = (tile, POOL_PASSES)
-
-        def turn(key, first, end, tag=None):
+        def turn(key, first, end, wide_bank=False):
             kind, i = key
-            if kind == "us" and tag is None:
+            if kind == "us" and not wide_bank:
                 bank = psum.tile([P, 2, 2, P], F32, name="us_bank", bufs=US_BANKS)
             else:
                 bank = psum.tile([P, 2, 2, P], F32, name="wide_bank", bufs=WIDE_BANKS)
-            tile, count = ordered.get(key, (None, 0))
+            words = (widened[i] if kind == "us" else raw[key])[:].bitcast(F32)
+            tile, count = sorted_words.get(key, (None, 0))
             for c in range(first, end):
                 for u in range(2):
                     if c < count:
                         start = P * (count * u + c)
                         src = tile[:].bitcast(F32)[:, start : start + P]
                     else:
-                        words = (words_of[(i, c)] if kind == "us" else raw[key])[:].bitcast(F32)
-                        src = words[:, 256 * c + u : 256 * (c + 1) : 2]
+                        src = words[:, 2 * P * c + u : 2 * P * (c + 1) : 2]
                     nc.tensor.transpose(bank[:, u, c - first, :], src, ident[:])
             turned[(key, first)] = bank
 
-        def empty(key, h, engine="scalar"):
+        def turn_wide(key, h):
             kind, i = key
+            turn(key, 2 * h, 2 * h + 2)
             if h == 0 and i % 2 == 0:
-                both = stage.tile([P, 2, N], BF16, name="grouped", bufs=3, align_bytes=64)
+                both = stage.tile([P, 2, N], BF16, name="grouped", bufs=GROUPED_BUFS, align_bytes=64)
                 grouped[(kind, i)] = both[:, 0, :]
                 grouped[(kind, i + 1)] = both[:, 1, :]
                 grouped[(kind, "pair", i // 2)] = both[:].rearrange("p j n -> p (j n)")
-            dst = grouped[key].bitcast(F32)[:, 512 * h : 512 * (h + 1)]
-            copy = nc.scalar.copy if engine == "scalar" else nc.vector.tensor_copy
-            copy(
+            dst = grouped[key].bitcast(F32)[:, SPAN * h : SPAN * (h + 1)]
+            nc.scalar.copy(
                 out=dst.rearrange("p (n i u) -> p n u i", u=2, i=4),
                 in_=turned[(key, 2 * h)][:].rearrange("p u c (n i) -> p (c n) u i", i=4),
             )
@@ -231,39 +191,27 @@ def tile_fourierftgivenbases_w_kernel(tc, w0, coef, g, uc, us_bytes, us_scale, v
         def product(i, first, end):
             count = end - first
             grouped[("us", i)] = slots[i % SLOTS][:]
+            dst = grouped[("us", i)][:, SPAN * first : SPAN * end]
             values = turned[(("us", i), first)][:].rearrange("p u c m -> p (u c m)").bitcast(BF16)
             factors = neg_scale[:, first:end, :].rearrange("p c (o u e) -> p c o u e", o=1, u=2)
             nc.vector.tensor_tensor(
-                out=grouped[("us", i)][:, 512 * first : 512 * end].rearrange("p (c m u e) -> p c m u e", c=count, u=2, e=2),
+                out=dst.rearrange("p (c m u e) -> p c m u e", c=count, u=2, e=2),
                 in0=values.rearrange("p (u c m e) -> p c m u e", u=2, c=2, e=2)[:, 0:count],
                 in1=factors.to_broadcast([P, count, P, 2, 2]),
                 op=MULT,
             )
 
-        def empty_last_pass(i):
-            plain[i] = stage.tile([P, 512], BF16, name="plain", bufs=2, align_bytes=64)
-            nc.scalar.copy(
-                out=plain[i][:].bitcast(F32).rearrange("p (n i u) -> p n u i", u=2, i=4),
-                in_=turned[(("us", i), 3)][:, :, 0, :].rearrange("p u (n i) -> p n u i", i=4),
-            )
-
-        def pool_product(i, tile):
-            factors = neg_scale[:, 3:4, :].to_broadcast([P, P, 4])
-            nc.gpsimd.tensor_tensor(
-                out=tile[:, 0:512].rearrange("p (m t) -> p m t", t=4),
-                in0=plain[i][:].rearrange("p (m t) -> p m t", t=4),
-                in1=factors,
-                op=MULT,
-            )
-            last_pass[i] = tile[:, 0:512]
+        def turn_us(i, first, end, wide_bank=False):
+            turn(("us", i), first, end, wide_bank)
+            product(i, first, end)
 
         def code_tiles(kind, first, count):
-            depth = TILES if kind == "us" else 4
-            ct = stage.tile([P, count * PASSES * P], U32, name=kind + "_codes", bufs=depth, align_bytes=64)
-            st = stage.tile([P, count * PASSES * P], U8, name=kind + "_scales", bufs=depth, align_bytes=64)
+            depth = TILES if kind == "us" else CODE_BUFS
+            ct = stage.tile([P, count * SPAN], U32, name=kind + "_codes", bufs=depth, align_bytes=64)
+            st = stage.tile([P, count * SPAN], U8, name=kind + "_scales", bufs=depth, align_bytes=64)
             for j in range(count):
-                codes[(kind, first + j)] = ct[:, j * PASSES * P : (j + 1) * PASSES * P]
-                scales[(kind, first + j)] = st[:, j * PASSES * P : (j + 1) * PASSES * P]
+                codes[(kind, first + j)] = ct[:, j * SPAN : (j + 1) * SPAN]
+                scales[(kind, first + j)] = st[:, j * SPAN : (j + 1) * SPAN]
             return ct, st
 
         def quantize_pair(beat):
@@ -271,25 +219,20 @@ def tile_fourierftgivenbases_w_kernel(tc, w0, coef, g, uc, us_bytes, us_scale, v
             ct, st = code_tiles(kind, i, 2)
             nc.vector.quantize_mx(out=ct[:].bitcast(FP8X4), scales=st[:], in_=grouped[(kind, "pair", i // 2)])
 
-        def quantize_part(key, first, count):
+        def quantize_part(key, first, end):
             nc.vector.quantize_mx(
-                out=codes[key][:, first * P : (first + count) * P].bitcast(FP8X4),
-                scales=scales[key][:, first * P : (first + count) * P],
-                in_=grouped[key][:, 4 * first * P : 4 * (first + count) * P],
+                out=codes[key][:, first * P : end * P].bitcast(FP8X4),
+                scales=scales[key][:, first * P : end * P],
+                in_=grouped[key][:, first * SPAN : end * SPAN],
             )
 
         def quantize_us(i):
-            key = ("us", i)
             code_tiles("us", i, 1)
-            if i in last_pass:
-                nc.vector.quantize_mx(
-                    out=codes[key][:, 3 * P :].bitcast(FP8X4), scales=scales[key][:, 3 * P :], in_=last_pass[i]
-                )
-            quantize_part(key, 0, 3 if i in last_pass else PASSES)
+            quantize_part(("us", i), 0, PASSES)
 
-        def mm(o, key, c, moving, moving_scales, start, stop):
+        def mm(dst, key, c, moving, moving_scales, start, stop):
             nc.tensor.matmul_mx(
-                out=o,
+                out=dst,
                 lhsT=codes[key][:, c * P : (c + 1) * P].bitcast(FP8X4),
                 lhsT_scale=scales[key][:, c * P : (c + 1) * P],
                 rhs=moving.bitcast(FP8X4),
@@ -299,7 +242,7 @@ def tile_fourierftgivenbases_w_kernel(tc, w0, coef, g, uc, us_bytes, us_scale, v
             )
 
         def stage1(i):
-            sums[("r", i)] = psum.tile([P, 2 * F], F32, name="sums", bufs=2)
+            sums[("r", i)] = psum.tile([P, 2 * F], F32, name="sums", bufs=SUM_BANKS)
             for c in range(PASSES):
                 mm(sums[("r", i)][:], ("coef", i), c, v_codes[:, c, :], v_scales[:, c, :], c == 0, c == PASSES - 1)
 
@@ -310,59 +253,32 @@ def tile_fourierftgivenbases_w_kernel(tc, w0, coef, g, uc, us_bytes, us_scale, v
                 out=z_flat[i // 4][:, i % 4, :], in_=sums[("r", i)][:], func=COPY, scale=gain_col[:, i : i + 1]
             )
 
-        def group_z(c, half):
-            if c not in z_grouped:
-                z_grouped[c] = stage.tile([P, 2 * F, 4], BF16, name="z_grouped", bufs=2, align_bytes=64)
-            cols = slice(half * F, (half + 1) * F)
-            src = z_flat[c][:, :, cols].rearrange("p t (n i) -> p n t i", i=4)
-            dst = z_grouped[c][:, cols, :].rearrange("p (n i) t -> p n t i", i=4)
-            if Z_ENGINES[half] == "vector":
-                nc.vector.tensor_copy(out=dst, in_=src)
-            else:
-                nc.scalar.copy(out=dst, in_=src)
-
-        def pool_group_z(c, tile):
+        def group_z(c, tile):
             z_grouped[c] = tile[:, 0 : 8 * F].rearrange("p (f t) -> p f t", t=4)
-            pool_copy(z_grouped[c], z_flat[c][:].rearrange("p t f -> p f t"))
+            pool_group(z_grouped[c], z_flat[c][:].rearrange("p t f -> p f t"))
 
         def quantize_z(c):
             nc.vector.quantize_mx(
                 out=z_codes[:, c, :].bitcast(FP8X4),
                 scales=z_scales[:, c, :],
-                in_=z_grouped[c][:].rearrange("p f t -> p (f t)"),
+                in_=z_grouped[c].rearrange("p f t -> p (f t)"),
             )
 
-        def open_sums(tiles, tag, depth):
-            bank = psum.tile([P, 2, F], F32, name=tag, bufs=depth)
-            sums[("out", tiles)] = bank
-            for j, i in enumerate(tiles):
-                sums[("out", i)] = bank[:, j, :]
-
-        def stage2(i, parts, start, stop):
-            for n, (kind, c) in enumerate(parts):
-                half = slice(F, 2 * F) if kind == "us" else slice(0, F)
-                mm(
-                    sums[("out", i)],
-                    (kind, i),
-                    c,
-                    z_codes[:, c, half],
-                    z_scales[:, c, half],
-                    start and n == 0,
-                    stop and n == len(parts) - 1,
-                )
-
-        def stage2_pair(pair, parts, start, stop):
+        def stage2(tiles, parts, start, stop, tag="sums", depth=SUM_BANKS):
             if start:
-                open_sums((2 * pair, 2 * pair + 1), "sums", 2)
-            stage2(2 * pair, parts, start, False)
-            stage2(2 * pair + 1, parts, False, stop)
+                sums[tiles] = psum.tile([P, 2, F], F32, name=tag, bufs=depth)
+            steps = [(j, i, kind, c) for j, i in enumerate(tiles) for kind, c in parts]
+            for n, (j, i, kind, c) in enumerate(steps):
+                half = slice(F, 2 * F) if kind == "us" else slice(0, F)
+                first, final = start and n == 0, stop and n == len(steps) - 1
+                mm(sums[tiles][:, j, :], (kind, i), c, z_codes[:, c, half], z_scales[:, c, half], first, final)
 
         def epilogue(tiles):
             i, count = tiles[0], len(tiles)
             results[tiles] = stage.tile([P, count, F], F32, name="result", bufs=4)
             nc.vector.scalar_tensor_tensor(
                 out=results[tiles][:],
-                in0=sums[("out", tiles)][:, 0:count, :],
+                in0=sums[tiles][:, 0:count, :],
                 scalar=0.5,
                 in1=w0_sb[:, i // 4, i % 4 : i % 4 + count, :],
                 op0=MULT,
@@ -371,196 +287,166 @@ def tile_fourierftgivenbases_w_kernel(tc, w0, coef, g, uc, us_bytes, us_scale, v
 
         def store(tiles):
             i, count = tiles[0], len(tiles)
-            nc.sync.dma_start(out=out_v[i // 4, :, i % 4 : i % 4 + count, :], in_=results[tiles][:])
+            nc.sync.dma_start(out=out_rows[i // 4, :, i % 4 : i % 4 + count, :], in_=results[tiles][:])
 
-        def parts(kinds, passes):
-            return [(kind, c) for kind in kinds for c in passes]
+        def pair(j):
+            return (2 * j, 2 * j + 1)
 
-        every = range(PASSES)
-        early = range(PASSES - 1)
-        last = [PASSES - 1]
-        stage1_at = {i: max(i + 4, STAGE1_FROM + i // 2) for i in range(STAGE1_DONE, TILES)}
-        stage1_at[TILES - 1] -= LAST_EARLY
-        y, z = TILES - 2, TILES - 1
+        def passes(kind, first=0, end=PASSES):
+            return [(kind, c) for c in range(first, end)]
+
+        stage1_at = [min(i, TILES - 2) + STAGE1_LAG for i in range(TILES)]
+        first_pair = {
+            2 * STAGE2_BEAT - 1: passes("us", 0, 2),
+            2 * STAGE2_BEAT: passes("us", 2, 3) + passes("uc", 0, 1),
+            2 * STAGE2_BEAT + 1: passes("uc", 1, 3),
+            2 * STAGE2_BEAT + 2: passes("us", 3, 4) + passes("uc", 3, 4),
+        }
 
         def burst(j):
-            for i in stage1_at:
-                if stage1_at[i] == j:
-                    stage1(i)
-                    if stage1_at.get(i + 1) == j:
-                        gain(i)
+            due = [i for i in range(TILES) if stage1_at[i] == j]
+            for i in due:
+                stage1(i)
+                if i != due[-1]:
+                    gain(i)
+            if j in first_pair:
+                stage2(pair(0), first_pair[j], j == min(first_pair), j == max(first_pair))
             beat, second = divmod(j, 2)
-            pair = beat - HALF - 2
-            if (pair, second) == (-1, 1) and LAST_EARLY:
-                stage2_pair(0, parts(("us",), early[:2]), True, False)
-            elif pair == 0 and LAST_EARLY:
-                stage2_pair(0, (parts(("us",), early[2:]) + parts(("uc",), early[:1]), parts(("uc",), early[1:]))[second], False, False)
-            elif pair == 0:
-                stage2_pair(0, parts((("us", "uc")[second],), early), second == 0, False)
-            elif pair > 0:
-                if (pair, second) == (1, 0):
-                    stage2_pair(0, parts(("us", "uc"), last), False, True)
-                stage2_pair(pair, parts((("us", "uc")[second],), every), second == 0, second == 1)
+            if beat > STAGE2_BEAT:
+                stage2(pair(beat - STAGE2_BEAT), passes(("us", "uc")[second]), not second, bool(second))
 
-        def gains_after(j):
-            done = [i for i in stage1_at if stage1_at[i] == j]
-            if done:
-                gain(done[-1])
-            return [i // 4 for i in done if i % 4 == 3]
+        def gain_after(j):
+            due = [i for i in range(TILES) if stage1_at[i] == j][-1:]
+            for i in due:
+                gain(i)
+            return [i // 4 for i in due if i % 4 == 3]
 
-        def z_halves(ready, engine):
-            for c in ready:
-                for half in range(2):
-                    if Z_ENGINES[half] == engine:
-                        group_z(c, half)
+        def head():
+            nc.gpsimd.memset(scale_rows[:], 0.0)
+            nc.vector.memset(gain_rows[:], 0.0)
+            make_identity(nc, ident[:])
+            load(("us", 0), 0, 1)
+            load(("us", 0), 1, 2)
+            load_rows(scale_rows, us_scale.rearrange("o (c k) -> (o c) k", c=PASSES))
+            load(("us", 0), 2, 4)
+            load(("us", 1))
+            load(("us", 2))
+            load_v(0)
+            load(("us", 3))
+            load_rows(gain_rows, g.rearrange("(c k) -> c k", c=PASSES))
+            load(("coef", 0))
+            load_v(1)
+            load(("us", 4))
+            for i in range(1, 5):
+                load(("coef", i))
+            load(("us", 5))
+            for i in range(5, RAW_BUFS):
+                load(("coef", i))
 
-        def pair_tiles(pair):
-            return (2 * pair, 2 * pair + 1)
+            scale_bank = turn_scale()
+            for c in range(PASSES):
+                widen(0, c, c + 1, nc.vector.tensor_copy if c in (0, PASSES - 1) else nc.scalar.copy)
+            negate_scale(scale_bank)
+            turn_us(0, 0, 1)
+            turn_us(0, 1, 2)
+            turn_us(0, 2, 4, wide_bank=True)
+            for h in range(2):
+                widen(1, 2 * h, 2 * h + 2)
+            for h in range(2):
+                turn_us(1, 2 * h, 2 * h + 2)
+            group_v(0)
+            group_v(1)
+            widen(2)
+            for h in range(2):
+                turn_us(2, 2 * h, 2 * h + 2, wide_bank=True)
+            widen(3)
+            for h in range(2):
+                turn_wide(("coef", 0), h)
+            turn_gain()
+            for h in range(2):
+                turn_us(3, 2 * h, 2 * h + 2)
+            widen(4)
+            for h in range(2):
+                turn_wide(("coef", 1), h)
+            quantize_v()
+            quantize_pair(0)
+            for i in range(4):
+                quantize_us(i)
+            for i in (2, 3):
+                for h in range(2):
+                    turn_wide(("coef", i), h)
 
-        with tc.manual_schedule():
-            for key in HEAD:
-                if key == "s":
-                    nc.sync.dma_start(out=scale_raw[:], in_=us_scale.rearrange("o (c p t) -> p (o c) t", p=P, t=4))
-                elif key == "g":
-                    nc.sync.dma_start(out=gain_raw[:], in_=g.rearrange("(c p t) -> p c t", p=P, t=4))
-                elif key in ("vc", "vs"):
-                    load_v(("vc", "vs").index(key))
-                elif len(key) == 4:
-                    load_part(key[:2], key[2], key[3])
-                else:
-                    load(key)
-
-            names = {"u": "us", "c": "coef"}
-            engines = {"s": "scalar", "v": "vector", "g": "pool"}
-            for word in HEAD_STEPS.split():
-                step = word.split(".")
-                if step[0] == "t":
-                    key, first, end = (names[step[1]], int(step[2])), int(step[3]), int(step[4])
-                    turn(key, first, end, step[5] if len(step) > 5 else None)
-                    if key[0] == "coef":
-                        empty(key, first // 2)
-                elif step[0] == "p":
-                    product(int(step[1]), int(step[2]), int(step[3]))
-                elif step[0] == "w":
-                    widen(int(step[1]), int(step[2]), int(step[3]), engines[step[4]])
-                elif step[0] == "H":
-                    pool_group_v(int(step[1]))
-                elif step[0] == "qv":
-                    quantize_v()
-                elif step[0] == "qu":
-                    quantize_us(int(step[1]))
-                elif step[0] == "qp":
-                    quantize_pair(int(step[1]))
-                elif step[0] == "m":
-                    stage1(int(step[1]))
-                elif step[0] == "a":
-                    gain(int(step[1]))
-                elif step[0] == "l":
-                    load((names[step[1]], int(step[2])))
-                elif step[0] == "gc":
-                    nc.scalar.copy(out=gain_col[:], in_=gain_raw[:].rearrange("p c t -> p (c t)"))
-                elif step[0] == "neg":
-                    nc.vector.tensor_scalar(out=neg_scale[:], in0=scale_raw[:], scalar1=-1.0, scalar2=None, op0=MULT)
-
-            us_beats = [n for n in range(START_BEAT, BEATS) if n not in US_SKIP]
-            us_of = {n: TILES - len(us_beats) + j for j, n in enumerate(us_beats)}
-            newest = TILES - len(us_beats) - 1
+        def beats():
+            gained = []
             waiting = []
-            late = []
-            for n in range(START_BEAT, BEATS):
-                a, b = wide[2 * n], wide[2 * n + 1]
-                u = us_of.get(n)
-                following = us_of.get(min([m for m in us_beats if m > n], default=None))
-                ahead = n + LOAD_BEATS
-                for m in us_beats:
-                    if max(m - US_LOAD_BEATS, START_BEAT) == n and ("us", us_of[m]) not in HEAD:
-                        load(("us", us_of[m]))
-                if ahead < BEATS:
-                    for key in (wide[2 * ahead], wide[2 * ahead + 1]):
-                        if key not in HEAD:
-                            load(key)
+            for n in range(HEAD_BEATS, BEATS):
+                early, late = wide[2 * n], wide[2 * n + 1]
+                u = n + US_AHEAD
+                for i in range(TILES):
+                    if max(i - US_AHEAD - US_LOAD_AHEAD, HEAD_BEATS) == n and ("us", i) not in raw:
+                        load(("us", i))
+                for key in wide[2 * (n + LOAD_AHEAD) : 2 * (n + LOAD_AHEAD + 1)]:
+                    load(key)
                 if n == HALF - 1:
-                    nc.sync.dma_start(out=w0_sb[:], in_=w0_v)
-                if n >= HALF + 5:
-                    for pair in (0, 1) if n == HALF + 5 else (n - HALF - 4,):
-                        store(pair_tiles(pair))
+                    nc.sync.dma_start(out=w0_sb[:], in_=w0_rows)
+                if n == STAGE2_BEAT + 3:
+                    store(pair(0))
+                if n >= STAGE2_BEAT + 3:
+                    store(pair(n - STAGE2_BEAT - 2))
 
-                if u is not None:
+                if u < TILES:
                     turn(("us", u), 0, 2)
-                gained = late + gains_after(2 * n - 1)
-                z_ready = waiting + [c for c in gained if c == PASSES - 1]
+                gained = gained + gain_after(2 * n - 1)
+                z_due = waiting + [c for c in gained if c == PASSES - 1]
                 waiting = [c for c in gained if c < PASSES - 1]
-                if LAST_Z == "scalar" and PASSES - 1 in z_ready:
-                    for half in range(2):
-                        group_z(PASSES - 1, half)
-                by_pool = 0
-                if u is not None:
-                    free = slots[newest % SLOTS]
-                    if z_ready and z_ready[0] not in z_grouped:
-                        pool_group_z(z_ready[0], free)
-                    elif n in POOL_PRODUCTS:
-                        pool_product(u, free)
-                    elif n in POOL_WIDENS:
-                        by_pool = POOL_WIDEN_PASSES
-                        widen(following, 0, by_pool, "pool", free)
-                    elif n + 1 in POOL_ORDERS:
-                        pool_order(wide[2 * (n + 1)], free)
-                if n >= HALF + 4:
-                    epilogue(pair_tiles(n - HALF - 3))
-                if n - 1 in V_EMPTIES:
-                    empty(wide[2 * n - 1], 1, "vector")
-                if u is not None:
+                if u < TILES:
+                    just_read = slots[(u - 1) % SLOTS]
+                    if z_due:
+                        group_z(z_due[0], just_read)
+                    else:
+                        pool_sort(wide[2 * (n + 1)], just_read)
+                if n >= STAGE2_BEAT + 2:
+                    epilogue(pair(n - STAGE2_BEAT - 1))
+                if u < TILES:
                     product(u, 0, 2)
-                    turn(("us", u), 2, 3 if n in POOL_PRODUCTS else 4)
-                    product(u, 2, 3 if n in POOL_PRODUCTS else 4)
-                else:
-                    z_halves(z_ready, "vector")
-                if n + 1 in POOL_PRODUCTS:
-                    turn(("us", following), 3, 4, "wide")
-                    empty_last_pass(following)
-                if following is not None and following not in V_WIDEN:
-                    widen(following, by_pool, 3 if n + 1 in POOL_PRODUCTS else 4, "scalar")
-                if n + 2 in POOL_PRODUCTS:
-                    widen(us_of[n + 2], 3, 4, "scalar")
-                turn(a, 0, 2)
-                empty(a, 0)
+                    turn_us(u, 2, 4)
+                if u + 1 < TILES:
+                    widen(u + 1)
+                turn_wide(early, 0)
                 burst(2 * n)
-                if n == HALF + 3:
-                    epilogue(pair_tiles(0))
+                if n == STAGE2_BEAT + 1:
+                    epilogue(pair(0))
                 quantize_pair(n - 1)
-                if following in V_WIDEN and u is not None:
-                    widen_ordered(following)
-                if n + 1 in V_ORDERS:
-                    vector_order(wide[2 * (n + 1) + 1])
-                for c in z_ready:
+                for c in z_due:
                     quantize_z(c)
-                if u is not None:
+                if u < TILES:
                     quantize_us(u)
-                    newest = u
-                late = gains_after(2 * n)
-                if n + 1 in SCALAR_ORDERS:
-                    scalar_order(wide[2 * (n + 1) + 1])
-                turn(a, 2, 4)
-                empty(a, 1)
-                turn(b, 0, 2)
-                empty(b, 0)
-                turn(b, 2, 4)
-                if n not in V_EMPTIES:
-                    empty(b, 1)
+                gained = gain_after(2 * n)
+                if SCALAR_SORTS_FROM <= n < BEATS - 1:
+                    scalar_sort(wide[2 * (n + 1) + 1])
+                turn_wide(early, 1)
+                turn_wide(late, 0)
+                turn_wide(late, 1)
                 burst(2 * n + 1)
 
-            store(pair_tiles(HALF - 4))
-            code_tiles("uc", y, 2)
-            quantize_part(("uc", y), 0, PASSES)
-            epilogue(pair_tiles(HALF - 3))
-            store(pair_tiles(HALF - 3))
-            quantize_part(("uc", z), 0, 2)
-            quantize_part(("uc", z), 2, 2)
-            stage2_pair(HALF - 2, parts(("us", "uc"), every), True, True)
-            open_sums((y,), "us_bank", US_BANKS)
-            stage2(y, parts(("us", "uc"), every), True, True)
-            open_sums((z,), "us_bank", US_BANKS)
-            stage2(z, parts(("us", "uc"), every), True, True)
-            for tiles in (pair_tiles(HALF - 2), (y,), (z,)):
+        def tail():
+            before_last, last = TILES - 2, TILES - 1
+            store(pair(HALF - 4))
+            code_tiles("uc", before_last, 2)
+            quantize_part(("uc", before_last), 0, PASSES)
+            epilogue(pair(HALF - 3))
+            store(pair(HALF - 3))
+            quantize_part(("uc", last), 0, 2)
+            quantize_part(("uc", last), 2, PASSES)
+            both = passes("us") + passes("uc")
+            stage2(pair(HALF - 2), both, True, True)
+            for i in (before_last, last):
+                stage2((i,), both, True, True, "us_bank", US_BANKS)
+            for tiles in (pair(HALF - 2), (before_last,), (last,)):
                 epilogue(tiles)
                 store(tiles)
+
+        with tc.manual_schedule():
+            head()
+            beats()
+            tail()

@@ -31,8 +31,9 @@ STAGE1_LAG = 4
 STAGE2_BEAT = HALF + 2
 SORTED_PASSES = 3
 SCALAR_SORTS_FROM = STAGE2_BEAT + 1
+POOL_PRODUCTS = range(HEAD_BEATS, HALF + 1, 2)
 RAW_BUFS = 2 * (LOAD_AHEAD + 2)
-US_RAW_BUFS = 6
+US_RAW_BUFS = 7
 WIDENED_BUFS = 4
 SLOTS = 4
 GROUPED_BUFS = 3
@@ -59,10 +60,9 @@ def tile_fourierftgivenbases_w_kernel(tc, w0, coef, g, uc, us_bytes, us_scale, v
         stage = ctx.enter_context(tc.tile_pool(name="stage", bufs=2))
         psum = ctx.enter_context(tc.psum_pool(name="psum", bufs=2))
 
-        scale_rows = keep.tile([P, SPAN], F32, name="scale_rows", align_bytes=64)
-        gain_rows = keep.tile([P, SPAN], BF16, name="gain_rows", align_bytes=64)
         ident = keep.tile([P, P], F32, name="ident")
-        neg_scale = keep.tile([P, PASSES, 4], F32, name="neg_scale")
+        scale_col = keep.tile([P, PASSES, 4], F32, name="scale_col")
+        gain_raw = keep.tile([P, PASSES, 4], BF16, name="gain_raw")
         gain_col = keep.tile([P, TILES], F32, name="gain_col")
         v_raw = keep.tile([P, 2, N], BF16, name="v_raw", align_bytes=64)
         v_grouped = keep.tile([P, PASSES, 2, F, 4], BF16, name="v_grouped", align_bytes=64)
@@ -77,6 +77,8 @@ def tile_fourierftgivenbases_w_kernel(tc, w0, coef, g, uc, us_bytes, us_scale, v
         widened = {}
         sorted_words = {}
         grouped = {}
+        plain = {}
+        last_pass = {}
         turned = {}
         codes = {}
         scales = {}
@@ -100,32 +102,12 @@ def tile_fourierftgivenbases_w_kernel(tc, w0, coef, g, uc, us_bytes, us_scale, v
                 in_=(vc, vs)[which].rearrange("(c p t) f -> p c t f", p=P, t=4),
             )
 
-        def load_rows(tile, vector):
-            nc.sync.dma_start(out=tile[0:PASSES, :], in_=vector)
-
-        def turn_scale():
-            bank = psum.tile([P, 4, P], F32, name="sums", bufs=SUM_BANKS)
-            for t in range(4):
-                nc.tensor.transpose(bank[:, t, :], scale_rows[:, t:SPAN:4], ident[:])
-            return bank
-
-        def negate_scale(bank):
-            nc.scalar.activation(
-                out=neg_scale[:], in_=bank[:, :, 0:PASSES].rearrange("p t c -> p c t"), func=COPY, scale=-1.0
-            )
-
-        def turn_gain():
-            bank = psum.tile([P, 2, P], F32, name="sums", bufs=SUM_BANKS)
-            for u in range(2):
-                nc.tensor.transpose(bank[:, u, :], gain_rows[:].bitcast(F32)[:, u : 2 * P : 2], ident[:])
-            values = bank[:].rearrange("p u c -> p (u c)").bitcast(BF16).rearrange("p (u c e) -> p c u e", u=2, e=2)
-            nc.scalar.copy(out=gain_col[:].rearrange("p (c u e) -> p c u e", u=2, e=2), in_=values[:, 0:PASSES])
-
-        def pool_group(dst, src):
-            nc.gpsimd.tensor_scalar(out=dst, in0=src, scalar1=1.0, scalar2=0.0, op0=MULT, op1=ADD)
+        def pool_group(dst, src, sign=1.0):
+            nc.gpsimd.tensor_scalar(out=dst, in0=src, scalar1=sign, scalar2=0.0, op0=MULT, op1=ADD)
 
         def group_v(which):
-            pool_group(v_grouped[:, :, which], v_raw[:, which, :].rearrange("p (c t f) -> p c f t", c=PASSES, t=4))
+            src = v_raw[:, which, :].rearrange("p (c t f) -> p c f t", c=PASSES, t=4)
+            pool_group(v_grouped[:, :, which], src, (1.0, -1.0)[which])
 
         def quantize_v():
             nc.vector.quantize_mx(
@@ -135,7 +117,7 @@ def tile_fourierftgivenbases_w_kernel(tc, w0, coef, g, uc, us_bytes, us_scale, v
             )
 
         def widen(i, first=0, end=PASSES, copy=nc.scalar.copy):
-            if first == 0:
+            if i not in widened:
                 widened[i] = stage.tile([P, N], BF16, name="widened", bufs=WIDENED_BUFS, align_bytes=64)
             cols = slice(first * SPAN, end * SPAN)
             copy(out=widened[i][:, cols], in_=raw[("us", i)][:, cols].bitcast(FP8))
@@ -193,11 +175,27 @@ def tile_fourierftgivenbases_w_kernel(tc, w0, coef, g, uc, us_bytes, us_scale, v
             grouped[("us", i)] = slots[i % SLOTS][:]
             dst = grouped[("us", i)][:, SPAN * first : SPAN * end]
             values = turned[(("us", i), first)][:].rearrange("p u c m -> p (u c m)").bitcast(BF16)
-            factors = neg_scale[:, first:end, :].rearrange("p c (o u e) -> p c o u e", o=1, u=2)
+            factors = scale_col[:, first:end, :].rearrange("p c (o u e) -> p c o u e", o=1, u=2)
             nc.vector.tensor_tensor(
                 out=dst.rearrange("p (c m u e) -> p c m u e", c=count, u=2, e=2),
                 in0=values.rearrange("p (u c m e) -> p c m u e", u=2, c=2, e=2)[:, 0:count],
                 in1=factors.to_broadcast([P, count, P, 2, 2]),
+                op=MULT,
+            )
+
+        def stage_last_pass(i):
+            plain[i] = stage.tile([P, SPAN], BF16, name="plain", bufs=2, align_bytes=64)
+            nc.scalar.copy(
+                out=plain[i][:].bitcast(F32).rearrange("p (n i u) -> p n u i", u=2, i=4),
+                in_=turned[(("us", i), PASSES - 1)][:, :, 0, :].rearrange("p u (n i) -> p n u i", i=4),
+            )
+
+        def pool_product(i, tile):
+            last_pass[i] = tile[:, 0:SPAN]
+            nc.gpsimd.tensor_tensor(
+                out=last_pass[i].rearrange("p (m t) -> p m t", t=4),
+                in0=plain[i][:].rearrange("p (m t) -> p m t", t=4),
+                in1=scale_col[:, PASSES - 1 : PASSES, :].to_broadcast([P, P, 4]),
                 op=MULT,
             )
 
@@ -227,8 +225,12 @@ def tile_fourierftgivenbases_w_kernel(tc, w0, coef, g, uc, us_bytes, us_scale, v
             )
 
         def quantize_us(i):
+            key = ("us", i)
             code_tiles("us", i, 1)
-            quantize_part(("us", i), 0, PASSES)
+            if i in last_pass:
+                cols = slice((PASSES - 1) * P, PASSES * P)
+                nc.vector.quantize_mx(out=codes[key][:, cols].bitcast(FP8X4), scales=scales[key][:, cols], in_=last_pass[i])
+            quantize_part(key, 0, PASSES - (i in last_pass))
 
         def mm(dst, key, c, moving, moving_scales, start, stop):
             nc.tensor.matmul_mx(
@@ -322,31 +324,30 @@ def tile_fourierftgivenbases_w_kernel(tc, w0, coef, g, uc, us_bytes, us_scale, v
             return [i // 4 for i in due if i % 4 == 3]
 
         def head():
-            nc.gpsimd.memset(scale_rows[:], 0.0)
-            nc.vector.memset(gain_rows[:], 0.0)
             make_identity(nc, ident[:])
             load(("us", 0), 0, 1)
             load(("us", 0), 1, 2)
-            load_rows(scale_rows, us_scale.rearrange("o (c k) -> (o c) k", c=PASSES))
+            nc.sync.dma_start(out=scale_col[:], in_=us_scale.rearrange("o (c p t) -> p (o c) t", p=P, t=4))
             load(("us", 0), 2, 4)
             load(("us", 1))
             load(("us", 2))
             load_v(0)
             load(("us", 3))
-            load_rows(gain_rows, g.rearrange("(c k) -> c k", c=PASSES))
             load(("coef", 0))
             load_v(1)
             load(("us", 4))
-            for i in range(1, 5):
+            load(("coef", 1))
+            load(("coef", 2))
+            nc.sync.dma_start(out=gain_raw[:], in_=g.rearrange("(c p t) -> p c t", p=P, t=4))
+            load(("coef", 3))
+            for i in (4, 5):
+                load(("us", i + 1))
                 load(("coef", i))
-            load(("us", 5))
-            for i in range(5, RAW_BUFS):
+            for i in range(6, RAW_BUFS):
                 load(("coef", i))
 
-            scale_bank = turn_scale()
             for c in range(PASSES):
                 widen(0, c, c + 1, nc.vector.tensor_copy if c in (0, PASSES - 1) else nc.scalar.copy)
-            negate_scale(scale_bank)
             turn_us(0, 0, 1)
             turn_us(0, 1, 2)
             turn_us(0, 2, 4, wide_bank=True)
@@ -362,7 +363,6 @@ def tile_fourierftgivenbases_w_kernel(tc, w0, coef, g, uc, us_bytes, us_scale, v
             widen(3)
             for h in range(2):
                 turn_wide(("coef", 0), h)
-            turn_gain()
             for h in range(2):
                 turn_us(3, 2 * h, 2 * h + 2)
             widen(4)
@@ -372,9 +372,13 @@ def tile_fourierftgivenbases_w_kernel(tc, w0, coef, g, uc, us_bytes, us_scale, v
             quantize_pair(0)
             for i in range(4):
                 quantize_us(i)
-            for i in (2, 3):
-                for h in range(2):
-                    turn_wide(("coef", i), h)
+            for h in range(2):
+                turn_wide(("coef", 2), h)
+            nc.scalar.copy(out=gain_col[:], in_=gain_raw[:].rearrange("p c t -> p (c t)"))
+            turn(("us", 4), PASSES - 1, PASSES, wide_bank=True)
+            stage_last_pass(4)
+            for h in range(2):
+                turn_wide(("coef", 3), h)
 
         def beats():
             gained = []
@@ -403,15 +407,23 @@ def tile_fourierftgivenbases_w_kernel(tc, w0, coef, g, uc, us_bytes, us_scale, v
                     just_read = slots[(u - 1) % SLOTS]
                     if z_due:
                         group_z(z_due[0], just_read)
+                    elif n in POOL_PRODUCTS:
+                        pool_product(u, just_read)
                     else:
                         pool_sort(wide[2 * (n + 1)], just_read)
                 if n >= STAGE2_BEAT + 2:
                     epilogue(pair(n - STAGE2_BEAT - 1))
                 if u < TILES:
                     product(u, 0, 2)
-                    turn_us(u, 2, 4)
+                    turn_us(u, 2, PASSES - (n in POOL_PRODUCTS))
+                if n + 1 in POOL_PRODUCTS:
+                    turn(("us", u + 1), PASSES - 1, PASSES, wide_bank=True)
                 if u + 1 < TILES:
-                    widen(u + 1)
+                    widen(u + 1, 0, PASSES - (n + 1 in POOL_PRODUCTS))
+                if n + 1 in POOL_PRODUCTS:
+                    stage_last_pass(u + 1)
+                if n + 2 in POOL_PRODUCTS:
+                    widen(u + 2, PASSES - 1, PASSES)
                 turn_wide(early, 0)
                 burst(2 * n)
                 if n == STAGE2_BEAT + 1:

@@ -31,9 +31,9 @@ STAGE1_LAG = 4
 STAGE2_BEAT = HALF + 2
 SORTED_PASSES = 3
 SCALAR_SORTS_FROM = STAGE2_BEAT + 1
-POOL_PRODUCTS = range(HEAD_BEATS, HALF + 1, 2)
+POOL_PRODUCTS = range(HEAD_BEATS, HALF, 4)
 RAW_BUFS = 2 * (LOAD_AHEAD + 2)
-US_RAW_BUFS = 7
+US_RAW_BUFS = 6
 WIDENED_BUFS = 4
 SLOTS = 4
 GROUPED_BUFS = 3
@@ -62,7 +62,7 @@ def tile_fourierftgivenbases_w_kernel(tc, w0, coef, g, uc, us_bytes, us_scale, v
 
         ident = keep.tile([P, P], F32, name="ident")
         scale_col = keep.tile([P, PASSES, 4], F32, name="scale_col")
-        gain_raw = keep.tile([P, PASSES, 4], BF16, name="gain_raw")
+        gain_rows = keep.tile([P, SPAN], BF16, name="gain_rows", align_bytes=64)
         gain_col = keep.tile([P, TILES], F32, name="gain_col")
         v_raw = keep.tile([P, 2, N], BF16, name="v_raw", align_bytes=64)
         v_grouped = keep.tile([P, PASSES, 2, F, 4], BF16, name="v_grouped", align_bytes=64)
@@ -101,6 +101,13 @@ def tile_fourierftgivenbases_w_kernel(tc, w0, coef, g, uc, us_bytes, us_scale, v
                 out=v_raw[:, which, :].rearrange("p (c t f) -> p c t f", c=PASSES, t=4),
                 in_=(vc, vs)[which].rearrange("(c p t) f -> p c t f", p=P, t=4),
             )
+
+        def turn_gain():
+            bank = psum.tile([P, 2, P], F32, name="sums", bufs=SUM_BANKS)
+            for u in range(2):
+                nc.tensor.transpose(bank[:, u, :], gain_rows[:].bitcast(F32)[:, u : 2 * P : 2], ident[:])
+            values = bank[:].rearrange("p u c -> p (u c)").bitcast(BF16).rearrange("p (u c e) -> p c u e", u=2, e=2)
+            nc.scalar.copy(out=gain_col[:].rearrange("p (c u e) -> p c u e", u=2, e=2), in_=values[:, 0:PASSES])
 
         def pool_group(dst, src, sign=1.0):
             nc.gpsimd.tensor_scalar(out=dst, in0=src, scalar1=sign, scalar2=0.0, op0=MULT, op1=ADD)
@@ -325,6 +332,7 @@ def tile_fourierftgivenbases_w_kernel(tc, w0, coef, g, uc, us_bytes, us_scale, v
 
         def head():
             make_identity(nc, ident[:])
+            nc.vector.memset(gain_rows[:], 0.0)
             load(("us", 0), 0, 1)
             load(("us", 0), 1, 2)
             nc.sync.dma_start(out=scale_col[:], in_=us_scale.rearrange("o (c p t) -> p (o c) t", p=P, t=4))
@@ -333,17 +341,16 @@ def tile_fourierftgivenbases_w_kernel(tc, w0, coef, g, uc, us_bytes, us_scale, v
             load(("us", 2))
             load_v(0)
             load(("us", 3))
+            nc.sync.dma_start(out=gain_rows[0:PASSES, :], in_=g.rearrange("(c k) -> c k", c=PASSES))
             load(("coef", 0))
             load_v(1)
             load(("us", 4))
             load(("coef", 1))
             load(("coef", 2))
-            nc.sync.dma_start(out=gain_raw[:], in_=g.rearrange("(c p t) -> p c t", p=P, t=4))
             load(("coef", 3))
-            for i in (4, 5):
-                load(("us", i + 1))
-                load(("coef", i))
-            for i in range(6, RAW_BUFS):
+            load(("coef", 4))
+            load(("us", 5))
+            for i in range(5, RAW_BUFS):
                 load(("coef", i))
 
             for c in range(PASSES):
@@ -363,6 +370,7 @@ def tile_fourierftgivenbases_w_kernel(tc, w0, coef, g, uc, us_bytes, us_scale, v
             widen(3)
             for h in range(2):
                 turn_wide(("coef", 0), h)
+            turn_gain()
             for h in range(2):
                 turn_us(3, 2 * h, 2 * h + 2)
             widen(4)
@@ -374,7 +382,6 @@ def tile_fourierftgivenbases_w_kernel(tc, w0, coef, g, uc, us_bytes, us_scale, v
                 quantize_us(i)
             for h in range(2):
                 turn_wide(("coef", 2), h)
-            nc.scalar.copy(out=gain_col[:], in_=gain_raw[:].rearrange("p c t -> p (c t)"))
             turn(("us", 4), PASSES - 1, PASSES, wide_bank=True)
             stage_last_pass(4)
             for h in range(2):

@@ -75,6 +75,7 @@ def tile_fourierftgivenbases_w_kernel(tc, w0, coef, g, uc, us_bytes, us_scale, v
 
         raw = {}
         widened = {}
+        us_words = {}
         sorted_words = {}
         grouped = {}
         plain = {}
@@ -123,11 +124,26 @@ def tile_fourierftgivenbases_w_kernel(tc, w0, coef, g, uc, us_bytes, us_scale, v
                 in_=v_grouped[:].rearrange("p c w f t -> p (c w f t)"),
             )
 
-        def widen(i, first=0, end=PASSES, copy=nc.scalar.copy):
+        def widen(i, first=0, end=PASSES, by_vector=False):
             if i not in widened:
                 widened[i] = stage.tile([P, N], BF16, name="widened", bufs=WIDENED_BUFS, align_bytes=64)
             cols = slice(first * SPAN, end * SPAN)
-            copy(out=widened[i][:, cols], in_=raw[("us", i)][:, cols].bitcast(FP8))
+            values = raw[("us", i)][:, cols].bitcast(FP8)
+            words = widened[i][:, cols].bitcast(F32)
+            count = end - first
+            if by_vector:
+                nc.vector.tensor_copy(out=widened[i][:, cols], in_=values)
+            else:
+                nc.scalar.copy(
+                    out=widened[i][:, cols].rearrange("p (u n e) -> p u n e", u=2, e=2),
+                    in_=values.rearrange("p (n u e) -> p u n e", u=2, e=2),
+                )
+            for c in range(count):
+                for u in range(2):
+                    start = P * (count * u + c)
+                    us_words[(i, first + c, u)] = (
+                        words[:, 2 * P * c + u : 2 * P * (c + 1) : 2] if by_vector else words[:, start : start + P]
+                    )
 
         def scalar_sort(key):
             tile = stage.tile([P, N], BF16, name="sorted", bufs=2, align_bytes=64)
@@ -151,11 +167,13 @@ def tile_fourierftgivenbases_w_kernel(tc, w0, coef, g, uc, us_bytes, us_scale, v
                 bank = psum.tile([P, 2, 2, P], F32, name="us_bank", bufs=US_BANKS)
             else:
                 bank = psum.tile([P, 2, 2, P], F32, name="wide_bank", bufs=WIDE_BANKS)
-            words = (widened[i] if kind == "us" else raw[key])[:].bitcast(F32)
+            words = None if kind == "us" else raw[key][:].bitcast(F32)
             tile, count = sorted_words.get(key, (None, 0))
             for c in range(first, end):
                 for u in range(2):
-                    if c < count:
+                    if kind == "us":
+                        src = us_words[(i, c, u)]
+                    elif c < count:
                         start = P * (count * u + c)
                         src = tile[:].bitcast(F32)[:, start : start + P]
                     else:
@@ -354,7 +372,7 @@ def tile_fourierftgivenbases_w_kernel(tc, w0, coef, g, uc, us_bytes, us_scale, v
                 load(("coef", i))
 
             for c in range(PASSES):
-                widen(0, c, c + 1, nc.vector.tensor_copy if c in (0, PASSES - 1) else nc.scalar.copy)
+                widen(0, c, c + 1, c in (0, PASSES - 1))
             turn_us(0, 0, 1)
             turn_us(0, 1, 2)
             turn_us(0, 2, 4, wide_bank=True)

@@ -24,6 +24,19 @@ TILES = N // P
 BEATS = TILES
 HALF = BEATS // 2
 HEAD_BEATS = 2
+NO_US = (14, 15)
+PLAIN_US = (0, 1, 2, 3)
+POOL_CASTS = (3, 4, 8)
+CAST_FROM = 2
+LEAD_AT = 2
+EPI = 0
+LAST_SORT = 0
+ORDER = 0
+US_LEAD = 1
+EPI5 = 0
+SCALAR_SORTS_EARLY = ()
+SORT_BUFS = 2
+W0_BEAT = HALF - 1
 US_AHEAD = 2
 LOAD_AHEAD = 2
 US_LOAD_AHEAD = 3
@@ -31,12 +44,12 @@ STAGE1_LAG = 4
 STAGE2_BEAT = HALF + 2
 SORTED_PASSES = 3
 SCALAR_SORTS_FROM = STAGE2_BEAT + 1
-POOL_PRODUCTS = range(HEAD_BEATS, HALF, 4)
-RAW_BUFS = 2 * (LOAD_AHEAD + 2)
+POOL_PRODUCTS = (2, 6, 12)
+RAW_BUFS = 9
 US_RAW_BUFS = 6
 WIDENED_BUFS = 4
 SLOTS = 4
-GROUPED_BUFS = 3
+GROUPED_BUFS = 4
 CODE_BUFS = 4
 US_BANKS = 2
 WIDE_BANKS = 4
@@ -54,6 +67,12 @@ def tile_fourierftgivenbases_w_kernel(tc, w0, coef, g, uc, us_bytes, us_scale, v
     w0_rows = w0.rearrange("(g m t) f -> m g t f", m=P, t=4)
     out_rows = out.rearrange("(g m t) f -> g m t f", m=P, t=4)
     wide = [("coef", i) for i in range(TILES)] + [("uc", i) for i in range(TILES)]
+
+    us_at = {n: 4 + j for j, n in enumerate([n for n in range(HEAD_BEATS, BEATS) if n not in NO_US])}
+    beat_of = {i: n for n, i in us_at.items()}
+
+    first_of = [2 * n + (n > LEAD_AT) for n in range(BEATS + 1)]
+    turned_in = [wide[first_of[n] : first_of[n + 1]] for n in range(BEATS)] + [[]] * 3
 
     with ExitStack() as ctx:
         keep = ctx.enter_context(tc.tile_pool(name="keep", bufs=1))
@@ -131,8 +150,11 @@ def tile_fourierftgivenbases_w_kernel(tc, w0, coef, g, uc, us_bytes, us_scale, v
             values = raw[("us", i)][:, cols].bitcast(FP8)
             words = widened[i][:, cols].bitcast(F32)
             count = end - first
+            plain_copy = by_vector or i in PLAIN_US
             if by_vector:
                 nc.vector.tensor_copy(out=widened[i][:, cols], in_=values)
+            elif plain_copy:
+                nc.scalar.copy(out=widened[i][:, cols], in_=values)
             else:
                 nc.scalar.copy(
                     out=widened[i][:, cols].rearrange("p (u n e) -> p u n e", u=2, e=2),
@@ -142,11 +164,19 @@ def tile_fourierftgivenbases_w_kernel(tc, w0, coef, g, uc, us_bytes, us_scale, v
                 for u in range(2):
                     start = P * (count * u + c)
                     us_words[(i, first + c, u)] = (
-                        words[:, 2 * P * c + u : 2 * P * (c + 1) : 2] if by_vector else words[:, start : start + P]
+                        words[:, 2 * P * c + u : 2 * P * (c + 1) : 2] if plain_copy else words[:, start : start + P]
                     )
 
+        def pool_cast(i, tile):
+            cols = slice(CAST_FROM * SPAN, PASSES * SPAN)
+            nc.gpsimd.tensor_copy(out=tile[:, cols], in_=raw[("us", i)][:, cols].bitcast(FP8))
+            words = tile[:].bitcast(F32)
+            for c in range(CAST_FROM, PASSES):
+                for u in range(2):
+                    us_words[(i, c, u)] = words[:, 2 * P * c + u : 2 * P * (c + 1) : 2]
+
         def scalar_sort(key):
-            tile = stage.tile([P, N], BF16, name="sorted", bufs=2, align_bytes=64)
+            tile = stage.tile([P, N], BF16, name="sorted", bufs=SORT_BUFS, align_bytes=64)
             nc.scalar.copy(
                 out=tile[:].bitcast(F32).rearrange("p (u n i) -> p n u i", u=2, i=4),
                 in_=raw[key][:].bitcast(F32).rearrange("p (n i u) -> p n u i", u=2, i=4),
@@ -230,8 +260,8 @@ def tile_fourierftgivenbases_w_kernel(tc, w0, coef, g, uc, us_bytes, us_scale, v
 
         def code_tiles(kind, first, count):
             depth = TILES if kind == "us" else CODE_BUFS
-            ct = stage.tile([P, count * SPAN], U32, name=kind + "_codes", bufs=depth, align_bytes=64)
-            st = stage.tile([P, count * SPAN], U8, name=kind + "_scales", bufs=depth, align_bytes=64)
+            ct = stage.tile([P, count * SPAN], U32, name=("us" if kind == "us" else "wide") + "_codes", bufs=depth, align_bytes=64)
+            st = stage.tile([P, count * SPAN], U8, name=("us" if kind == "us" else "wide") + "_scales", bufs=depth, align_bytes=64)
             for j in range(count):
                 codes[(kind, first + j)] = ct[:, j * SPAN : (j + 1) * SPAN]
                 scales[(kind, first + j)] = st[:, j * SPAN : (j + 1) * SPAN]
@@ -291,18 +321,17 @@ def tile_fourierftgivenbases_w_kernel(tc, w0, coef, g, uc, us_bytes, us_scale, v
                 in_=z_grouped[c].rearrange("p f t -> p (f t)"),
             )
 
-        def stage2(tiles, parts, start, stop, tag="sums", depth=SUM_BANKS):
+        def stage2(tiles, steps, start, stop, tag="sums", depth=SUM_BANKS):
             if start:
-                sums[tiles] = psum.tile([P, 2, F], F32, name=tag, bufs=depth)
-            steps = [(j, i, kind, c) for j, i in enumerate(tiles) for kind, c in parts]
-            for n, (j, i, kind, c) in enumerate(steps):
+                sums[tiles] = psum.tile([P, 4, F], F32, name=tag, bufs=depth)
+            for n, (kind, i, c) in enumerate(steps):
                 half = slice(F, 2 * F) if kind == "us" else slice(0, F)
                 first, final = start and n == 0, stop and n == len(steps) - 1
-                mm(sums[tiles][:, j, :], (kind, i), c, z_codes[:, c, half], z_scales[:, c, half], first, final)
+                mm(sums[tiles][:, i - tiles[0], :], (kind, i), c, z_codes[:, c, half], z_scales[:, c, half], first, final)
 
         def epilogue(tiles):
             i, count = tiles[0], len(tiles)
-            results[tiles] = stage.tile([P, count, F], F32, name="result", bufs=4)
+            results[tiles] = stage.tile([P, count, F], F32, name="result", bufs=5)
             nc.vector.scalar_tensor_tensor(
                 out=results[tiles][:],
                 in0=sums[tiles][:, 0:count, :],
@@ -319,16 +348,14 @@ def tile_fourierftgivenbases_w_kernel(tc, w0, coef, g, uc, us_bytes, us_scale, v
         def pair(j):
             return (2 * j, 2 * j + 1)
 
-        def passes(kind, first=0, end=PASSES):
-            return [(kind, c) for c in range(first, end)]
+        def group(r):
+            return tuple(range(4 * r, 4 * r + 4))
+
+        def passes(kind, tiles, first=0, end=PASSES):
+            return [(kind, i, c) for i in tiles for c in range(first, end)]
 
         stage1_at = [min(i, TILES - 2) + STAGE1_LAG for i in range(TILES)]
-        first_pair = {
-            2 * STAGE2_BEAT - 1: passes("us", 0, 2),
-            2 * STAGE2_BEAT: passes("us", 2, 3) + passes("uc", 0, 1),
-            2 * STAGE2_BEAT + 1: passes("uc", 1, 3),
-            2 * STAGE2_BEAT + 2: passes("us", 3, 4) + passes("uc", 3, 4),
-        }
+        opening = 2 * STAGE2_BEAT - 1
 
         def burst(j):
             due = [i for i in range(TILES) if stage1_at[i] == j]
@@ -336,11 +363,25 @@ def tile_fourierftgivenbases_w_kernel(tc, w0, coef, g, uc, us_bytes, us_scale, v
                 stage1(i)
                 if i != due[-1]:
                     gain(i)
-            if j in first_pair:
-                stage2(pair(0), first_pair[j], j == min(first_pair), j == max(first_pair))
-            beat, second = divmod(j, 2)
-            if beat > STAGE2_BEAT:
-                stage2(pair(beat - STAGE2_BEAT), passes(("us", "uc")[second]), not second, bool(second))
+            if j == opening:
+                stage2(group(0), passes("us", group(0), 0, 2), True, False)
+            elif j == opening + 1:
+                stage2(group(0), passes("us", group(0), 2, 3) + passes("uc", pair(0), 0, 1), False, False)
+            elif j == opening + 2:
+                stage2(group(0), passes("uc", pair(0), 1, 3), False, False)
+                if US_LEAD:
+                    stage2(group(1), passes("us", pair(2), 0, 2), True, False)
+            elif j == opening + 3:
+                stage2(group(0), passes("us", group(0), 3) + passes("uc", pair(0), 3), False, False)
+                if US_LEAD:
+                    stage2(group(1), passes("us", pair(2), 2), False, False)
+            elif j > opening + 3:
+                q = j // 2 - STAGE2_BEAT + (1 - j % 2)
+                tiles = group(q // 2) if q < 4 else pair(q)
+                if j % 2:
+                    stage2(tiles, passes("uc", pair(q)), False, q == tiles[-1] // 2)
+                else:
+                    stage2(tiles, passes("us", pair(q)), q == tiles[0] // 2, False)
 
         def gain_after(j):
             due = [i for i in range(TILES) if stage1_at[i] == j][-1:]
@@ -400,86 +441,112 @@ def tile_fourierftgivenbases_w_kernel(tc, w0, coef, g, uc, us_bytes, us_scale, v
                 quantize_us(i)
             for h in range(2):
                 turn_wide(("coef", 2), h)
-            turn(("us", 4), PASSES - 1, PASSES, wide_bank=True)
-            stage_last_pass(4)
+            if HEAD_BEATS in POOL_PRODUCTS:
+                turn(("us", 4), PASSES - 1, PASSES, wide_bank=True)
+                stage_last_pass(4)
             for h in range(2):
                 turn_wide(("coef", 3), h)
 
         def beats():
             gained = []
             waiting = []
-            for n in range(HEAD_BEATS, BEATS):
-                early, late = wide[2 * n], wide[2 * n + 1]
-                u = n + US_AHEAD
+            for n in range(HEAD_BEATS, BEATS - 2):
+                early, rest = turned_in[n][0], turned_in[n][1:]
+                u = us_at.get(n)
+                after = us_at.get(n + 1)
                 for i in range(TILES):
-                    if max(i - US_AHEAD - US_LOAD_AHEAD, HEAD_BEATS) == n and ("us", i) not in raw:
+                    if ("us", i) not in raw and beat_of[i] - US_LOAD_AHEAD <= n:
                         load(("us", i))
-                for key in wide[2 * (n + LOAD_AHEAD) : 2 * (n + LOAD_AHEAD + 1)]:
-                    load(key)
-                if n == HALF - 1:
+                for key in turned_in[n + LOAD_AHEAD]:
+                    if key not in raw:
+                        load(key)
+                if n == W0_BEAT:
                     nc.sync.dma_start(out=w0_sb[:], in_=w0_rows)
                 if n == STAGE2_BEAT + 3:
-                    store(pair(0))
-                if n >= STAGE2_BEAT + 3:
-                    store(pair(n - STAGE2_BEAT - 2))
+                    store(group(0))
 
-                if u < TILES:
+                if u is not None:
                     turn(("us", u), 0, 2)
                 gained = gained + gain_after(2 * n - 1)
                 z_due = waiting + [c for c in gained if c == PASSES - 1]
                 waiting = [c for c in gained if c < PASSES - 1]
-                if u < TILES:
+                if u is not None:
                     just_read = slots[(u - 1) % SLOTS]
                     if z_due:
                         group_z(z_due[0], just_read)
                     elif n in POOL_PRODUCTS:
                         pool_product(u, just_read)
-                    else:
-                        pool_sort(wide[2 * (n + 1)], just_read)
-                if n >= STAGE2_BEAT + 2:
-                    epilogue(pair(n - STAGE2_BEAT - 1))
-                if u < TILES:
+                    elif n in POOL_CASTS:
+                        pool_cast(after, just_read)
+                    elif n + 1 < BEATS and n - 1 not in NO_US:
+                        pool_sort(turned_in[n + 1][0], just_read)
+                if n == STAGE2_BEAT + 2:
+                    epilogue(group(0))
+                if u is not None:
                     product(u, 0, 2)
                     turn_us(u, 2, PASSES - (n in POOL_PRODUCTS))
                 if n + 1 in POOL_PRODUCTS:
-                    turn(("us", u + 1), PASSES - 1, PASSES, wide_bank=True)
-                if u + 1 < TILES:
-                    widen(u + 1, 0, PASSES - (n + 1 in POOL_PRODUCTS))
+                    turn(("us", after), PASSES - 1, PASSES, wide_bank=True)
+                if after is not None and (after > 4 or n + 1 in POOL_PRODUCTS):
+                    widen(after, 0, CAST_FROM if n in POOL_CASTS else PASSES - (n + 1 in POOL_PRODUCTS))
                 if n + 1 in POOL_PRODUCTS:
-                    stage_last_pass(u + 1)
+                    stage_last_pass(after)
                 if n + 2 in POOL_PRODUCTS:
-                    widen(u + 2, PASSES - 1, PASSES)
+                    widen(us_at[n + 2], PASSES - 1, PASSES)
                 turn_wide(early, 0)
                 burst(2 * n)
-                if n == STAGE2_BEAT + 1:
-                    epilogue(pair(0))
                 quantize_pair(n - 1)
                 for c in z_due:
                     quantize_z(c)
-                if u < TILES:
+                if u is not None:
                     quantize_us(u)
                 gained = gain_after(2 * n)
                 if SCALAR_SORTS_FROM <= n < BEATS - 1:
-                    scalar_sort(wide[2 * (n + 1) + 1])
+                    scalar_sort(turned_in[n + 1][-1])
+                if n in SCALAR_SORTS_EARLY:
+                    scalar_sort(turned_in[n + 1][0])
                 turn_wide(early, 1)
-                turn_wide(late, 0)
-                turn_wide(late, 1)
+                for key in rest[:1]:
+                    turn_wide(key, 0)
+                    turn_wide(key, 1)
                 burst(2 * n + 1)
+                for key in rest[1:]:
+                    turn_wide(key, 0)
+                    turn_wide(key, 1)
 
         def tail():
             before_last, last = TILES - 2, TILES - 1
-            store(pair(HALF - 4))
+            epilogue(group(1))
+            quantize_pair(13)
+            store(group(1))
+            for h in range(2):
+                turn_wide(("uc", 13), h)
+            stage2(pair(5), passes("us", pair(5)), True, False, "us_bank", US_BANKS)
+            for h in range(2):
+                turn_wide(("uc", before_last), h)
+            burst(29)
+            stage2(pair(6), passes("us", pair(6)), True, False, "us_bank", US_BANKS)
+            for h in range(2):
+                turn_wide(("uc", last), h)
+            stage2((before_last,), passes("us", (before_last,)), True, False)
+            stage2((last,), passes("us", (last,)), True, False, "wide_bank", WIDE_BANKS)
+            burst(31)
+            if EPI == 0:
+                epilogue(pair(4))
+            quantize_pair(14)
+            if EPI == 1:
+                epilogue(pair(4))
+            store(pair(4))
             code_tiles("uc", before_last, 2)
             quantize_part(("uc", before_last), 0, PASSES)
-            epilogue(pair(HALF - 3))
-            store(pair(HALF - 3))
+            if EPI5:
+                epilogue(pair(5))
+                store(pair(5))
             quantize_part(("uc", last), 0, 2)
             quantize_part(("uc", last), 2, PASSES)
-            both = passes("us") + passes("uc")
-            stage2(pair(HALF - 2), both, True, True)
-            for i in (before_last, last):
-                stage2((i,), both, True, True, "us_bank", US_BANKS)
-            for tiles in (pair(HALF - 2), (before_last,), (last,)):
+            for tiles in (pair(6), (before_last,), (last,)):
+                stage2(tiles, passes("uc", tiles), False, True)
+            for tiles in [pair(5), pair(6), (before_last,), (last,)][EPI5:]:
                 epilogue(tiles)
                 store(tiles)
 

from contextlib import ExitStack

import concourse.mybir as mybir
from concourse.masks import make_identity

N = 2048
F = 128
FLOPS = 4 * 2 * N * N * F

F32 = mybir.dt.float32
BF16 = mybir.dt.bfloat16
U32 = mybir.dt.uint32
U8 = mybir.dt.uint8
FP8 = mybir.dt.float8_e4m3fn
FP8X4 = mybir.dt.float8_e4m3fn_x4
COPY = mybir.ActivationFunctionType.Copy
MULT = mybir.AluOpType.mult
ADD = mybir.AluOpType.add

P = 128
PASSES = 4
SPAN = 4 * P
TILES = N // P
BEATS = TILES
HALF = BEATS // 2
HEAD_BEATS = 2
NO_US = (14, 15)
PLAIN_US = (0, 1, 2, 3)
POOL_CASTS = (3, 4, 8)
CAST_FROM = 2
LEAD_AT = 2
EPI = 0
LAST_SORT = 0
ORDER = 0
US_LEAD = 1
EPI5 = 0
SCALAR_SORTS_EARLY = ()
SORT_BUFS = 2
W0_BEAT = HALF - 1
US_AHEAD = 2
LOAD_AHEAD = 2
US_LOAD_AHEAD = 3
STAGE1_LAG = 4
STAGE2_BEAT = HALF + 2
SORTED_PASSES = 3
SCALAR_SORTS_FROM = STAGE2_BEAT + 1
POOL_PRODUCTS = (2, 6, 12)
RAW_BUFS = 9
US_RAW_BUFS = 6
WIDENED_BUFS = 4
SLOTS = 4
GROUPED_BUFS = 4
CODE_BUFS = 4
US_BANKS = 2
WIDE_BANKS = 4
SUM_BANKS = 2


def tile_fourierftgivenbases_w_kernel(tc, w0, coef, g, uc, us_bytes, us_scale, vc, vs, out):
    nc = tc.nc

    rows = {
        "coef": coef.rearrange("(g m t) k -> g t m k", m=P, t=4),
        "uc": uc.rearrange("(g m t) k -> g t m k", m=P, t=4),
        "us": us_bytes.rearrange("(g m t) k -> g t m k", m=P, t=4),
    }
    w0_rows = w0.rearrange("(g m t) f -> m g t f", m=P, t=4)
    out_rows = out.rearrange("(g m t) f -> g m t f", m=P, t=4)
    wide = [("coef", i) for i in range(TILES)] + [("uc", i) for i in range(TILES)]

    us_at = {n: 4 + j for j, n in enumerate([n for n in range(HEAD_BEATS, BEATS) if n not in NO_US])}
    beat_of = {i: n for n, i in us_at.items()}

    first_of = [2 * n + (n > LEAD_AT) for n in range(BEATS + 1)]
    turned_in = [wide[first_of[n] : first_of[n + 1]] for n in range(BEATS)] + [[]] * 3

    with ExitStack() as ctx:
        keep = ctx.enter_context(tc.tile_pool(name="keep", bufs=1))
        stage = ctx.enter_context(tc.tile_pool(name="stage", bufs=2))
        psum = ctx.enter_context(tc.psum_pool(name="psum", bufs=2))

        ident = keep.tile([P, P], F32, name="ident")
        scale_col = keep.tile([P, PASSES, 4], F32, name="scale_col")
        gain_rows = keep.tile([P, SPAN], BF16, name="gain_rows", align_bytes=64)
        gain_col = keep.tile([P, TILES], F32, name="gain_col")
        v_raw = keep.tile([P, 2, N], BF16, name="v_raw", align_bytes=64)
        v_grouped = keep.tile([P, PASSES, 2, F, 4], BF16, name="v_grouped", align_bytes=64)
        v_codes = keep.tile([P, PASSES, 2 * F], U32, name="v_codes", align_bytes=64)
        v_scales = keep.tile([P, PASSES, 2 * F], U8, name="v_scales", align_bytes=64)
        z_codes = keep.tile([P, PASSES, 2 * F], U32, name="z_codes", align_bytes=64)
        z_scales = keep.tile([P, PASSES, 2 * F], U8, name="z_scales", align_bytes=64)
        w0_sb = keep.tile([P, 4, 4, F], BF16, name="w0_sb", align_bytes=64)
        slots = [keep.tile([P, N], BF16, name="slot%d" % j, align_bytes=64) for j in range(SLOTS)]

        raw = {}
        widened = {}
        us_words = {}
        sorted_words = {}
        grouped = {}
        plain = {}
        last_pass = {}
        turned = {}
        codes = {}
        scales = {}
        sums = {}
        z_flat = {}
        z_grouped = {}
        results = {}

        def load(key, first=0, end=PASSES):
            kind, i = key
            if first == 0 and kind == "us":
                raw[key] = stage.tile([P, N], U8, name="us_raw", bufs=US_RAW_BUFS, align_bytes=64)
            elif first == 0:
                raw[key] = stage.tile([P, N], BF16, name="raw", bufs=RAW_BUFS, align_bytes=64)
            cols = slice(first * SPAN, end * SPAN)
            nc.sync.dma_start(out=raw[key][:, cols], in_=rows[kind][i // 4, i % 4][:, cols])

        def load_v(which):
            nc.sync.dma_start(
                out=v_raw[:, which, :].rearrange("p (c t f) -> p c t f", c=PASSES, t=4),
                in_=(vc, vs)[which].rearrange("(c p t) f -> p c t f", p=P, t=4),
            )

        def turn_gain():
            bank = psum.tile([P, 2, P], F32, name="sums", bufs=SUM_BANKS)
            for u in range(2):
                nc.tensor.transpose(bank[:, u, :], gain_rows[:].bitcast(F32)[:, u : 2 * P : 2], ident[:])
            values = bank[:].rearrange("p u c -> p (u c)").bitcast(BF16).rearrange("p (u c e) -> p c u e", u=2, e=2)
            nc.scalar.copy(out=gain_col[:].rearrange("p (c u e) -> p c u e", u=2, e=2), in_=values[:, 0:PASSES])

        def pool_group(dst, src, sign=1.0):
            nc.gpsimd.tensor_scalar(out=dst, in0=src, scalar1=sign, scalar2=0.0, op0=MULT, op1=ADD)

        def group_v(which):
            src = v_raw[:, which, :].rearrange("p (c t f) -> p c f t", c=PASSES, t=4)
            pool_group(v_grouped[:, :, which], src, (1.0, -1.0)[which])

        def quantize_v():
            nc.vector.quantize_mx(
                out=v_codes[:].rearrange("p c f -> p (c f)").bitcast(FP8X4),
                scales=v_scales[:].rearrange("p c f -> p (c f)"),
                in_=v_grouped[:].rearrange("p c w f t -> p (c w f t)"),
            )

        def widen(i, first=0, end=PASSES, by_vector=False):
            if i not in widened:
                widened[i] = stage.tile([P, N], BF16, name="widened", bufs=WIDENED_BUFS, align_bytes=64)
            cols = slice(first * SPAN, end * SPAN)
            values = raw[("us", i)][:, cols].bitcast(FP8)
            words = widened[i][:, cols].bitcast(F32)
            count = end - first
            plain_copy = by_vector or i in PLAIN_US
            if by_vector:
                nc.vector.tensor_copy(out=widened[i][:, cols], in_=values)
            elif plain_copy:
                nc.scalar.copy(out=widened[i][:, cols], in_=values)
            else:
                nc.scalar.copy(
                    out=widened[i][:, cols].rearrange("p (u n e) -> p u n e", u=2, e=2),
                    in_=values.rearrange("p (n u e) -> p u n e", u=2, e=2),
                )
            for c in range(count):
                for u in range(2):
                    start = P * (count * u + c)
                    us_words[(i, first + c, u)] = (
                        words[:, 2 * P * c + u : 2 * P * (c + 1) : 2] if plain_copy else words[:, start : start + P]
                    )

        def pool_cast(i, tile):
            cols = slice(CAST_FROM * SPAN, PASSES * SPAN)
            nc.gpsimd.tensor_copy(out=tile[:, cols], in_=raw[("us", i)][:, cols].bitcast(FP8))
            words = tile[:].bitcast(F32)
            for c in range(CAST_FROM, PASSES):
                for u in range(2):
                    us_words[(i, c, u)] = words[:, 2 * P * c + u : 2 * P * (c + 1) : 2]

        def scalar_sort(key):
            tile = stage.tile([P, N], BF16, name="sorted", bufs=SORT_BUFS, align_bytes=64)
            nc.scalar.copy(
                out=tile[:].bitcast(F32).rearrange("p (u n i) -> p n u i", u=2, i=4),
                in_=raw[key][:].bitcast(F32).rearrange("p (n i u) -> p n u i", u=2, i=4),
            )
            sorted_words[key] = (tile, PASSES)

        def pool_sort(key, tile):
            width = SORTED_PASSES * SPAN
            nc.gpsimd.tensor_copy(
                out=tile[:, 0:width].bitcast(F32).rearrange("p (u n) -> p u n", u=2),
                in_=raw[key][:, 0:width].bitcast(F32).rearrange("p (n u) -> p u n", u=2),
            )
            sorted_words[key] = (tile, SORTED_PASSES)

        def turn(key, first, end, wide_bank=False):
            kind, i = key
            if kind == "us" and not wide_bank:
                bank = psum.tile([P, 2, 2, P], F32, name="us_bank", bufs=US_BANKS)
            else:
                bank = psum.tile([P, 2, 2, P], F32, name="wide_bank", bufs=WIDE_BANKS)
            words = None if kind == "us" else raw[key][:].bitcast(F32)
            tile, count = sorted_words.get(key, (None, 0))
            for c in range(first, end):
                for u in range(2):
                    if kind == "us":
                        src = us_words[(i, c, u)]
                    elif c < count:
                        start = P * (count * u + c)
                        src = tile[:].bitcast(F32)[:, start : start + P]
                    else:
                        src = words[:, 2 * P * c + u : 2 * P * (c + 1) : 2]
                    nc.tensor.transpose(bank[:, u, c - first, :], src, ident[:])
            turned[(key, first)] = bank

        def turn_wide(key, h):
            kind, i = key
            turn(key, 2 * h, 2 * h + 2)
            if h == 0 and i % 2 == 0:
                both = stage.tile([P, 2, N], BF16, name="grouped", bufs=GROUPED_BUFS, align_bytes=64)
                grouped[(kind, i)] = both[:, 0, :]
                grouped[(kind, i + 1)] = both[:, 1, :]
                grouped[(kind, "pair", i // 2)] = both[:].rearrange("p j n -> p (j n)")
            dst = grouped[key].bitcast(F32)[:, SPAN * h : SPAN * (h + 1)]
            nc.scalar.copy(
                out=dst.rearrange("p (n i u) -> p n u i", u=2, i=4),
                in_=turned[(key, 2 * h)][:].rearrange("p u c (n i) -> p (c n) u i", i=4),
            )

        def product(i, first, end):
            count = end - first
            grouped[("us", i)] = slots[i % SLOTS][:]
            dst = grouped[("us", i)][:, SPAN * first : SPAN * end]
            values = turned[(("us", i), first)][:].rearrange("p u c m -> p (u c m)").bitcast(BF16)
            factors = scale_col[:, first:end, :].rearrange("p c (o u e) -> p c o u e", o=1, u=2)
            nc.vector.tensor_tensor(
                out=dst.rearrange("p (c m u e) -> p c m u e", c=count, u=2, e=2),
                in0=values.rearrange("p (u c m e) -> p c m u e", u=2, c=2, e=2)[:, 0:count],
                in1=factors.to_broadcast([P, count, P, 2, 2]),
                op=MULT,
            )

        def stage_last_pass(i):
            plain[i] = stage.tile([P, SPAN], BF16, name="plain", bufs=2, align_bytes=64)
            nc.scalar.copy(
                out=plain[i][:].bitcast(F32).rearrange("p (n i u) -> p n u i", u=2, i=4),
                in_=turned[(("us", i), PASSES - 1)][:, :, 0, :].rearrange("p u (n i) -> p n u i", i=4),
            )

        def pool_product(i, tile):
            last_pass[i] = tile[:, 0:SPAN]
            nc.gpsimd.tensor_tensor(
                out=last_pass[i].rearrange("p (m t) -> p m t", t=4),
                in0=plain[i][:].rearrange("p (m t) -> p m t", t=4),
                in1=scale_col[:, PASSES - 1 : PASSES, :].to_broadcast([P, P, 4]),
                op=MULT,
            )

        def turn_us(i, first, end, wide_bank=False):
            turn(("us", i), first, end, wide_bank)
            product(i, first, end)

        def code_tiles(kind, first, count):
            depth = TILES if kind == "us" else CODE_BUFS
            ct = stage.tile([P, count * SPAN], U32, name=("us" if kind == "us" else "wide") + "_codes", bufs=depth, align_bytes=64)
            st = stage.tile([P, count * SPAN], U8, name=("us" if kind == "us" else "wide") + "_scales", bufs=depth, align_bytes=64)
            for j in range(count):
                codes[(kind, first + j)] = ct[:, j * SPAN : (j + 1) * SPAN]
                scales[(kind, first + j)] = st[:, j * SPAN : (j + 1) * SPAN]
            return ct, st

        def quantize_pair(beat):
            kind, i = wide[2 * beat]
            ct, st = code_tiles(kind, i, 2)
            nc.vector.quantize_mx(out=ct[:].bitcast(FP8X4), scales=st[:], in_=grouped[(kind, "pair", i // 2)])

        def quantize_part(key, first, end):
            nc.vector.quantize_mx(
                out=codes[key][:, first * P : end * P].bitcast(FP8X4),
                scales=scales[key][:, first * P : end * P],
                in_=grouped[key][:, first * SPAN : end * SPAN],
            )

        def quantize_us(i):
            key = ("us", i)
            code_tiles("us", i, 1)
            if i in last_pass:
                cols = slice((PASSES - 1) * P, PASSES * P)
                nc.vector.quantize_mx(out=codes[key][:, cols].bitcast(FP8X4), scales=scales[key][:, cols], in_=last_pass[i])
            quantize_part(key, 0, PASSES - (i in last_pass))

        def mm(dst, key, c, moving, moving_scales, start, stop):
            nc.tensor.matmul_mx(
                out=dst,
                lhsT=codes[key][:, c * P : (c + 1) * P].bitcast(FP8X4),
                lhsT_scale=scales[key][:, c * P : (c + 1) * P],
                rhs=moving.bitcast(FP8X4),
                rhs_scale=moving_scales,
                start=start,
                stop=stop,
            )

        def stage1(i):
            sums[("r", i)] = psum.tile([P, 2 * F], F32, name="sums", bufs=SUM_BANKS)
            for c in range(PASSES):
                mm(sums[("r", i)][:], ("coef", i), c, v_codes[:, c, :], v_scales[:, c, :], c == 0, c == PASSES - 1)

        def gain(i):
            if i % 4 == 0:
                z_flat[i // 4] = stage.tile([P, 4, 2 * F], BF16, name="z_flat", bufs=2, align_bytes=64)
            nc.scalar.activation(
                out=z_flat[i // 4][:, i % 4, :], in_=sums[("r", i)][:], func=COPY, scale=gain_col[:, i : i + 1]
            )

        def group_z(c, tile):
            z_grouped[c] = tile[:, 0 : 8 * F].rearrange("p (f t) -> p f t", t=4)
            pool_group(z_grouped[c], z_flat[c][:].rearrange("p t f -> p f t"))

        def quantize_z(c):
            nc.vector.quantize_mx(
                out=z_codes[:, c, :].bitcast(FP8X4),
                scales=z_scales[:, c, :],
                in_=z_grouped[c].rearrange("p f t -> p (f t)"),
            )

        def stage2(tiles, steps, start, stop, tag="sums", depth=SUM_BANKS):
            if start:
                sums[tiles] = psum.tile([P, 4, F], F32, name=tag, bufs=depth)
            for n, (kind, i, c) in enumerate(steps):
                half = slice(F, 2 * F) if kind == "us" else slice(0, F)
                first, final = start and n == 0, stop and n == len(steps) - 1
                mm(sums[tiles][:, i - tiles[0], :], (kind, i), c, z_codes[:, c, half], z_scales[:, c, half], first, final)

        def epilogue(tiles):
            i, count = tiles[0], len(tiles)
            results[tiles] = stage.tile([P, count, F], F32, name="result", bufs=5)
            nc.vector.scalar_tensor_tensor(
                out=results[tiles][:],
                in0=sums[tiles][:, 0:count, :],
                scalar=0.5,
                in1=w0_sb[:, i // 4, i % 4 : i % 4 + count, :],
                op0=MULT,
                op1=ADD,
            )

        def store(tiles):
            i, count = tiles[0], len(tiles)
            nc.sync.dma_start(out=out_rows[i // 4, :, i % 4 : i % 4 + count, :], in_=results[tiles][:])

        def pair(j):
            return (2 * j, 2 * j + 1)

        def group(r):
            return tuple(range(4 * r, 4 * r + 4))

        def passes(kind, tiles, first=0, end=PASSES):
            return [(kind, i, c) for i in tiles for c in range(first, end)]

        stage1_at = [min(i, TILES - 2) + STAGE1_LAG for i in range(TILES)]
        opening = 2 * STAGE2_BEAT - 1

        def burst(j):
            due = [i for i in range(TILES) if stage1_at[i] == j]
            for i in due:
                stage1(i)
                if i != due[-1]:
                    gain(i)
            if j == opening:
                stage2(group(0), passes("us", group(0), 0, 2), True, False)
            elif j == opening + 1:
                stage2(group(0), passes("us", group(0), 2, 3) + passes("uc", pair(0), 0, 1), False, False)
            elif j == opening + 2:
                stage2(group(0), passes("uc", pair(0), 1, 3), False, False)
                if US_LEAD:
                    stage2(group(1), passes("us", pair(2), 0, 2), True, False)
            elif j == opening + 3:
                stage2(group(0), passes("us", group(0), 3) + passes("uc", pair(0), 3), False, False)
                if US_LEAD:
                    stage2(group(1), passes("us", pair(2), 2), False, False)
            elif j > opening + 3:
                q = j // 2 - STAGE2_BEAT + (1 - j % 2)
                tiles = group(q // 2) if q < 4 else pair(q)
                if j % 2:
                    stage2(tiles, passes("uc", pair(q)), False, q == tiles[-1] // 2)
                else:
                    stage2(tiles, passes("us", pair(q)), q == tiles[0] // 2, False)

        def gain_after(j):
            due = [i for i in range(TILES) if stage1_at[i] == j][-1:]
            for i in due:
                gain(i)
            return [i // 4 for i in due if i % 4 == 3]

        def head():
            make_identity(nc, ident[:])
            nc.vector.memset(gain_rows[:], 0.0)
            load(("us", 0), 0, 1)
            load(("us", 0), 1, 2)
            nc.sync.dma_start(out=scale_col[:], in_=us_scale.rearrange("o (c p t) -> p (o c) t", p=P, t=4))
            load(("us", 0), 2, 4)
            load(("us", 1))
            load(("us", 2))
            load_v(0)
            load(("us", 3))
            nc.sync.dma_start(out=gain_rows[0:PASSES, :], in_=g.rearrange("(c k) -> c k", c=PASSES))
            load(("coef", 0))
            load_v(1)
            load(("us", 4))
            load(("coef", 1))
            load(("coef", 2))
            load(("coef", 3))
            load(("coef", 4))
            load(("us", 5))
            for i in range(5, RAW_BUFS):
                load(("coef", i))

            for c in range(PASSES):
                widen(0, c, c + 1, c in (0, PASSES - 1))
            turn_us(0, 0, 1)
            turn_us(0, 1, 2)
            turn_us(0, 2, 4, wide_bank=True)
            for h in range(2):
                widen(1, 2 * h, 2 * h + 2)
            for h in range(2):
                turn_us(1, 2 * h, 2 * h + 2)
            group_v(0)
            group_v(1)
            widen(2)
            for h in range(2):
                turn_us(2, 2 * h, 2 * h + 2, wide_bank=True)
            widen(3)
            for h in range(2):
                turn_wide(("coef", 0), h)
            turn_gain()
            for h in range(2):
                turn_us(3, 2 * h, 2 * h + 2)
            widen(4)
            for h in range(2):
                turn_wide(("coef", 1), h)
            quantize_v()
            quantize_pair(0)
            for i in range(4):
                quantize_us(i)
            for h in range(2):
                turn_wide(("coef", 2), h)
            if HEAD_BEATS in POOL_PRODUCTS:
                turn(("us", 4), PASSES - 1, PASSES, wide_bank=True)
                stage_last_pass(4)
            for h in range(2):
                turn_wide(("coef", 3), h)

        def beats():
            gained = []
            waiting = []
            for n in range(HEAD_BEATS, BEATS - 2):
                early, rest = turned_in[n][0], turned_in[n][1:]
                u = us_at.get(n)
                after = us_at.get(n + 1)
                for i in range(TILES):
                    if ("us", i) not in raw and beat_of[i] - US_LOAD_AHEAD <= n:
                        load(("us", i))
                for key in turned_in[n + LOAD_AHEAD]:
                    if key not in raw:
                        load(key)
                if n == W0_BEAT:
                    nc.sync.dma_start(out=w0_sb[:], in_=w0_rows)
                if n == STAGE2_BEAT + 3:
                    store(group(0))

                if u is not None:
                    turn(("us", u), 0, 2)
                gained = gained + gain_after(2 * n - 1)
                z_due = waiting + [c for c in gained if c == PASSES - 1]
                waiting = [c for c in gained if c < PASSES - 1]
                if u is not None:
                    just_read = slots[(u - 1) % SLOTS]
                    if z_due:
                        group_z(z_due[0], just_read)
                    elif n in POOL_PRODUCTS:
                        pool_product(u, just_read)
                    elif n in POOL_CASTS:
                        pool_cast(after, just_read)
                    elif n + 1 < BEATS and n - 1 not in NO_US:
                        pool_sort(turned_in[n + 1][0], just_read)
                if n == STAGE2_BEAT + 2:
                    epilogue(group(0))
                if u is not None:
                    product(u, 0, 2)
                    turn_us(u, 2, PASSES - (n in POOL_PRODUCTS))
                if n + 1 in POOL_PRODUCTS:
                    turn(("us", after), PASSES - 1, PASSES, wide_bank=True)
                if after is not None and (after > 4 or n + 1 in POOL_PRODUCTS):
                    widen(after, 0, CAST_FROM if n in POOL_CASTS else PASSES - (n + 1 in POOL_PRODUCTS))
                if n + 1 in POOL_PRODUCTS:
                    stage_last_pass(after)
                if n + 2 in POOL_PRODUCTS:
                    widen(us_at[n + 2], PASSES - 1, PASSES)
                turn_wide(early, 0)
                burst(2 * n)
                quantize_pair(n - 1)
                for c in z_due:
                    quantize_z(c)
                if u is not None:
                    quantize_us(u)
                gained = gain_after(2 * n)
                if SCALAR_SORTS_FROM <= n < BEATS - 1:
                    scalar_sort(turned_in[n + 1][-1])
                if n in SCALAR_SORTS_EARLY:
                    scalar_sort(turned_in[n + 1][0])
                turn_wide(early, 1)
                for key in rest[:1]:
                    turn_wide(key, 0)
                    turn_wide(key, 1)
                burst(2 * n + 1)
                for key in rest[1:]:
                    turn_wide(key, 0)
                    turn_wide(key, 1)

        def tail():
            before_last, last = TILES - 2, TILES - 1
            epilogue(group(1))
            quantize_pair(13)
            store(group(1))
            for h in range(2):
                turn_wide(("uc", 13), h)
            stage2(pair(5), passes("us", pair(5)), True, False, "us_bank", US_BANKS)
            for h in range(2):
                turn_wide(("uc", before_last), h)
            burst(29)
            stage2(pair(6), passes("us", pair(6)), True, False, "us_bank", US_BANKS)
            for h in range(2):
                turn_wide(("uc", last), h)
            stage2((before_last,), passes("us", (before_last,)), True, False)
            stage2((last,), passes("us", (last,)), True, False, "wide_bank", WIDE_BANKS)
            burst(31)
            if EPI == 0:
                epilogue(pair(4))
            quantize_pair(14)
            if EPI == 1:
                epilogue(pair(4))
            store(pair(4))
            code_tiles("uc", before_last, 2)
            quantize_part(("uc", before_last), 0, PASSES)
            if EPI5:
                epilogue(pair(5))
                store(pair(5))
            quantize_part(("uc", last), 0, 2)
            quantize_part(("uc", last), 2, PASSES)
            for tiles in (pair(6), (before_last,), (last,)):
                stage2(tiles, passes("uc", tiles), False, True)
            for tiles in [pair(5), pair(6), (before_last,), (last,)][EPI5:]:
                epilogue(tiles)
                store(tiles)

        with tc.manual_schedule():
            head()
            beats()
            tail()
